import numpy as np
import ml_dtypes


def mxq(x, axis, fmt="e4m3"):
    dtype, down = {"e4m3": (ml_dtypes.float8_e4m3fn, 7), "e5m2": (ml_dtypes.float8_e5m2, 14)}[fmt]
    v = np.moveaxis(np.asarray(x, np.float32).astype(ml_dtypes.bfloat16).astype(np.float64), axis, -1)
    blocks = v.reshape(v.shape[:-1] + (-1, 32))
    amax = np.abs(blocks).max(-1, keepdims=True)
    byte = np.maximum(np.where(amax > 0, np.frexp(amax)[1] - 1 + 127, 0) - down, 1)
    scale = np.exp2(byte - 127.0)
    codes = (blocks / scale).astype(np.float32).astype(dtype).astype(np.float64)
    return np.moveaxis((codes * scale).reshape(v.shape), -1, axis)


WIDE = False


def mx_kscale(k):
    if not WIDE:
        return np.ones(k)
    levels = np.array([10, -10, 5, -5, 0])
    if k % 512:
        return np.exp2(np.random.permutation(np.resize(levels, k // 32))).repeat(32)
    a = np.empty((k // 512, 16))
    for p in range(k // 512):
        a[p, :8] = np.random.permutation(np.resize(levels, 8))
        for g in range(8):
            far = levels[np.abs(levels - a[p, g]) >= 10]
            a[p, g + 8] = far[np.random.randint(len(far))]
    return np.exp2(a.ravel()).repeat(32)


def f64(x):
    return np.asarray(x).astype(np.float64)


def striped(idx):
    return np.tile(idx.reshape(-1, 16).T, (8, 1)).astype(np.uint16)


def unstriped(offs):
    return offs[:16].T.reshape(-1).astype(np.int64)


E2M1 = np.array([0.0, 0.5, 1.0, 1.5, 2.0, 3.0, 4.0, 6.0, -0.0, -0.5, -1.0, -1.5, -2.0, -3.0, -4.0, -6.0])


def pack_weight(w, fmt):
    k, n = w.shape
    w = f64(np.asarray(w, np.float32).astype(ml_dtypes.bfloat16)).reshape(k // 32, 32, n)
    amax = np.abs(w).max(1)
    if fmt == "e4m3":
        byte = np.frexp(amax)[1] - 1 + 127 - 7
    else:
        mant, ex = np.frexp(amax / 6.0)
        byte = np.where(mant > 0.5, ex, ex - 1) + 127
    byte = np.clip(np.where(amax > 0, byte, 1), 1, 254)
    scaled = (w * np.exp2(127.0 - byte)[:, None, :]).reshape(k, n).astype(np.float32)
    by_word = np.ascontiguousarray(scaled.reshape(k // 512, 128, 4, n).transpose(0, 1, 3, 2))
    if fmt == "e4m3":
        words = by_word.astype(ml_dtypes.float8_e4m3fn).view(np.uint8)
    else:
        c = by_word.astype(ml_dtypes.float4_e2m1fn).view(np.uint8) & 0xF
        words = (c[..., 0::2] | (c[..., 1::2] << 4)).reshape(k // 512, 128, 2 * n)
    return np.ascontiguousarray(words), np.ascontiguousarray(byte.astype(np.uint8).reshape(k // 512, 16, n))


def unpack_weight(words, scales, fmt):
    g, _, n = scales.shape
    words = np.ascontiguousarray(words).reshape(g, 128, n, -1)
    if fmt == "e4m3":
        vals = words.view(ml_dtypes.float8_e4m3fn).astype(np.float64)
    else:
        nib = np.empty((g, 128, n, 4), np.uint8)
        nib[..., 0::2] = words & 0xF
        nib[..., 1::2] = words >> 4
        vals = E2M1[nib]
    vals = vals * np.repeat(np.exp2(scales.astype(np.float64) - 127.0), 8, axis=1)[..., None]
    return vals.transpose(0, 1, 3, 2).reshape(g * 512, n)


def relu(v):
    return np.maximum(v, 0.0)


K, T, Q, E, C, D, H = 1024, 768, 1024, 12, 128, 128, 0
N = 128


def by_expert(wq, xq, C):
    return np.concatenate([wq[e].T @ xq[:, e * C:(e + 1) * C] for e in range(E)], axis=1)


def setup_inputs():
    n = np.random.standard_normal
    s = mx_kscale(K)
    first = np.random.permutation(np.repeat(np.arange(E), T // E))
    second = (first + 1 + np.random.permutation(np.repeat(np.arange(E - 1), -(-T // (E - 1)))[:T])) % E
    while np.bincount(second, minlength=E).max() != T // E:
        load = np.bincount(second, minlength=E); hi, lo = int(load.argmax()), int(load.argmin())
        t = np.flatnonzero((second == hi) & (first != lo))[0]; second[t] = lo
    slot_token = np.empty(E * C, np.int64); pos = np.empty((2, T), np.int64); fill = np.zeros(E, np.int64)
    place = np.stack([np.random.permutation(C) for _ in range(E)])
    for r, deal in enumerate((first, second)):
        for t in np.random.permutation(T):
            e = deal[t]; j = e * C + place[e, fill[e]]; fill[e] += 1; slot_token[j] = t; pos[r, t] = j
    g = np.random.uniform(0.2, 0.8, T)
    slots2 = np.concatenate([np.random.permutation(Q)[:D] for e in range(E)])
    x = pack_weight(n((K, Q)) * s[:, None], "e4m3")
    w = [pack_weight(m, "e2m1") for m in n((E, K, N)) / np.sqrt(K) / s[None, :, None]]
    return {
        "x_words": x[0],
        "x_scales": x[1],
        "xo": (n((K, T)) * s[:, None]).astype(np.float32),
        "w_words": np.stack([m[0] for m in w]),
        "w_scales": np.stack([m[1] for m in w]),
        "gate": np.stack([np.tile(g, (128, 1)), np.tile(1.0 - g, (128, 1))]).astype(np.float32),
        "offs": striped(slot_token),
        "pos1": striped(pos[0]),
        "pos2": striped(pos[1]),
        "offs2": striped(slots2),
    }


def reference(x_words, x_scales, xo, w_words, w_scales, gate, offs, pos1, pos2, offs2):
    w = np.stack([unpack_weight(w_words[e], w_scales[e], "e2m1") for e in range(E)])
    idx, idx2 = unstriped(offs), unstriped(offs2)
    xq = mxq(f64(xo)[:, idx], 0, "e4m3")
    rq = unpack_weight(x_words, x_scales, "e4m3")[:, idx2]
    y = relu(by_expert(w, xq, C))
    z = relu(by_expert(w, rq, D))
    own = sum(f64(gate[r, :1]) * y[:, unstriped(p)] for r, p in enumerate((pos1, pos2)))
    return np.concatenate([own, z], axis=1)

@@ -1,0 +1,182 @@
+from contextlib import ExitStack
+
+import concourse.mybir as mybir
+
+K, T, Q, E, C, N = 1024, 768, 1024, 12, 128, 128
+S = E * C
+FLOPS = 2 * K * N * 2 * S
+
+F32 = mybir.dt.float32
+BF16 = mybir.dt.bfloat16
+I32 = mybir.dt.int32
+U32 = mybir.dt.uint32
+U16 = mybir.dt.uint16
+U8 = mybir.dt.uint8
+FP8X4 = mybir.dt.float8_e4m3fn_x4
+FP4X4 = mybir.dt.float4_e2m1fn_x4
+ACT = mybir.ActivationFunctionType
+ALU = mybir.AluOpType
+
+P = 128
+PASSES = 2
+CH = 512
+NCH = S // CH
+LC = 16
+COMBINE = ((0, 384), (384, 640), (640, 768))
+
+
+def tile_moe_loc_lin_relu_kernel(
+    tc, x_words, x_scales, xo, w_words, w_scales, gate, offs, pos1, pos2, offs2, out
+):
+    nc = tc.nc
+    with ExitStack() as ctx:
+        sb = ctx.enter_context(tc.tile_pool(name="sb", bufs=1))
+        ps = ctx.enter_context(tc.psum_pool(name="ps", bufs=1))
+
+        def tile(shape, dtype, name, tag=None):
+            return sb.tile(shape, dtype, name=name, tag=tag or name, align_bytes=64)
+
+        def cut(lst, a, b):
+            return lst[:, a // LC : b // LC]
+
+        l_own = tile([P, S // LC], U16, "l_own")
+        l_far = tile([P, S // LC], U16, "l_far")
+        l_pos = [tile([P, T // LC], U16, "l_pos%d" % r) for r in range(2)]
+
+        xs = tile([P, Q], U8, "xs")
+        far_s1 = tile([P, S], U8, "far_s1")
+        ws = tile([P, E * PASSES * N], U8, "ws")
+        nc.vector.memset(ws[:].bitcast(I32), 0)
+        nc.vector.memset(xs[:].bitcast(I32), 0)
+        nc.vector.memset(far_s1[:].bitcast(I32), 0)
+
+        xw = [tile([P, Q], I32, "xw%d" % s) for s in range(PASSES)]
+        raw = [tile([P, 2, T], F32, "raw%d" % i, tag="slot_d" if i == 3 else None) for i in range(4)]
+        xo_v = xo.rearrange("(s p u e) t -> s u p e t", s=PASSES, u=2, e=2)
+
+        def load_xw(s):
+            nc.sync.dma_start(xw[s][:], x_words[s].rearrange("p t d -> p (t d)").bitcast(I32))
+
+        def load_raw(i):
+            nc.sync.dma_start(raw[i][:], xo_v[i // 2, i % 2])
+
+        nc.sync.dma_start(l_far[:], offs2)
+        load_xw(0)
+        load_xw(1)
+        load_raw(0)
+        nc.sync.dma_start(l_own[:], offs)
+        for i in range(1, 4):
+            load_raw(i)
+        ws_v = w_scales.bitcast(I32).rearrange("e s (q r) n -> r q (e s) n", r=4)
+        ws_i = ws[:].bitcast(I32).rearrange("p (g n) -> p g n", n=N // 4)
+        for r in range(4):
+            nc.sync.dma_start(ws_i[r:P:32, :, :], ws_v[r])
+        xs_v = x_scales.bitcast(I32)
+        for q in range(4):
+            nc.sync.dma_start(xs[32 * q : 32 * q + 8, :].bitcast(I32), xs_v[:, 4 * q : 4 * q + 4, :])
+        ww = tile([P, E * PASSES * 2 * N], U8, "ww")
+        nc.sync.dma_start(
+            ww[:].bitcast(I32).rearrange("p (g n) -> p g n", n=N // 2),
+            w_words.bitcast(I32).rearrange("e s p n -> p (e s) n"),
+        )
+        nc.sync.dma_start(l_pos[0][:], pos1)
+        nc.sync.dma_start(l_pos[1][:], pos2)
+        g = [tile([P, T], F32, "g%d" % r) for r in range(2)]
+        for r in range(2):
+            nc.sync.dma_start(g[r][:], gate[r])
+
+        far_w0 = tile([P, S], U32, "far_w0")
+        for a, b in ((0, S // 2), (S // 2, S)):
+            nc.vector.tensor_copy(far_w0[:, a:b], xw[0][:].bitcast(U32).indirect(cut(l_far, a, b)))
+        far_w1a = tile([P, CH], U32, "far_w1a")
+        nc.vector.tensor_copy(far_w1a[:], xw[1][:].bitcast(U32).indirect(cut(l_far, 0, CH)))
+
+        pairs = [tile([P, 2 * T], BF16, "pairs%d" % i) for i in range(4)]
+        for i in range(4):
+            nc.scalar.activation(
+                pairs[i][:].rearrange("p (t e) -> p t e", e=2), raw[i][:].rearrange("p e t -> p t e"), ACT.Copy
+            )
+
+        def gather(dst, s, u, c):
+            nc.vector.tensor_copy(
+                dst[:, u * CH : (u + 1) * CH],
+                pairs[2 * s + u][:].bitcast(U32).indirect(cut(l_own, c * CH, (c + 1) * CH)),
+            )
+
+        codes = [[tile([P, CH], U32, "codes%d%d" % (s, c)) for c in range(NCH)] for s in range(PASSES)]
+        scales = [[tile([P, CH], U8, "scales%d%d" % (s, c)) for c in range(NCH)] for s in range(PASSES)]
+
+        def weave(src, name, tag):
+            woven = tile([P, 4 * CH], BF16, name, tag)
+            nc.scalar.copy(
+                woven[:].bitcast(U32).rearrange("p (j u) -> p j u", u=2), src[:].rearrange("p (u j) -> p j u", u=2)
+            )
+            return woven
+
+        def quantize(woven, s, c):
+            nc.vector.quantize_mx(codes[s][c][:].bitcast(FP8X4), scales[s][c][:], woven[:])
+
+        got0 = [tile([P, 2 * CH], U32, "got0%d" % c) for c in range(NCH)]
+        for u in range(2):
+            for c in range(NCH):
+                gather(got0[c], 0, u, c)
+
+        far_s = tile([P, S], U8, "far_s")
+        for a, b in ((0, S // 2), (S // 2, S)):
+            nc.vector.tensor_copy(far_s[:, a:b], xs[:].indirect(cut(l_far, a, b)))
+        for q in range(4):
+            nc.sync.dma_start(
+                far_s1[32 * q : 32 * q + 4, :].bitcast(I32), far_s[32 * q + 4 : 32 * q + 8, :].bitcast(I32)
+            )
+
+        ring = ("slot_e", "slot_d")
+        for c in range(NCH):
+            got1 = tile([P, 2 * CH], U32, "got1%d" % c, ring[c % 2])
+            for u in range(2):
+                gather(got1, 1, u, c)
+            quantize(weave(got0[c], "woven0%d" % c, ring[(c + 1) % 2]), 0, c)
+            quantize(weave(got1, "woven1%d" % c, "woven1%d" % c), 1, c)
+
+        far_w1b = tile([P, S - CH], U32, "far_w1b", "woven1%d" % (NCH - 1))
+        for c in range(1, NCH):
+            nc.vector.tensor_copy(
+                far_w1b[:, (c - 1) * CH : c * CH], xw[1][:].bitcast(U32).indirect(cut(l_far, c * CH, (c + 1) * CH))
+            )
+
+        def experts(c, name, words, planes):
+            bank = ps.tile([P, CH], F32, name=name)
+            for j in range(CH // C):
+                e = c * (CH // C) + j
+                for s in range(PASSES):
+                    i = e * PASSES + s
+                    nc.tensor.matmul_mx(
+                        bank[:, j * C : (j + 1) * C],
+                        lhsT=ww[:, i * 2 * N : (i + 1) * 2 * N].bitcast(FP4X4),
+                        lhsT_scale=ws[:, i * N : (i + 1) * N],
+                        rhs=words[s][:, j * C : (j + 1) * C].bitcast(FP8X4),
+                        rhs_scale=planes[s][:, j * C : (j + 1) * C],
+                        start=(s == 0),
+                        stop=(s == PASSES - 1),
+                    )
+            return bank
+
+        y = tile([P, S], F32, "y")
+        for c in range(NCH):
+            bank = experts(c, "own%d" % c, [codes[s][c] for s in range(PASSES)], [scales[s][c] for s in range(PASSES)])
+            nc.scalar.activation(y[:, c * CH : (c + 1) * CH], bank[:], ACT.Relu)
+
+        for c in range(NCH):
+            cols = slice(c * CH, (c + 1) * CH)
+            w1 = far_w1a[:] if c == 0 else far_w1b[:, (c - 1) * CH : c * CH]
+            bank = experts(c, "far%d" % c, [far_w0[:, cols], w1], [far_s[:, cols], far_s1[:, cols]])
+            z = tile([P, CH], F32, "z%d" % c)
+            nc.scalar.activation(z[:], bank[:], ACT.Relu)
+            nc.sync.dma_start(out[:, T + c * CH : T + (c + 1) * CH], z[:])
+
+        for a, b in COMBINE:
+            part = [tile([P, b - a], F32, "part%d_%d" % (r, a), "xw1" if (r, a) == (0, 0) else None) for r in range(2)]
+            for r in range(2):
+                nc.vector.tensor_tensor(part[r][:], y[:].indirect(cut(l_pos[r], a, b)), g[r][:, a:b], ALU.mult)
+            own = tile([P, b - a], F32, "sum%d" % a)
+            nc.vector.tensor_tensor(own[:], part[0][:], part[1][:], ALU.add)
+            nc.sync.dma_start(out[:, a:b], own[:])

@@ -46,12 +46,12 @@ def tile_moe_loc_lin_relu_kernel(
         xs = tile([P, Q], U8, "xs")
         far_s1 = tile([P, S], U8, "far_s1")
         ws = tile([P, E * PASSES * N], U8, "ws")
-        nc.vector.memset(ws[:].bitcast(I32), 0)
         nc.vector.memset(xs[:].bitcast(I32), 0)
+        nc.vector.memset(ws[:].bitcast(I32), 0)
         nc.vector.memset(far_s1[:].bitcast(I32), 0)
 
         xw = [tile([P, Q], I32, "xw%d" % s) for s in range(PASSES)]
-        raw = [tile([P, 2, T], F32, "raw%d" % i, tag="slot_d" if i == 3 else None) for i in range(4)]
+        raw = {i: tile([P, 2, T], F32, "raw%d" % i, tag="slot_d" if i == 3 else None) for i in range(1, 4)}
         xo_v = xo.rearrange("(s p u e) t -> s u p e t", s=PASSES, u=2, e=2)
 
         def load_xw(s):
@@ -62,28 +62,22 @@ def tile_moe_loc_lin_relu_kernel(
 
         nc.sync.dma_start(l_far[:], offs2)
         load_xw(0)
-        load_xw(1)
-        load_raw(0)
+        first_raw = [tile([P, 2, T // 2], F32, "first_raw%d" % h) for h in range(2)]
+        for h in range(2):
+            nc.sync.dma_start(first_raw[h][:], xo_v[0, 0, :, :, h * T // 2 : (h + 1) * T // 2])
         nc.sync.dma_start(l_own[:], offs)
         for i in range(1, 4):
             load_raw(i)
+        load_xw(1)
+        xs_v = x_scales.bitcast(I32)
+        for q in range(4):
+            nc.sync.dma_start(xs[32 * q : 32 * q + 8, :].bitcast(I32), xs_v[:, 4 * q : 4 * q + 4, :])
         ws_v = w_scales.bitcast(I32).rearrange("e s (q r) n -> r q (e s) n", r=4)
         ws_i = ws[:].bitcast(I32).rearrange("p (g n) -> p g n", n=N // 4)
         for r in range(4):
             nc.sync.dma_start(ws_i[r:P:32, :, :], ws_v[r])
-        xs_v = x_scales.bitcast(I32)
-        for q in range(4):
-            nc.sync.dma_start(xs[32 * q : 32 * q + 8, :].bitcast(I32), xs_v[:, 4 * q : 4 * q + 4, :])
-        ww = tile([P, E * PASSES * 2 * N], U8, "ww")
-        nc.sync.dma_start(
-            ww[:].bitcast(I32).rearrange("p (g n) -> p g n", n=N // 2),
-            w_words.bitcast(I32).rearrange("e s p n -> p (e s) n"),
-        )
         nc.sync.dma_start(l_pos[0][:], pos1)
         nc.sync.dma_start(l_pos[1][:], pos2)
-        g = [tile([P, T], F32, "g%d" % r) for r in range(2)]
-        for r in range(2):
-            nc.sync.dma_start(g[r][:], gate[r])
 
         far_w0 = tile([P, S], U32, "far_w0")
         for a, b in ((0, S // 2), (S // 2, S)):
@@ -92,10 +86,26 @@ def tile_moe_loc_lin_relu_kernel(
         nc.vector.tensor_copy(far_w1a[:], xw[1][:].bitcast(U32).indirect(cut(l_far, 0, CH)))
 
         pairs = [tile([P, 2 * T], BF16, "pairs%d" % i) for i in range(4)]
-        for i in range(4):
+        for h in range(2):
+            nc.scalar.activation(
+                pairs[0][:, h * T : (h + 1) * T].rearrange("p (t e) -> p t e", e=2),
+                first_raw[h][:].rearrange("p e t -> p t e"),
+                ACT.Copy,
+            )
+        for i in range(1, 3):
             nc.scalar.activation(
                 pairs[i][:].rearrange("p (t e) -> p t e", e=2), raw[i][:].rearrange("p e t -> p t e"), ACT.Copy
             )
+        nc.scalar.activation(pairs[3][:], raw[3][:].rearrange("p e t -> p (e t)"), ACT.Copy)
+
+        ww = tile([P, E * PASSES * 2 * N], U8, "ww", "raw1")
+        nc.sync.dma_start(
+            ww[:].bitcast(I32).rearrange("p (g n) -> p g n", n=N // 2),
+            w_words.bitcast(I32).rearrange("e s p n -> p (e s) n"),
+        )
+        g = [tile([P, T], F32, "g%d" % r, "first_raw%d" % r) for r in range(2)]
+        for r in range(2):
+            nc.sync.dma_start(g[r][:], gate[r])
 
         def gather(dst, s, u, c):
             nc.vector.tensor_copy(
@@ -106,12 +116,28 @@ def tile_moe_loc_lin_relu_kernel(
         codes = [[tile([P, CH], U32, "codes%d%d" % (s, c)) for c in range(NCH)] for s in range(PASSES)]
         scales = [[tile([P, CH], U8, "scales%d%d" % (s, c)) for c in range(NCH)] for s in range(PASSES)]
 
-        def weave(src, name, tag):
+        def weave(src, name, tag, on_vector=False):
             woven = tile([P, 4 * CH], BF16, name, tag)
-            nc.scalar.copy(
-                woven[:].bitcast(U32).rearrange("p (j u) -> p j u", u=2), src[:].rearrange("p (u j) -> p j u", u=2)
-            )
+            if on_vector:
+                nc.vector.tensor_copy(
+                    woven[:].bitcast(I32).rearrange("p (j u) -> p j u", u=2),
+                    src[:].bitcast(I32).rearrange("p (u j) -> p j u", u=2),
+                )
+            else:
+                nc.scalar.copy(
+                    woven[:].bitcast(U32).rearrange("p (j u) -> p j u", u=2),
+                    src[:].rearrange("p (u j) -> p j u", u=2),
+                )
             return woven
+
+        def gather_single(dst, c):
+            half = dst[:, CH : 2 * CH].bitcast(BF16).rearrange("p (j e) -> p e j", e=2)
+            for e in range(2):
+                nc.scalar.activation(
+                    half[:, e, :],
+                    pairs[3][:, e * T : (e + 1) * T].indirect(cut(l_own, c * CH, (c + 1) * CH)),
+                    ACT.Copy,
+                )
 
         def quantize(woven, s, c):
             nc.vector.quantize_mx(codes[s][c][:].bitcast(FP8X4), scales[s][c][:], woven[:])
@@ -121,7 +147,15 @@ def tile_moe_loc_lin_relu_kernel(
             for c in range(NCH):
                 gather(got0[c], 0, u, c)
 
-        far_s = tile([P, S], U8, "far_s")
+        on_vector = ()
+        early = [weave(got0[c], "woven0%d" % c, None, True) for c in on_vector]
+        got1 = [tile([P, 2 * CH], U32, "got1%d" % c) for c in range(NCH)]
+        for c in range(NCH):
+            gather(got1[c], 1, 0, c)
+        for c, woven in zip(on_vector, early):
+            quantize(woven, 0, c)
+
+        far_s = tile([P, S], U8, "far_s", "pairs2")
         for a, b in ((0, S // 2), (S // 2, S)):
             nc.vector.tensor_copy(far_s[:, a:b], xs[:].indirect(cut(l_far, a, b)))
         for q in range(4):
@@ -129,13 +163,11 @@ def tile_moe_loc_lin_relu_kernel(
                 far_s1[32 * q : 32 * q + 4, :].bitcast(I32), far_s[32 * q + 4 : 32 * q + 8, :].bitcast(I32)
             )
 
-        ring = ("slot_e", "slot_d")
         for c in range(NCH):
-            got1 = tile([P, 2 * CH], U32, "got1%d" % c, ring[c % 2])
-            for u in range(2):
-                gather(got1, 1, u, c)
-            quantize(weave(got0[c], "woven0%d" % c, ring[(c + 1) % 2]), 0, c)
-            quantize(weave(got1, "woven1%d" % c, "woven1%d" % c), 1, c)
+            gather_single(got1[c], c)
+            if c not in on_vector:
+                quantize(weave(got0[c], "woven0%d" % c, "slot_d" if c == 0 else "got1%d" % (c - 1)), 0, c)
+            quantize(weave(got1[c], "woven1%d" % c, "woven1%d" % c), 1, c)
 
         far_w1b = tile([P, S - CH], U32, "far_w1b", "woven1%d" % (NCH - 1))
         for c in range(1, NCH):
@@ -143,8 +175,8 @@ def tile_moe_loc_lin_relu_kernel(
                 far_w1b[:, (c - 1) * CH : c * CH], xw[1][:].bitcast(U32).indirect(cut(l_far, c * CH, (c + 1) * CH))
             )
 
-        def experts(c, name, words, planes):
-            bank = ps.tile([P, CH], F32, name=name)
+        def experts(c, name, tag, words, planes):
+            bank = ps.tile([P, CH], F32, name=name, tag=tag)
             for j in range(CH // C):
                 e = c * (CH // C) + j
                 for s in range(PASSES):
@@ -162,21 +194,31 @@ def tile_moe_loc_lin_relu_kernel(
 
         y = tile([P, S], F32, "y")
         for c in range(NCH):
-            bank = experts(c, "own%d" % c, [codes[s][c] for s in range(PASSES)], [scales[s][c] for s in range(PASSES)])
+            bank = experts(
+                c, "own%d" % c, "own%d" % c, [codes[s][c] for s in range(PASSES)], [scales[s][c] for s in range(PASSES)]
+            )
             nc.scalar.activation(y[:, c * CH : (c + 1) * CH], bank[:], ACT.Relu)
 
         for c in range(NCH):
             cols = slice(c * CH, (c + 1) * CH)
             w1 = far_w1a[:] if c == 0 else far_w1b[:, (c - 1) * CH : c * CH]
-            bank = experts(c, "far%d" % c, [far_w0[:, cols], w1], [far_s[:, cols], far_s1[:, cols]])
+            bank = experts(c, "far%d" % c, "own2" if c == 0 else "far%d" % c, [far_w0[:, cols], w1], [far_s[:, cols], far_s1[:, cols]])
             z = tile([P, CH], F32, "z%d" % c)
             nc.scalar.activation(z[:], bank[:], ACT.Relu)
             nc.sync.dma_start(out[:, T + c * CH : T + (c + 1) * CH], z[:])
 
-        for a, b in COMBINE:
-            part = [tile([P, b - a], F32, "part%d_%d" % (r, a), "xw1" if (r, a) == (0, 0) else None) for r in range(2)]
-            for r in range(2):
-                nc.vector.tensor_tensor(part[r][:], y[:].indirect(cut(l_pos[r], a, b)), g[r][:, a:b], ALU.mult)
+        first = tile([P, T], F32, "first", "xw1")
+        nc.vector.tensor_tensor(first[:], y[:].indirect(l_pos[0][:]), g[0][:], ALU.mult)
+        second = [tile([P, b - a], F32, "second%d" % a) for a, b in COMBINE]
+
+        def product(i):
+            a, b = COMBINE[i]
+            nc.vector.tensor_tensor(second[i][:], y[:].indirect(cut(l_pos[1], a, b)), g[1][:, a:b], ALU.mult)
+
+        product(0)
+        for i, (a, b) in enumerate(COMBINE):
+            if i + 1 < len(COMBINE):
+                product(i + 1)
             own = tile([P, b - a], F32, "sum%d" % a)
-            nc.vector.tensor_tensor(own[:], part[0][:], part[1][:], ALU.add)
+            nc.vector.tensor_tensor(own[:], first[:, a:b], second[i][:], ALU.add)
             nc.sync.dma_start(out[:, a:b], own[:])

@@ -22,6 +22,7 @@ PASSES = 2
 CH = 512
 NCH = S // CH
 LC = 16
+WIDE = 2048
 COMBINE = ((0, 384), (384, 640), (640, 768))
 
 
@@ -43,15 +44,20 @@ def tile_moe_loc_lin_relu_kernel(
         l_far = tile([P, S // LC], U16, "l_far")
         l_pos = [tile([P, T // LC], U16, "l_pos%d" % r) for r in range(2)]
 
-        xs = tile([P, Q], U8, "xs")
+        xs = tile([P, WIDE], U8, "xs")
         far_s1 = tile([P, S], U8, "far_s1")
         ws = tile([P, E * PASSES * N], U8, "ws")
         nc.vector.memset(xs[:].bitcast(I32), 0)
-        nc.vector.memset(ws[:].bitcast(I32), 0)
-        nc.vector.memset(far_s1[:].bitcast(I32), 0)
+        nc.gpsimd.memset(ws[:].bitcast(I32), 0)
+        nc.gpsimd.memset(far_s1[:].bitcast(I32), 0)
+
+        table = tile([P, 2 * (T + WIDE)], BF16, "table")
+        nc.vector.memset(table[:, 4 * T :].bitcast(I32), 0)
 
         xw = [tile([P, Q], I32, "xw%d" % s) for s in range(PASSES)]
-        raw = {i: tile([P, 2, T], F32, "raw%d" % i, tag="slot_d" if i == 3 else None) for i in range(1, 4)}
+        raw = {i: tile([P, 2, T], F32, "raw%d" % i) for i in range(1, 3)}
+        last_raw = [tile([P, T], F32, "last_raw%d" % e) for e in range(2)]
+        single = [tile([P, T], BF16, "single%d" % e) for e in range(2)]
         xo_v = xo.rearrange("(s p u e) t -> s u p e t", s=PASSES, u=2, e=2)
 
         def load_xw(s):
@@ -60,18 +66,20 @@ def tile_moe_loc_lin_relu_kernel(
         def load_raw(i):
             nc.sync.dma_start(raw[i][:], xo_v[i // 2, i % 2])
 
-        nc.sync.dma_start(l_far[:], offs2)
         load_xw(0)
+        nc.sync.dma_start(l_far[:], offs2)
         first_raw = [tile([P, 2, T // 2], F32, "first_raw%d" % h) for h in range(2)]
         for h in range(2):
             nc.sync.dma_start(first_raw[h][:], xo_v[0, 0, :, :, h * T // 2 : (h + 1) * T // 2])
         nc.sync.dma_start(l_own[:], offs)
-        for i in range(1, 4):
-            load_raw(i)
+        nc.sync.dma_start(last_raw[0][:], xo_v[1, 1, :, 0, :])
+        load_raw(1)
+        load_raw(2)
+        nc.sync.dma_start(last_raw[1][:], xo_v[1, 1, :, 1, :])
         load_xw(1)
         xs_v = x_scales.bitcast(I32)
         for q in range(4):
-            nc.sync.dma_start(xs[32 * q : 32 * q + 8, :].bitcast(I32), xs_v[:, 4 * q : 4 * q + 4, :])
+            nc.sync.dma_start(xs[32 * q : 32 * q + 8, :Q].bitcast(I32), xs_v[:, 4 * q : 4 * q + 4, :])
         ws_v = w_scales.bitcast(I32).rearrange("e s (q r) n -> r q (e s) n", r=4)
         ws_i = ws[:].bitcast(I32).rearrange("p (g n) -> p g n", n=N // 4)
         for r in range(4):
@@ -85,20 +93,21 @@ def tile_moe_loc_lin_relu_kernel(
         far_w1a = tile([P, CH], U32, "far_w1a")
         nc.vector.tensor_copy(far_w1a[:], xw[1][:].bitcast(U32).indirect(cut(l_far, 0, CH)))
 
-        pairs = [tile([P, 2 * T], BF16, "pairs%d" % i) for i in range(4)]
+        pairs = [table[:, 2 * T : 4 * T], table[:, : 2 * T], tile([P, 2 * T], BF16, "pairs2")]
         for h in range(2):
             nc.scalar.activation(
                 pairs[0][:, h * T : (h + 1) * T].rearrange("p (t e) -> p t e", e=2),
                 first_raw[h][:].rearrange("p e t -> p t e"),
                 ACT.Copy,
             )
+        nc.scalar.activation(single[0][:], last_raw[0][:], ACT.Copy)
         for i in range(1, 3):
             nc.scalar.activation(
                 pairs[i][:].rearrange("p (t e) -> p t e", e=2), raw[i][:].rearrange("p e t -> p t e"), ACT.Copy
             )
-        nc.scalar.activation(pairs[3][:], raw[3][:].rearrange("p e t -> p (e t)"), ACT.Copy)
+        nc.scalar.activation(single[1][:], last_raw[1][:], ACT.Copy)
 
-        ww = tile([P, E * PASSES * 2 * N], U8, "ww", "raw1")
+        ww = tile([P, E * PASSES * 2 * N], U8, "ww", "last_raw0")
         nc.sync.dma_start(
             ww[:].bitcast(I32).rearrange("p (g n) -> p g n", n=N // 2),
             w_words.bitcast(I32).rearrange("e s p n -> p (e s) n"),
@@ -107,27 +116,19 @@ def tile_moe_loc_lin_relu_kernel(
         for r in range(2):
             nc.sync.dma_start(g[r][:], gate[r])
 
-        def gather(dst, s, u, c):
-            nc.vector.tensor_copy(
-                dst[:, u * CH : (u + 1) * CH],
-                pairs[2 * s + u][:].bitcast(U32).indirect(cut(l_own, c * CH, (c + 1) * CH)),
-            )
+        def gather(dst, i):
+            at = (1 - i) * T
+            nc.vector.tensor_copy(dst, table[:].bitcast(U32)[:, at : at + WIDE].indirect(l_own[:]))
 
         codes = [[tile([P, CH], U32, "codes%d%d" % (s, c)) for c in range(NCH)] for s in range(PASSES)]
         scales = [[tile([P, CH], U8, "scales%d%d" % (s, c)) for c in range(NCH)] for s in range(PASSES)]
 
-        def weave(src, name, tag, on_vector=False):
+        def weave(src, name, tag):
             woven = tile([P, 4 * CH], BF16, name, tag)
-            if on_vector:
-                nc.vector.tensor_copy(
-                    woven[:].bitcast(I32).rearrange("p (j u) -> p j u", u=2),
-                    src[:].bitcast(I32).rearrange("p (u j) -> p j u", u=2),
-                )
-            else:
-                nc.scalar.copy(
-                    woven[:].bitcast(U32).rearrange("p (j u) -> p j u", u=2),
-                    src[:].rearrange("p (u j) -> p j u", u=2),
-                )
+            nc.scalar.copy(
+                woven[:].bitcast(U32).rearrange("p (j u) -> p j u", u=2),
+                src,
+            )
             return woven
 
         def gather_single(dst, c):
@@ -135,39 +136,39 @@ def tile_moe_loc_lin_relu_kernel(
             for e in range(2):
                 nc.scalar.activation(
                     half[:, e, :],
-                    pairs[3][:, e * T : (e + 1) * T].indirect(cut(l_own, c * CH, (c + 1) * CH)),
+                    single[e][:].indirect(cut(l_own, c * CH, (c + 1) * CH)),
                     ACT.Copy,
                 )
 
         def quantize(woven, s, c):
             nc.vector.quantize_mx(codes[s][c][:].bitcast(FP8X4), scales[s][c][:], woven[:])
 
-        got0 = [tile([P, 2 * CH], U32, "got0%d" % c) for c in range(NCH)]
+        got0 = tile([P, 2 * S], U32, "got0")
         for u in range(2):
-            for c in range(NCH):
-                gather(got0[c], 0, u, c)
-
-        on_vector = ()
-        early = [weave(got0[c], "woven0%d" % c, None, True) for c in on_vector]
-        got1 = [tile([P, 2 * CH], U32, "got1%d" % c) for c in range(NCH)]
+            gather(got0[:, u * S : (u + 1) * S], u)
+        got1_first = tile([P, 2 * CH], U32, "got1_first")
+        got1_rest = tile([P, 4 * CH], U32, "got1_rest", "raw2")
+        got1 = [got1_first[:], got1_rest[:, : 2 * CH], got1_rest[:, 2 * CH :]]
         for c in range(NCH):
-            gather(got1[c], 1, 0, c)
-        for c, woven in zip(on_vector, early):
-            quantize(woven, 0, c)
+            nc.vector.tensor_copy(
+                got1[c][:, :CH], pairs[2][:].bitcast(U32).indirect(cut(l_own, c * CH, (c + 1) * CH))
+            )
+        slot0 = ("last_raw1", "got1_first", "last_raw1")
 
         far_s = tile([P, S], U8, "far_s", "pairs2")
-        for a, b in ((0, S // 2), (S // 2, S)):
-            nc.vector.tensor_copy(far_s[:, a:b], xs[:].indirect(cut(l_far, a, b)))
+        nc.vector.tensor_copy(far_s[:], xs[:].indirect(l_far[:]))
         for q in range(4):
             nc.sync.dma_start(
                 far_s1[32 * q : 32 * q + 4, :].bitcast(I32), far_s[32 * q + 4 : 32 * q + 8, :].bitcast(I32)
             )
 
+        got0_woven = got0[:].rearrange("p (u j) -> p j u", u=2)
+        gather_single(got1[0], 0)
         for c in range(NCH):
-            gather_single(got1[c], c)
-            if c not in on_vector:
-                quantize(weave(got0[c], "woven0%d" % c, "slot_d" if c == 0 else "got1%d" % (c - 1)), 0, c)
-            quantize(weave(got1[c], "woven1%d" % c, "woven1%d" % c), 1, c)
+            if c + 1 < NCH:
+                gather_single(got1[c + 1], c + 1)
+            quantize(weave(got0_woven[:, c * CH : (c + 1) * CH, :], "woven0%d" % c, slot0[c]), 0, c)
+            quantize(weave(got1[c].rearrange("p (u j) -> p j u", u=2), "woven1%d" % c, "woven1%d" % c), 1, c)
 
         far_w1b = tile([P, S - CH], U32, "far_w1b", "woven1%d" % (NCH - 1))
         for c in range(1, NCH):
@@ -221,4 +222,5 @@ def tile_moe_loc_lin_relu_kernel(
                 product(i + 1)
             own = tile([P, b - a], F32, "sum%d" % a)
             nc.vector.tensor_tensor(own[:], first[:, a:b], second[i][:], ALU.add)
-            nc.sync.dma_start(out[:, a:b], own[:])
+            queue = nc.scalar if b == T else nc.sync
+            queue.dma_start(out[:, a:b], own[:])

@@ -44,7 +44,7 @@ def tile_moe_loc_lin_relu_kernel(
         l_far = tile([P, S // LC], U16, "l_far")
         l_pos = [tile([P, T // LC], U16, "l_pos%d" % r) for r in range(2)]
 
-        xs = tile([P, WIDE], U8, "xs")
+        xs = tile([P, Q], U8, "xs")
         far_s1 = tile([P, S], U8, "far_s1")
         ws = tile([P, E * PASSES * N], U8, "ws")
         nc.vector.memset(xs[:].bitcast(I32), 0)
@@ -55,9 +55,11 @@ def tile_moe_loc_lin_relu_kernel(
         nc.vector.memset(table[:, 4 * T :].bitcast(I32), 0)
 
         xw = [tile([P, Q], I32, "xw%d" % s) for s in range(PASSES)]
-        raw = {i: tile([P, 2, T], F32, "raw%d" % i) for i in range(1, 3)}
-        last_raw = [tile([P, T], F32, "last_raw%d" % e) for e in range(2)]
-        single = [tile([P, T], BF16, "single%d" % e) for e in range(2)]
+        raw = {i: tile([P, 2, T], F32, "raw%d" % i) for i in range(1, 2)}
+        last_raw = [tile([P, T], F32, "last_raw%d" % e) for e in range(4)]
+        singles = tile([P, 3 * T + WIDE], BF16, "singles")
+        nc.gpsimd.memset(singles[:, 4 * T :].bitcast(I32), 0)
+        single = [singles[:, (3 - d) * T : (4 - d) * T] for d in range(4)]
         xo_v = xo.rearrange("(s p u e) t -> s u p e t", s=PASSES, u=2, e=2)
 
         def load_xw(s):
@@ -72,14 +74,14 @@ def tile_moe_loc_lin_relu_kernel(
         for h in range(2):
             nc.sync.dma_start(first_raw[h][:], xo_v[0, 0, :, :, h * T // 2 : (h + 1) * T // 2])
         nc.sync.dma_start(l_own[:], offs)
-        nc.sync.dma_start(last_raw[0][:], xo_v[1, 1, :, 0, :])
+        nc.sync.dma_start(last_raw[0][:], xo_v[1, 0, :, 0, :])
         load_raw(1)
-        load_raw(2)
-        nc.sync.dma_start(last_raw[1][:], xo_v[1, 1, :, 1, :])
-        load_xw(1)
         xs_v = x_scales.bitcast(I32)
         for q in range(4):
             nc.sync.dma_start(xs[32 * q : 32 * q + 8, :Q].bitcast(I32), xs_v[:, 4 * q : 4 * q + 4, :])
+        for d in range(1, 4):
+            nc.sync.dma_start(last_raw[d][:], xo_v[1, d // 2, :, d % 2, :])
+        load_xw(1)
         ws_v = w_scales.bitcast(I32).rearrange("e s (q r) n -> r q (e s) n", r=4)
         ws_i = ws[:].bitcast(I32).rearrange("p (g n) -> p g n", n=N // 4)
         for r in range(4):
@@ -93,19 +95,20 @@ def tile_moe_loc_lin_relu_kernel(
         far_w1a = tile([P, CH], U32, "far_w1a")
         nc.vector.tensor_copy(far_w1a[:], xw[1][:].bitcast(U32).indirect(cut(l_far, 0, CH)))
 
-        pairs = [table[:, 2 * T : 4 * T], table[:, : 2 * T], tile([P, 2 * T], BF16, "pairs2")]
+        pairs = [table[:, 2 * T : 4 * T], table[:, : 2 * T]]
         for h in range(2):
             nc.scalar.activation(
                 pairs[0][:, h * T : (h + 1) * T].rearrange("p (t e) -> p t e", e=2),
                 first_raw[h][:].rearrange("p e t -> p t e"),
                 ACT.Copy,
             )
-        nc.scalar.activation(single[0][:], last_raw[0][:], ACT.Copy)
-        for i in range(1, 3):
-            nc.scalar.activation(
-                pairs[i][:].rearrange("p (t e) -> p t e", e=2), raw[i][:].rearrange("p e t -> p t e"), ACT.Copy
-            )
-        nc.scalar.activation(single[1][:], last_raw[1][:], ACT.Copy)
+        def round_on_gpsimd(dst, src):
+            nc.gpsimd.tensor_scalar(dst, src, 1.0, 0.0, ALU.mult, ALU.add)
+
+        nc.scalar.activation(single[0], last_raw[0][:], ACT.Copy)
+        round_on_gpsimd(pairs[1].rearrange("p (t e) -> p t e", e=2), raw[1][:].rearrange("p e t -> p t e"))
+        for d in range(1, 4):
+            round_on_gpsimd(single[d], last_raw[d][:])
 
         ww = tile([P, E * PASSES * 2 * N], U8, "ww", "last_raw0")
         nc.sync.dma_start(
@@ -123,22 +126,21 @@ def tile_moe_loc_lin_relu_kernel(
         codes = [[tile([P, CH], U32, "codes%d%d" % (s, c)) for c in range(NCH)] for s in range(PASSES)]
         scales = [[tile([P, CH], U8, "scales%d%d" % (s, c)) for c in range(NCH)] for s in range(PASSES)]
 
-        def weave(src, name, tag):
-            woven = tile([P, 4 * CH], BF16, name, tag)
-            nc.scalar.copy(
-                woven[:].bitcast(U32).rearrange("p (j u) -> p j u", u=2),
-                src,
-            )
+        def weave(src, name, on_vector):
+            woven = tile([P, 4 * CH], BF16, name)
+            if on_vector:
+                nc.vector.tensor_copy(
+                    woven[:].bitcast(I32).rearrange("p (j u) -> p j u", u=2),
+                    src.bitcast(I32).rearrange("p u j -> p j u"),
+                )
+            else:
+                nc.scalar.copy(woven[:].bitcast(U32).rearrange("p (j u) -> p j u", u=2), src.rearrange("p u j -> p j u"))
             return woven
 
-        def gather_single(dst, c):
-            half = dst[:, CH : 2 * CH].bitcast(BF16).rearrange("p (j e) -> p e j", e=2)
-            for e in range(2):
-                nc.scalar.activation(
-                    half[:, e, :],
-                    single[e][:].indirect(cut(l_own, c * CH, (c + 1) * CH)),
-                    ACT.Copy,
-                )
+        def gather_single(dst, d, a, b, width):
+            at = (3 - d) * T
+            half = dst[:, (d // 2) * S + a : (d // 2) * S + b].bitcast(BF16).rearrange("p (j e) -> p e j", e=2)
+            nc.scalar.activation(half[:, d % 2, :], singles[:, at : at + width].indirect(cut(l_own, a, b)), ACT.Copy)
 
         def quantize(woven, s, c):
             nc.vector.quantize_mx(codes[s][c][:].bitcast(FP8X4), scales[s][c][:], woven[:])
@@ -146,29 +148,33 @@ def tile_moe_loc_lin_relu_kernel(
         got0 = tile([P, 2 * S], U32, "got0")
         for u in range(2):
             gather(got0[:, u * S : (u + 1) * S], u)
-        got1_first = tile([P, 2 * CH], U32, "got1_first")
-        got1_rest = tile([P, 4 * CH], U32, "got1_rest", "raw2")
-        got1 = [got1_first[:], got1_rest[:, : 2 * CH], got1_rest[:, 2 * CH :]]
+        got0_v = got0[:].rearrange("p (u j) -> p u j", u=2)
+        woven0 = [weave(got0_v[:, :, c * CH : (c + 1) * CH], "woven0%d" % c, True) for c in range(NCH)]
         for c in range(NCH):
-            nc.vector.tensor_copy(
-                got1[c][:, :CH], pairs[2][:].bitcast(U32).indirect(cut(l_own, c * CH, (c + 1) * CH))
-            )
-        slot0 = ("last_raw1", "got1_first", "last_raw1")
+            quantize(woven0[c], 0, c)
+        got1 = tile([P, 2 * S], U32, "got1")
+        got1_v = got1[:].rearrange("p (u j) -> p u j", u=2)
+        for d in range(3):
+            gather_single(got1, d, 0, S, WIDE)
 
-        far_s = tile([P, S], U8, "far_s", "pairs2")
-        nc.vector.tensor_copy(far_s[:], xs[:].indirect(l_far[:]))
-        for q in range(4):
-            nc.sync.dma_start(
-                far_s1[32 * q : 32 * q + 4, :].bitcast(I32), far_s[32 * q + 4 : 32 * q + 8, :].bitcast(I32)
-            )
+        half = S // 2
 
-        got0_woven = got0[:].rearrange("p (u j) -> p j u", u=2)
-        gather_single(got1[0], 0)
+        def far_bytes(h, slot):
+            got = tile([P, half], U8, "far_s%d" % h, slot)
+            nc.vector.tensor_copy(got[:], xs[:].indirect(cut(l_far, h * half, (h + 1) * half)))
+            for q in range(4):
+                nc.sync.dma_start(
+                    far_s1[32 * q : 32 * q + 4, h * half : (h + 1) * half].bitcast(I32),
+                    got[32 * q + 4 : 32 * q + 8, :].bitcast(I32),
+                )
+            return got
+
+        far_s = [far_bytes(0, "woven02")]
         for c in range(NCH):
-            if c + 1 < NCH:
-                gather_single(got1[c + 1], c + 1)
-            quantize(weave(got0_woven[:, c * CH : (c + 1) * CH, :], "woven0%d" % c, slot0[c]), 0, c)
-            quantize(weave(got1[c].rearrange("p (u j) -> p j u", u=2), "woven1%d" % c, "woven1%d" % c), 1, c)
+            gather_single(got1, 3, c * CH, (c + 1) * CH, T)
+            quantize(weave(got1_v[:, :, c * CH : (c + 1) * CH], "woven1%d" % c, c == 0), 1, c)
+            if c == 1:
+                far_s.append(far_bytes(1, "woven11"))
 
         far_w1b = tile([P, S - CH], U32, "far_w1b", "woven1%d" % (NCH - 1))
         for c in range(1, NCH):
@@ -187,23 +193,33 @@ def tile_moe_loc_lin_relu_kernel(
                         lhsT=ww[:, i * 2 * N : (i + 1) * 2 * N].bitcast(FP4X4),
                         lhsT_scale=ws[:, i * N : (i + 1) * N],
                         rhs=words[s][:, j * C : (j + 1) * C].bitcast(FP8X4),
-                        rhs_scale=planes[s][:, j * C : (j + 1) * C],
+                        rhs_scale=planes(s, e),
                         start=(s == 0),
                         stop=(s == PASSES - 1),
                     )
             return bank
 
+        def own_plane(s, e):
+            j = e % (CH // C)
+            return scales[s][e // (CH // C)][:, j * C : (j + 1) * C]
+
+        def far_plane(s, e):
+            if s == 1:
+                return far_s1[:, e * C : (e + 1) * C]
+            j = e % (E // 2)
+            return far_s[e // (E // 2)][:, j * C : (j + 1) * C]
+
         y = tile([P, S], F32, "y")
         for c in range(NCH):
             bank = experts(
-                c, "own%d" % c, "own%d" % c, [codes[s][c] for s in range(PASSES)], [scales[s][c] for s in range(PASSES)]
+                c, "own%d" % c, "own%d" % c, [codes[s][c] for s in range(PASSES)], own_plane
             )
             nc.scalar.activation(y[:, c * CH : (c + 1) * CH], bank[:], ACT.Relu)
 
         for c in range(NCH):
             cols = slice(c * CH, (c + 1) * CH)
             w1 = far_w1a[:] if c == 0 else far_w1b[:, (c - 1) * CH : c * CH]
-            bank = experts(c, "far%d" % c, "own2" if c == 0 else "far%d" % c, [far_w0[:, cols], w1], [far_s[:, cols], far_s1[:, cols]])
+            bank = experts(c, "far%d" % c, "own2" if c == 0 else "far%d" % c, [far_w0[:, cols], w1], far_plane)
             z = tile([P, CH], F32, "z%d" % c)
             nc.scalar.activation(z[:], bank[:], ACT.Relu)
             nc.sync.dma_start(out[:, T + c * CH : T + (c + 1) * CH], z[:])
@@ -222,5 +238,4 @@ def tile_moe_loc_lin_relu_kernel(
                 product(i + 1)
             own = tile([P, b - a], F32, "sum%d" % a)
             nc.vector.tensor_tensor(own[:], first[:, a:b], second[i][:], ALU.add)
-            queue = nc.scalar if b == T else nc.sync
-            queue.dma_start(out[:, a:b], own[:])
+            nc.sync.dma_start(out[:, a:b], own[:])

@@ -18,12 +18,16 @@ ACT = mybir.ActivationFunctionType
 ALU = mybir.AluOpType
 
 P = 128
-PASSES = 2
-CH = 512
-NCH = S // CH
-LC = 16
+PASSES = K // 512
+PACK = 4
+QUADRANTS = 4
+CHUNK = 512
+CHUNKS = S // CHUNK
+PER_CHUNK = CHUNK // C
+LIST_ROWS = 16
 WIDE = 2048
-COMBINE = ((0, 384), (384, 640), (640, 768))
+HALVES = ((0, S // 2), (S // 2, S))
+COMBINE = ((0, 384), (384, 640), (640, T))
 
 
 def tile_moe_loc_lin_relu_kernel(
@@ -34,208 +38,181 @@ def tile_moe_loc_lin_relu_kernel(
         sb = ctx.enter_context(tc.tile_pool(name="sb", bufs=1))
         ps = ctx.enter_context(tc.psum_pool(name="ps", bufs=1))
 
-        def tile(shape, dtype, name, tag=None):
-            return sb.tile(shape, dtype, name=name, tag=tag or name, align_bytes=64)
+        def tile(shape, dtype, name, after=None):
+            return sb.tile(shape, dtype, name=name, tag=after or name, align_bytes=64)
 
-        def cut(lst, a, b):
-            return lst[:, a // LC : b // LC]
+        def entries(lst, a, b):
+            return lst[:, a // LIST_ROWS : b // LIST_ROWS]
 
-        l_own = tile([P, S // LC], U16, "l_own")
-        l_far = tile([P, S // LC], U16, "l_far")
-        l_pos = [tile([P, T // LC], U16, "l_pos%d" % r) for r in range(2)]
+        own_list = tile([P, S // LIST_ROWS], U16, "own_list")
+        far_list = tile([P, S // LIST_ROWS], U16, "far_list")
+        pos_list = [tile([P, T // LIST_ROWS], U16, "pos_list%d" % r) for r in range(2)]
 
-        xs = tile([P, Q], U8, "xs")
-        far_s1 = tile([P, S], U8, "far_s1")
-        ws = tile([P, E * PASSES * N], U8, "ws")
-        nc.vector.memset(xs[:].bitcast(I32), 0)
-        nc.gpsimd.memset(ws[:].bitcast(I32), 0)
-        nc.gpsimd.memset(far_s1[:].bitcast(I32), 0)
+        far_scale_table = tile([P, Q], U8, "far_scale_table")
+        singles = tile([P, (PACK - 1) * T + WIDE], BF16, "singles")
+        pairs = tile([P, 2 * (T + WIDE)], BF16, "pairs")
+        w_scale = tile([P, E * PASSES * N], U8, "w_scale")
+        far_scale1 = tile([P, S], U8, "far_scale1")
+        for zeroed in (far_scale_table[:], singles[:, PACK * T :], pairs[:, PACK * T :], w_scale[:], far_scale1[:]):
+            nc.gpsimd.memset(zeroed.bitcast(I32), 0)
 
-        table = tile([P, 2 * (T + WIDE)], BF16, "table")
-        nc.vector.memset(table[:, 4 * T :].bitcast(I32), 0)
+        xo_k = xo.rearrange("(s p u e) t -> s u p e t", s=PASSES, u=2, e=2)
+        far_table = [tile([P, Q], I32, "far_table%d" % s) for s in range(PASSES)]
+        raw_pair = [tile([P, 2, T], F32, "raw_pair%d" % u) for u in range(2)]
+        raw_single = [tile([P, T], F32, "raw_single%d" % d) for d in range(PACK)]
 
-        xw = [tile([P, Q], I32, "xw%d" % s) for s in range(PASSES)]
-        raw = {i: tile([P, 2, T], F32, "raw%d" % i) for i in range(1, 2)}
-        last_raw = [tile([P, T], F32, "last_raw%d" % e) for e in range(4)]
-        singles = tile([P, 3 * T + WIDE], BF16, "singles")
-        nc.gpsimd.memset(singles[:, 4 * T :].bitcast(I32), 0)
-        single = [singles[:, (3 - d) * T : (4 - d) * T] for d in range(4)]
-        xo_v = xo.rearrange("(s p u e) t -> s u p e t", s=PASSES, u=2, e=2)
+        def load_far_words(s):
+            nc.sync.dma_start(far_table[s][:], x_words[s].rearrange("p t d -> p (t d)").bitcast(I32))
 
-        def load_xw(s):
-            nc.sync.dma_start(xw[s][:], x_words[s].rearrange("p t d -> p (t d)").bitcast(I32))
+        def load_single(d):
+            nc.sync.dma_start(raw_single[d][:], xo_k[1, d // 2, :, d % 2, :])
 
-        def load_raw(i):
-            nc.sync.dma_start(raw[i][:], xo_v[i // 2, i % 2])
-
-        load_xw(0)
-        nc.sync.dma_start(l_far[:], offs2)
-        first_raw = [tile([P, 2, T // 2], F32, "first_raw%d" % h) for h in range(2)]
-        for h in range(2):
-            nc.sync.dma_start(first_raw[h][:], xo_v[0, 0, :, :, h * T // 2 : (h + 1) * T // 2])
-        nc.sync.dma_start(l_own[:], offs)
-        nc.sync.dma_start(last_raw[0][:], xo_v[1, 0, :, 0, :])
-        load_raw(1)
-        xs_v = x_scales.bitcast(I32)
-        for q in range(4):
-            nc.sync.dma_start(xs[32 * q : 32 * q + 8, :Q].bitcast(I32), xs_v[:, 4 * q : 4 * q + 4, :])
-        for d in range(1, 4):
-            nc.sync.dma_start(last_raw[d][:], xo_v[1, d // 2, :, d % 2, :])
-        load_xw(1)
-        ws_v = w_scales.bitcast(I32).rearrange("e s (q r) n -> r q (e s) n", r=4)
-        ws_i = ws[:].bitcast(I32).rearrange("p (g n) -> p g n", n=N // 4)
-        for r in range(4):
-            nc.sync.dma_start(ws_i[r:P:32, :, :], ws_v[r])
-        nc.sync.dma_start(l_pos[0][:], pos1)
-        nc.sync.dma_start(l_pos[1][:], pos2)
-
-        far_w0 = tile([P, S], U32, "far_w0")
-        for a, b in ((0, S // 2), (S // 2, S)):
-            nc.vector.tensor_copy(far_w0[:, a:b], xw[0][:].bitcast(U32).indirect(cut(l_far, a, b)))
-        far_w1a = tile([P, CH], U32, "far_w1a")
-        nc.vector.tensor_copy(far_w1a[:], xw[1][:].bitcast(U32).indirect(cut(l_far, 0, CH)))
-
-        pairs = [table[:, 2 * T : 4 * T], table[:, : 2 * T]]
-        for h in range(2):
-            nc.scalar.activation(
-                pairs[0][:, h * T : (h + 1) * T].rearrange("p (t e) -> p t e", e=2),
-                first_raw[h][:].rearrange("p e t -> p t e"),
-                ACT.Copy,
+        nc.sync.dma_start(far_list[:], offs2)
+        for q in range(QUADRANTS):
+            nc.sync.dma_start(
+                far_scale_table[32 * q : 32 * q + 8, :].bitcast(I32), x_scales.bitcast(I32)[:, 4 * q : 4 * q + 4, :]
             )
+        load_single(0)
+        nc.sync.dma_start(own_list[:], offs)
+        load_far_words(0)
+        for u in range(2):
+            load_single(u + 1)
+            nc.sync.dma_start(raw_pair[u][:], xo_k[0, u])
+        load_single(PACK - 1)
+        load_far_words(1)
+        w_scale_rows = w_scales.bitcast(I32).rearrange("e s (q r) n -> r q (e s) n", r=4)
+        w_scale_words = w_scale[:].bitcast(I32).rearrange("p (g n) -> p g n", n=N // 4)
+        for r in range(4):
+            nc.sync.dma_start(w_scale_words[r:P:32, :, :], w_scale_rows[r])
+        nc.sync.dma_start(pos_list[0][:], pos1)
+        nc.sync.dma_start(pos_list[1][:], pos2)
+
+        far_scale0 = tile([P, S], U8, "far_scale0")
+        for a, b in HALVES:
+            nc.vector.tensor_copy(far_scale0[:, a:b], far_scale_table[:].indirect(entries(far_list, a, b)))
+        far_words0 = tile([P, S], U32, "far_words0")
+        for a, b in HALVES:
+            nc.vector.tensor_copy(far_words0[:, a:b], far_table[0][:].bitcast(U32).indirect(entries(far_list, a, b)))
+        for q in range(QUADRANTS):
+            nc.sync.dma_start(
+                far_scale1[32 * q : 32 * q + 4, :].bitcast(I32), far_scale0[32 * q + 4 : 32 * q + 8, :].bitcast(I32)
+            )
+
+        single_at = [(PACK - 1 - d) * T for d in range(PACK)]
+        pair_at = [(1 - u) * T for u in range(2)]
+
         def round_on_gpsimd(dst, src):
             nc.gpsimd.tensor_scalar(dst, src, 1.0, 0.0, ALU.mult, ALU.add)
 
-        nc.scalar.activation(single[0], last_raw[0][:], ACT.Copy)
-        round_on_gpsimd(pairs[1].rearrange("p (t e) -> p t e", e=2), raw[1][:].rearrange("p e t -> p t e"))
-        for d in range(1, 4):
-            round_on_gpsimd(single[d], last_raw[d][:])
+        def single(d):
+            return singles[:, single_at[d] : single_at[d] + T]
 
-        ww = tile([P, E * PASSES * 2 * N], U8, "ww", "last_raw0")
+        nc.scalar.activation(single(0), raw_single[0][:], ACT.Copy)
+        for u in range(2):
+            round_on_gpsimd(single(u + 1), raw_single[u + 1][:])
+            pair = pairs[:, 2 * pair_at[u] : 2 * (pair_at[u] + T)]
+            round_on_gpsimd(pair.rearrange("p (t e) -> p t e", e=2), raw_pair[u][:].rearrange("p e t -> p t e"))
+        round_on_gpsimd(single(PACK - 1), raw_single[PACK - 1][:])
+
+        w_code = tile([P, E * PASSES * 2 * N], U8, "w_code", "raw_pair0")
         nc.sync.dma_start(
-            ww[:].bitcast(I32).rearrange("p (g n) -> p g n", n=N // 2),
+            w_code[:].bitcast(I32).rearrange("p (g n) -> p g n", n=N // 2),
             w_words.bitcast(I32).rearrange("e s p n -> p (e s) n"),
         )
-        g = [tile([P, T], F32, "g%d" % r, "first_raw%d" % r) for r in range(2)]
+        gates = [tile([P, T], F32, "gate%d" % r, "raw_single%d" % (r + 1)) for r in range(2)]
         for r in range(2):
-            nc.sync.dma_start(g[r][:], gate[r])
+            nc.sync.dma_start(gates[r][:], gate[r])
 
-        def gather(dst, i):
-            at = (1 - i) * T
-            nc.vector.tensor_copy(dst, table[:].bitcast(U32)[:, at : at + WIDE].indirect(l_own[:]))
+        own_words = [[tile([P, CHUNK], U32, "own_words%d%d" % (s, c)) for c in range(CHUNKS)] for s in range(PASSES)]
+        own_scale = [[tile([P, CHUNK], U8, "own_scale%d%d" % (s, c)) for c in range(CHUNKS)] for s in range(PASSES)]
+        halves = [tile([P, 2 * S], U32, "halves%d" % s) for s in range(PASSES)]
 
-        codes = [[tile([P, CH], U32, "codes%d%d" % (s, c)) for c in range(NCH)] for s in range(PASSES)]
-        scales = [[tile([P, CH], U8, "scales%d%d" % (s, c)) for c in range(NCH)] for s in range(PASSES)]
-
-        def weave(src, name, on_vector):
-            woven = tile([P, 4 * CH], BF16, name)
-            if on_vector:
-                nc.vector.tensor_copy(
-                    woven[:].bitcast(I32).rearrange("p (j u) -> p j u", u=2),
-                    src.bitcast(I32).rearrange("p u j -> p j u"),
-                )
-            else:
-                nc.scalar.copy(woven[:].bitcast(U32).rearrange("p (j u) -> p j u", u=2), src.rearrange("p u j -> p j u"))
+        def weave(copy, dtype, s, c):
+            woven = tile([P, PACK * CHUNK], BF16, "woven%d%d" % (s, c))
+            src = halves[s][:].rearrange("p (u j) -> p u j", u=2)[:, :, c * CHUNK : (c + 1) * CHUNK]
+            copy(woven[:].bitcast(dtype).rearrange("p (j u) -> p j u", u=2), src.bitcast(dtype).rearrange("p u j -> p j u"))
             return woven
 
-        def gather_single(dst, d, a, b, width):
-            at = (3 - d) * T
-            half = dst[:, (d // 2) * S + a : (d // 2) * S + b].bitcast(BF16).rearrange("p (j e) -> p e j", e=2)
-            nc.scalar.activation(half[:, d % 2, :], singles[:, at : at + width].indirect(cut(l_own, a, b)), ACT.Copy)
-
         def quantize(woven, s, c):
-            nc.vector.quantize_mx(codes[s][c][:].bitcast(FP8X4), scales[s][c][:], woven[:])
+            nc.vector.quantize_mx(own_words[s][c][:].bitcast(FP8X4), own_scale[s][c][:], woven[:])
 
-        got0 = tile([P, 2 * S], U32, "got0")
-        for u in range(2):
-            gather(got0[:, u * S : (u + 1) * S], u)
-        got0_v = got0[:].rearrange("p (u j) -> p u j", u=2)
-        woven0 = [weave(got0_v[:, :, c * CH : (c + 1) * CH], "woven0%d" % c, True) for c in range(NCH)]
-        for c in range(NCH):
-            quantize(woven0[c], 0, c)
-        got1 = tile([P, 2 * S], U32, "got1")
-        got1_v = got1[:].rearrange("p (u j) -> p u j", u=2)
-        for d in range(3):
-            gather_single(got1, d, 0, S, WIDE)
+        def gather_single(d, a, b, width):
+            at = (d // 2) * S
+            dst = halves[1][:, at + a : at + b].bitcast(BF16).rearrange("p (j e) -> p e j", e=2)
+            window = singles[:, single_at[d] : single_at[d] + width]
+            nc.scalar.activation(dst[:, d % 2, :], window.indirect(entries(own_list, a, b)), ACT.Copy)
 
-        half = S // 2
-
-        def far_bytes(h, slot):
-            got = tile([P, half], U8, "far_s%d" % h, slot)
-            nc.vector.tensor_copy(got[:], xs[:].indirect(cut(l_far, h * half, (h + 1) * half)))
-            for q in range(4):
-                nc.sync.dma_start(
-                    far_s1[32 * q : 32 * q + 4, h * half : (h + 1) * half].bitcast(I32),
-                    got[32 * q + 4 : 32 * q + 8, :].bitcast(I32),
-                )
-            return got
-
-        far_s = [far_bytes(0, "woven02")]
-        for c in range(NCH):
-            gather_single(got1, 3, c * CH, (c + 1) * CH, T)
-            quantize(weave(got1_v[:, :, c * CH : (c + 1) * CH], "woven1%d" % c, c == 0), 1, c)
-            if c == 1:
-                far_s.append(far_bytes(1, "woven11"))
-
-        far_w1b = tile([P, S - CH], U32, "far_w1b", "woven1%d" % (NCH - 1))
-        for c in range(1, NCH):
+        def gather_far_words1(dst, c):
             nc.vector.tensor_copy(
-                far_w1b[:, (c - 1) * CH : c * CH], xw[1][:].bitcast(U32).indirect(cut(l_far, c * CH, (c + 1) * CH))
+                dst, far_table[1][:].bitcast(U32).indirect(entries(far_list, c * CHUNK, (c + 1) * CHUNK))
             )
 
-        def experts(c, name, tag, words, planes):
-            bank = ps.tile([P, CH], F32, name=name, tag=tag)
-            for j in range(CH // C):
-                e = c * (CH // C) + j
+        for u in range(2):
+            window = pairs[:].bitcast(U32)[:, pair_at[u] : pair_at[u] + WIDE]
+            nc.vector.tensor_copy(halves[0][:, u * S : (u + 1) * S], window.indirect(own_list[:]))
+        woven0 = [weave(nc.vector.tensor_copy, I32, 0, c) for c in range(CHUNKS)]
+        for c in range(CHUNKS):
+            quantize(woven0[c], 0, c)
+
+        for d in range(PACK - 1):
+            gather_single(d, 0, S, WIDE)
+        for c in range(CHUNKS):
+            gather_single(PACK - 1, c * CHUNK, (c + 1) * CHUNK, T)
+            quantize(weave(nc.scalar.copy, U32, 1, c), 1, c)
+            if c == CHUNKS - 2:
+                far_words1_first = tile([P, CHUNK], U32, "far_words1_first", "woven1%d" % c)
+                gather_far_words1(far_words1_first[:], 0)
+        far_words1_rest = tile([P, S - CHUNK], U32, "far_words1_rest", "woven1%d" % (CHUNKS - 1))
+        far_words1 = [far_words1_first[:]] + [far_words1_rest[:, c * CHUNK : (c + 1) * CHUNK] for c in range(CHUNKS - 1)]
+        for c in range(1, CHUNKS):
+            gather_far_words1(far_words1[c], c)
+
+        def experts(c, name, tag, words, scale):
+            bank = ps.tile([P, CHUNK], F32, name=name, tag=tag)
+            for j in range(PER_CHUNK):
+                slots = slice(j * C, (j + 1) * C)
                 for s in range(PASSES):
-                    i = e * PASSES + s
+                    i = (c * PER_CHUNK + j) * PASSES + s
                     nc.tensor.matmul_mx(
-                        bank[:, j * C : (j + 1) * C],
-                        lhsT=ww[:, i * 2 * N : (i + 1) * 2 * N].bitcast(FP4X4),
-                        lhsT_scale=ws[:, i * N : (i + 1) * N],
-                        rhs=words[s][:, j * C : (j + 1) * C].bitcast(FP8X4),
-                        rhs_scale=planes(s, e),
+                        bank[:, slots],
+                        lhsT=w_code[:, i * 2 * N : (i + 1) * 2 * N].bitcast(FP4X4),
+                        lhsT_scale=w_scale[:, i * N : (i + 1) * N],
+                        rhs=words[s][:, slots].bitcast(FP8X4),
+                        rhs_scale=scale[s][:, slots],
                         start=(s == 0),
                         stop=(s == PASSES - 1),
                     )
             return bank
 
-        def own_plane(s, e):
-            j = e % (CH // C)
-            return scales[s][e // (CH // C)][:, j * C : (j + 1) * C]
-
-        def far_plane(s, e):
-            if s == 1:
-                return far_s1[:, e * C : (e + 1) * C]
-            j = e % (E // 2)
-            return far_s[e // (E // 2)][:, j * C : (j + 1) * C]
-
         y = tile([P, S], F32, "y")
-        for c in range(NCH):
+        for c in range(CHUNKS):
+            words = [own_words[s][c] for s in range(PASSES)]
+            scale = [own_scale[s][c] for s in range(PASSES)]
+            bank = experts(c, "own%d" % c, "own%d" % c, words, scale)
+            nc.scalar.activation(y[:, c * CHUNK : (c + 1) * CHUNK], bank[:], ACT.Relu)
+
+        for c in range(CHUNKS):
+            cols = slice(c * CHUNK, (c + 1) * CHUNK)
+            tag = "own%d" % (CHUNKS - 1) if c == 0 else "far%d" % c
             bank = experts(
-                c, "own%d" % c, "own%d" % c, [codes[s][c] for s in range(PASSES)], own_plane
+                c, "far%d" % c, tag, [far_words0[:, cols], far_words1[c]], [far_scale0[:, cols], far_scale1[:, cols]]
             )
-            nc.scalar.activation(y[:, c * CH : (c + 1) * CH], bank[:], ACT.Relu)
-
-        for c in range(NCH):
-            cols = slice(c * CH, (c + 1) * CH)
-            w1 = far_w1a[:] if c == 0 else far_w1b[:, (c - 1) * CH : c * CH]
-            bank = experts(c, "far%d" % c, "own2" if c == 0 else "far%d" % c, [far_w0[:, cols], w1], far_plane)
-            z = tile([P, CH], F32, "z%d" % c)
+            z = tile([P, CHUNK], F32, "z%d" % c)
             nc.scalar.activation(z[:], bank[:], ACT.Relu)
-            nc.sync.dma_start(out[:, T + c * CH : T + (c + 1) * CH], z[:])
+            nc.sync.dma_start(out[:, T + c * CHUNK : T + (c + 1) * CHUNK], z[:])
 
-        first = tile([P, T], F32, "first", "xw1")
-        nc.vector.tensor_tensor(first[:], y[:].indirect(l_pos[0][:]), g[0][:], ALU.mult)
+        first = tile([P, T], F32, "first", "far_table1")
+        nc.vector.tensor_tensor(first[:], y[:].indirect(pos_list[0][:]), gates[0][:], ALU.mult)
         second = [tile([P, b - a], F32, "second%d" % a) for a, b in COMBINE]
 
-        def product(i):
+        def second_product(i):
             a, b = COMBINE[i]
-            nc.vector.tensor_tensor(second[i][:], y[:].indirect(cut(l_pos[1], a, b)), g[1][:, a:b], ALU.mult)
+            nc.vector.tensor_tensor(second[i][:], y[:].indirect(entries(pos_list[1], a, b)), gates[1][:, a:b], ALU.mult)
 
-        product(0)
+        second_product(0)
         for i, (a, b) in enumerate(COMBINE):
             if i + 1 < len(COMBINE):
-                product(i + 1)
-            own = tile([P, b - a], F32, "sum%d" % a)
-            nc.vector.tensor_tensor(own[:], first[:, a:b], second[i][:], ALU.add)
-            nc.sync.dma_start(out[:, a:b], own[:])
+                second_product(i + 1)
+            total = tile([P, b - a], F32, "total%d" % a)
+            nc.vector.tensor_tensor(total[:], first[:, a:b], second[i][:], ALU.add)
+            nc.sync.dma_start(out[:, a:b], total[:])

@@ -23,9 +23,8 @@ PACK = 4
 QUADRANTS = 4
 CHUNK = 512
 CHUNKS = S // CHUNK
-PER_CHUNK = CHUNK // C
+OWN = ((0, 512), (512, 1024), (1024, 1280), (1280, S))
 LIST_ROWS = 16
-WIDE = 2048
 HALVES = ((0, S // 2), (S // 2, S))
 COMBINE = ((0, 384), (384, 640), (640, T))
 
@@ -36,6 +35,7 @@ def tile_moe_loc_lin_relu_kernel(
     nc = tc.nc
     with ExitStack() as ctx:
         sb = ctx.enter_context(tc.tile_pool(name="sb", bufs=1))
+        heirs = ctx.enter_context(tc.tile_pool(name="heirs", bufs=1))
         ps = ctx.enter_context(tc.psum_pool(name="ps", bufs=1))
 
         def tile(shape, dtype, name, after=None):
@@ -49,16 +49,15 @@ def tile_moe_loc_lin_relu_kernel(
         pos_list = [tile([P, T // LIST_ROWS], U16, "pos_list%d" % r) for r in range(2)]
 
         far_scale_table = tile([P, Q], U8, "far_scale_table")
-        singles = tile([P, (PACK - 1) * T + WIDE], BF16, "singles")
-        pairs = tile([P, 2 * (T + WIDE)], BF16, "pairs")
         w_scale = tile([P, E * PASSES * N], U8, "w_scale")
         far_scale1 = tile([P, S], U8, "far_scale1")
-        for zeroed in (far_scale_table[:], singles[:, PACK * T :], pairs[:, PACK * T :], w_scale[:], far_scale1[:]):
-            nc.gpsimd.memset(zeroed.bitcast(I32), 0)
+        nc.vector.memset(far_scale_table[:].bitcast(I32), 0)
+        for zeroed in (w_scale, far_scale1):
+            nc.gpsimd.memset(zeroed[:].bitcast(I32), 0)
 
         xo_k = xo.rearrange("(s p u e) t -> s u p e t", s=PASSES, u=2, e=2)
         far_table = [tile([P, Q], I32, "far_table%d" % s) for s in range(PASSES)]
-        raw_pair = [tile([P, 2, T], F32, "raw_pair%d" % u) for u in range(2)]
+        raw_pair = [tile([P, 2, T], F32, "raw_pair0"), heirs.tile([P, 2, T], F32, name="raw_pair1", offset=6144, align_bytes=64)]
         raw_single = [tile([P, T], F32, "raw_single%d" % d) for d in range(PACK)]
 
         def load_far_words(s):
@@ -75,10 +74,11 @@ def tile_moe_loc_lin_relu_kernel(
         load_single(0)
         nc.sync.dma_start(own_list[:], offs)
         load_far_words(0)
-        for u in range(2):
-            load_single(u + 1)
-            nc.sync.dma_start(raw_pair[u][:], xo_k[0, u])
-        load_single(PACK - 1)
+        load_single(1)
+        load_single(2)
+        nc.sync.dma_start(raw_pair[0][:], xo_k[0, 0])
+        load_single(3)
+        nc.sync.dma_start(raw_pair[1][:], xo_k[0, 1])
         load_far_words(1)
         w_scale_rows = w_scales.bitcast(I32).rearrange("e s (q r) n -> r q (e s) n", r=4)
         w_scale_words = w_scale[:].bitcast(I32).rearrange("p (g n) -> p g n", n=N // 4)
@@ -86,6 +86,9 @@ def tile_moe_loc_lin_relu_kernel(
             nc.sync.dma_start(w_scale_words[r:P:32, :, :], w_scale_rows[r])
         nc.sync.dma_start(pos_list[0][:], pos1)
         nc.sync.dma_start(pos_list[1][:], pos2)
+
+        def chunk_entries(lst, c):
+            return entries(lst, c * CHUNK, (c + 1) * CHUNK)
 
         far_scale0 = tile([P, S], U8, "far_scale0")
         for a, b in HALVES:
@@ -98,21 +101,22 @@ def tile_moe_loc_lin_relu_kernel(
                 far_scale1[32 * q : 32 * q + 4, :].bitcast(I32), far_scale0[32 * q + 4 : 32 * q + 8, :].bitcast(I32)
             )
 
-        single_at = [(PACK - 1 - d) * T for d in range(PACK)]
-        pair_at = [(1 - u) * T for u in range(2)]
+        singles = [tile([P, T], BF16, "single%d" % d) for d in range(PACK)]
+        pairs = [tile([P, 2 * T], BF16, "pair%d" % u) for u in range(2)]
 
-        def round_on_gpsimd(dst, src):
+        def move_on_gpsimd(dst, src):
             nc.gpsimd.tensor_scalar(dst, src, 1.0, 0.0, ALU.mult, ALU.add)
 
-        def single(d):
-            return singles[:, single_at[d] : single_at[d] + T]
+        def round_pair(u):
+            move_on_gpsimd(pairs[u][:].rearrange("p (t e) -> p t e", e=2), raw_pair[u][:].rearrange("p e t -> p t e"))
 
-        nc.scalar.activation(single(0), raw_single[0][:], ACT.Copy)
-        for u in range(2):
-            round_on_gpsimd(single(u + 1), raw_single[u + 1][:])
-            pair = pairs[:, 2 * pair_at[u] : 2 * (pair_at[u] + T)]
-            round_on_gpsimd(pair.rearrange("p (t e) -> p t e", e=2), raw_pair[u][:].rearrange("p e t -> p t e"))
-        round_on_gpsimd(single(PACK - 1), raw_single[PACK - 1][:])
+        nc.scalar.activation(singles[0][:, : T // 2], raw_single[0][:, : T // 2], ACT.Copy)
+        move_on_gpsimd(singles[0][:, T // 2 :], raw_single[0][:, T // 2 :])
+        move_on_gpsimd(singles[1][:], raw_single[1][:])
+        move_on_gpsimd(singles[2][:], raw_single[2][:])
+        round_pair(0)
+        move_on_gpsimd(singles[3][:], raw_single[3][:])
+        round_pair(1)
 
         w_code = tile([P, E * PASSES * 2 * N], U8, "w_code", "raw_pair0")
         nc.sync.dma_start(
@@ -123,56 +127,76 @@ def tile_moe_loc_lin_relu_kernel(
         for r in range(2):
             nc.sync.dma_start(gates[r][:], gate[r])
 
-        own_words = [[tile([P, CHUNK], U32, "own_words%d%d" % (s, c)) for c in range(CHUNKS)] for s in range(PASSES)]
-        own_scale = [[tile([P, CHUNK], U8, "own_scale%d%d" % (s, c)) for c in range(CHUNKS)] for s in range(PASSES)]
-        halves = [tile([P, 2 * S], U32, "halves%d" % s) for s in range(PASSES)]
+        last = CHUNKS - 1
+        halves = [
+            [tile([P, 2 * CHUNK], U32, "halves0%d" % c) for c in range(CHUNKS)],
+            [tile([P, 2 * CHUNK], U32, "halves1%d" % c, "raw_single3" if c == last else None) for c in range(CHUNKS)],
+        ]
 
-        def weave(copy, dtype, s, c):
-            woven = tile([P, PACK * CHUNK], BF16, "woven%d%d" % (s, c))
-            src = halves[s][:].rearrange("p (u j) -> p u j", u=2)[:, :, c * CHUNK : (c + 1) * CHUNK]
-            copy(woven[:].bitcast(dtype).rearrange("p (j u) -> p j u", u=2), src.bitcast(dtype).rearrange("p u j -> p j u"))
-            return woven
+        def gather_single(d, c):
+            at = (d // 2) * CHUNK
+            dst = halves[1][c][:, at : at + CHUNK].bitcast(BF16).rearrange("p (j e) -> p e j", e=2)
+            nc.scalar.activation(dst[:, d % 2, :], singles[d][:].indirect(chunk_entries(own_list, c)), ACT.Copy)
 
-        def quantize(woven, s, c):
-            nc.vector.quantize_mx(own_words[s][c][:].bitcast(FP8X4), own_scale[s][c][:], woven[:])
-
-        def gather_single(d, a, b, width):
-            at = (d // 2) * S
-            dst = halves[1][:, at + a : at + b].bitcast(BF16).rearrange("p (j e) -> p e j", e=2)
-            window = singles[:, single_at[d] : single_at[d] + width]
-            nc.scalar.activation(dst[:, d % 2, :], window.indirect(entries(own_list, a, b)), ACT.Copy)
-
-        def gather_far_words1(dst, c):
+        def gather_pair(u, c):
             nc.vector.tensor_copy(
-                dst, far_table[1][:].bitcast(U32).indirect(entries(far_list, c * CHUNK, (c + 1) * CHUNK))
+                halves[0][c][:, u * CHUNK : (u + 1) * CHUNK], pairs[u][:].bitcast(U32).indirect(chunk_entries(own_list, c))
             )
 
-        for u in range(2):
-            window = pairs[:].bitcast(U32)[:, pair_at[u] : pair_at[u] + WIDE]
-            nc.vector.tensor_copy(halves[0][:, u * S : (u + 1) * S], window.indirect(own_list[:]))
-        woven0 = [weave(nc.vector.tensor_copy, I32, 0, c) for c in range(CHUNKS)]
-        for c in range(CHUNKS):
-            quantize(woven0[c], 0, c)
+        def gather_far_words1(dst, c):
+            nc.vector.tensor_copy(dst, far_table[1][:].bitcast(U32).indirect(chunk_entries(far_list, c)))
 
-        for d in range(PACK - 1):
-            gather_single(d, 0, S, WIDE)
+        def weave(copy, dtype, s, a, b):
+            woven = tile([P, PACK * (b - a)], BF16, "woven%d_%d" % (s, a))
+            at = a % CHUNK
+            src = halves[s][a // CHUNK][:].bitcast(dtype).rearrange("p (u j) -> p j u", u=2)[:, at : at + b - a, :]
+            copy(woven[:].bitcast(dtype).rearrange("p (j u) -> p j u", u=2), src)
+            return woven
+
+        for d in range(PACK):
+            for c in range(last):
+                gather_single(d, c)
+        for d in range(PACK):
+            gather_single(d, last)
         for c in range(CHUNKS):
-            gather_single(PACK - 1, c * CHUNK, (c + 1) * CHUNK, T)
-            quantize(weave(nc.scalar.copy, U32, 1, c), 1, c)
-            if c == CHUNKS - 2:
-                far_words1_first = tile([P, CHUNK], U32, "far_words1_first", "woven1%d" % c)
-                gather_far_words1(far_words1_first[:], 0)
-        far_words1_rest = tile([P, S - CHUNK], U32, "far_words1_rest", "woven1%d" % (CHUNKS - 1))
-        far_words1 = [far_words1_first[:]] + [far_words1_rest[:, c * CHUNK : (c + 1) * CHUNK] for c in range(CHUNKS - 1)]
-        for c in range(1, CHUNKS):
+            gather_pair(0, c)
+        for c in range(CHUNKS):
+            gather_pair(1, c)
+        far_words1_first = heirs.tile([P, last * CHUNK], U32, name="far_words1_first", offset=8192, align_bytes=64)
+        far_words1 = [far_words1_first[:, c * CHUNK : (c + 1) * CHUNK] for c in range(last)]
+        for c in range(last):
             gather_far_words1(far_words1[c], c)
 
-        def experts(c, name, tag, words, scale):
-            bank = ps.tile([P, CHUNK], F32, name=name, tag=tag)
-            for j in range(PER_CHUNK):
+        woven_early = heirs.tile([P, PACK * last * CHUNK], BF16, name="woven_early", offset=0, align_bytes=64)
+        for c in range(last):
+            move_on_gpsimd(
+                woven_early[:, c * PACK * CHUNK : (c + 1) * PACK * CHUNK].rearrange("p (j u e) -> p j u e", u=2, e=2),
+                halves[1][c][:].bitcast(BF16).rearrange("p (u j e) -> p j u e", u=2, e=2),
+            )
+        early_words = tile([P, last * CHUNK], U32, "early_words")
+        early_scale = tile([P, last * CHUNK], U8, "early_scale")
+        nc.vector.quantize_mx(early_words[:].bitcast(FP8X4), early_scale[:], woven_early[:])
+
+        late_words = tile([P, S + CHUNK], U32, "late_words", "halves1%d" % (last - 1))
+        late_scale = tile([P, S + CHUNK], U8, "late_scale")
+        def quantize_late(woven, at):
+            end = at + woven.shape[1] // PACK
+            nc.vector.quantize_mx(late_words[:, at:end].bitcast(FP8X4), late_scale[:, at:end], woven[:])
+
+        quantize_late(weave(nc.vector.tensor_copy, I32, 0, 0, CHUNK), 0)
+        quantize_late(weave(nc.scalar.copy, U32, 0, CHUNK, last * CHUNK), CHUNK)
+        quantize_late(weave(nc.scalar.copy, U32, 1, last * CHUNK, S), S)
+        for a, b in OWN[last:]:
+            quantize_late(weave(nc.scalar.copy, U32, 0, a, b), a)
+        far_words1_last = tile([P, CHUNK], U32, "far_words1_last", "halves0%d" % last)
+        far_words1.append(far_words1_last[:])
+        gather_far_words1(far_words1[last], last)
+
+        def experts(a, b, bank, words, scale):
+            for j in range((b - a) // C):
                 slots = slice(j * C, (j + 1) * C)
                 for s in range(PASSES):
-                    i = (c * PER_CHUNK + j) * PASSES + s
+                    i = (a // C + j) * PASSES + s
                     nc.tensor.matmul_mx(
                         bank[:, slots],
                         lhsT=w_code[:, i * 2 * N : (i + 1) * 2 * N].bitcast(FP4X4),
@@ -182,26 +206,32 @@ def tile_moe_loc_lin_relu_kernel(
                         start=(s == 0),
                         stop=(s == PASSES - 1),
                     )
+
+        def far_experts(c):
+            a, b = c * CHUNK, (c + 1) * CHUNK
+            bank = ps.tile([P, CHUNK], F32, name="far%d" % c)
+            experts(a, b, bank, [far_words0[:, a:b], far_words1[c]], [far_scale0[:, a:b], far_scale1[:, a:b]])
             return bank
 
+        far_banks = [far_experts(c) for c in range(last)]
         y = tile([P, S], F32, "y")
-        for c in range(CHUNKS):
-            words = [own_words[s][c] for s in range(PASSES)]
-            scale = [own_scale[s][c] for s in range(PASSES)]
-            bank = experts(c, "own%d" % c, "own%d" % c, words, scale)
-            nc.scalar.activation(y[:, c * CHUNK : (c + 1) * CHUNK], bank[:], ACT.Relu)
+        for a, b in OWN:
+            if a < last * CHUNK:
+                words1, scale1 = early_words[:, a:b], early_scale[:, a:b]
+            else:
+                words1, scale1 = late_words[:, a + CHUNK : b + CHUNK], late_scale[:, a + CHUNK : b + CHUNK]
+            bank = ps.tile([P, b - a], F32, name="own%d" % a)
+            experts(a, b, bank, [late_words[:, a:b], words1], [late_scale[:, a:b], scale1])
+            nc.scalar.activation(y[:, a:b], bank[:], ACT.Relu)
 
-        for c in range(CHUNKS):
-            cols = slice(c * CHUNK, (c + 1) * CHUNK)
-            tag = "own%d" % (CHUNKS - 1) if c == 0 else "far%d" % c
-            bank = experts(
-                c, "far%d" % c, tag, [far_words0[:, cols], far_words1[c]], [far_scale0[:, cols], far_scale1[:, cols]]
-            )
-            z = tile([P, CHUNK], F32, "z%d" % c)
+        far_banks.append(far_experts(last))
+        for c, bank in enumerate(far_banks):
+            a, b = c * CHUNK, (c + 1) * CHUNK
+            z = tile([P, CHUNK], F32, "z%d" % c, ("halves1%d" % (last - 1), "late_scale", None)[c])
             nc.scalar.activation(z[:], bank[:], ACT.Relu)
-            nc.sync.dma_start(out[:, T + c * CHUNK : T + (c + 1) * CHUNK], z[:])
+            nc.sync.dma_start(out[:, T + a : T + b], z[:])
 
-        first = tile([P, T], F32, "first", "far_table1")
+        first = tile([P, T], F32, "first")
         nc.vector.tensor_tensor(first[:], y[:].indirect(pos_list[0][:]), gates[0][:], ALU.mult)
         second = [tile([P, b - a], F32, "second%d" % a) for a, b in COMBINE]
 

@@ -24,6 +24,7 @@ QUADRANTS = 4
 CHUNK = 512
 CHUNKS = S // CHUNK
 OWN = ((0, 512), (512, 1024), (1024, 1280), (1280, S))
+GPSIMD_LATE = 256
 LIST_ROWS = 16
 HALVES = ((0, S // 2), (S // 2, S))
 COMBINE = ((0, 384), (384, 640), (640, T))
@@ -50,9 +51,10 @@ def tile_moe_loc_lin_relu_kernel(
 
         far_scale_table = tile([P, Q], U8, "far_scale_table")
         w_scale = tile([P, E * PASSES * N], U8, "w_scale")
-        far_scale1 = tile([P, S], U8, "far_scale1")
-        nc.vector.memset(far_scale_table[:].bitcast(I32), 0)
-        for zeroed in (w_scale, far_scale1):
+        far_scale = tile([P, PASSES * S], U8, "far_scale")
+        for a, b in ((32, 64), (64, P)):
+            nc.vector.memset(far_scale_table[a:b, :].bitcast(I32), 0)
+        for zeroed in (w_scale, far_scale):
             nc.gpsimd.memset(zeroed[:].bitcast(I32), 0)
 
         xo_k = xo.rearrange("(s p u e) t -> s u p e t", s=PASSES, u=2, e=2)
@@ -67,10 +69,7 @@ def tile_moe_loc_lin_relu_kernel(
             nc.sync.dma_start(raw_single[d][:], xo_k[1, d // 2, :, d % 2, :])
 
         nc.sync.dma_start(far_list[:], offs2)
-        for q in range(QUADRANTS):
-            nc.sync.dma_start(
-                far_scale_table[32 * q : 32 * q + 8, :].bitcast(I32), x_scales.bitcast(I32)[:, 4 * q : 4 * q + 4, :]
-            )
+        nc.sync.dma_start(far_scale_table[: PASSES * 16, :].bitcast(I32), x_scales.bitcast(I32).rearrange("s b t -> (s b) t"))
         load_single(0)
         nc.sync.dma_start(own_list[:], offs)
         load_far_words(0)
@@ -90,16 +89,18 @@ def tile_moe_loc_lin_relu_kernel(
         def chunk_entries(lst, c):
             return entries(lst, c * CHUNK, (c + 1) * CHUNK)
 
-        far_scale0 = tile([P, S], U8, "far_scale0")
+        far_scale_rows = tile([P, S], U8, "far_scale_rows")
         for a, b in HALVES:
-            nc.vector.tensor_copy(far_scale0[:, a:b], far_scale_table[:].indirect(entries(far_list, a, b)))
+            nc.vector.tensor_copy(far_scale_rows[:, a:b], far_scale_table[:].indirect(entries(far_list, a, b)))
         far_words0 = tile([P, S], U32, "far_words0")
         for a, b in HALVES:
             nc.vector.tensor_copy(far_words0[:, a:b], far_table[0][:].bitcast(U32).indirect(entries(far_list, a, b)))
-        for q in range(QUADRANTS):
-            nc.sync.dma_start(
-                far_scale1[32 * q : 32 * q + 4, :].bitcast(I32), far_scale0[32 * q + 4 : 32 * q + 8, :].bitcast(I32)
-            )
+        for s in range(PASSES):
+            for q in range(QUADRANTS):
+                row = 16 * s + 4 * q
+                nc.sync.dma_start(
+                    far_scale[32 * q : 32 * q + 4, s * S : (s + 1) * S].bitcast(I32), far_scale_rows[row : row + 4, :].bitcast(I32)
+                )
 
         singles = [tile([P, T], BF16, "single%d" % d) for d in range(PACK)]
         pairs = [tile([P, 2 * T], BF16, "pair%d" % u) for u in range(2)]
@@ -146,12 +147,15 @@ def tile_moe_loc_lin_relu_kernel(
         def gather_far_words1(dst, c):
             nc.vector.tensor_copy(dst, far_table[1][:].bitcast(U32).indirect(chunk_entries(far_list, c)))
 
-        def weave(copy, dtype, s, a, b):
-            woven = tile([P, PACK * (b - a)], BF16, "woven%d_%d" % (s, a))
+        def weave_on_scalar(dst, s, a, b):
             at = a % CHUNK
-            src = halves[s][a // CHUNK][:].bitcast(dtype).rearrange("p (u j) -> p j u", u=2)[:, at : at + b - a, :]
-            copy(woven[:].bitcast(dtype).rearrange("p (j u) -> p j u", u=2), src)
-            return woven
+            src = halves[s][a // CHUNK][:].rearrange("p (u j) -> p j u", u=2)[:, at : at + b - a, :]
+            nc.scalar.copy(dst.bitcast(U32).rearrange("p (j u) -> p j u", u=2), src)
+
+        def weave_on_gpsimd(dst, s, a, b):
+            at = a % CHUNK
+            src = halves[s][a // CHUNK][:].rearrange("p (u j) -> p j u", u=2)[:, at : at + b - a, :]
+            nc.gpsimd.tensor_copy(dst.bitcast(U32).rearrange("p (j u) -> p j u", u=2), src)
 
         for d in range(PACK):
             for c in range(last):
@@ -169,10 +173,7 @@ def tile_moe_loc_lin_relu_kernel(
 
         woven_early = heirs.tile([P, PACK * last * CHUNK], BF16, name="woven_early", offset=0, align_bytes=64)
         for c in range(last):
-            move_on_gpsimd(
-                woven_early[:, c * PACK * CHUNK : (c + 1) * PACK * CHUNK].rearrange("p (j u e) -> p j u e", u=2, e=2),
-                halves[1][c][:].bitcast(BF16).rearrange("p (u j e) -> p j u e", u=2, e=2),
-            )
+            weave_on_gpsimd(woven_early[:, c * PACK * CHUNK : (c + 1) * PACK * CHUNK], 1, c * CHUNK, (c + 1) * CHUNK)
         early_words = tile([P, last * CHUNK], U32, "early_words")
         early_scale = tile([P, last * CHUNK], U8, "early_scale")
         nc.vector.quantize_mx(early_words[:].bitcast(FP8X4), early_scale[:], woven_early[:])
@@ -183,11 +184,13 @@ def tile_moe_loc_lin_relu_kernel(
             end = at + woven.shape[1] // PACK
             nc.vector.quantize_mx(late_words[:, at:end].bitcast(FP8X4), late_scale[:, at:end], woven[:])
 
-        quantize_late(weave(nc.vector.tensor_copy, I32, 0, 0, CHUNK), 0)
-        quantize_late(weave(nc.scalar.copy, U32, 0, CHUNK, last * CHUNK), CHUNK)
-        quantize_late(weave(nc.scalar.copy, U32, 1, last * CHUNK, S), S)
-        for a, b in OWN[last:]:
-            quantize_late(weave(nc.scalar.copy, U32, 0, a, b), a)
+        for s, a, b in [(0, 0, CHUNK), (0, CHUNK, last * CHUNK), (1, last * CHUNK, S)] + [(0, a, b) for a, b in OWN[last:]]:
+            woven = tile([P, PACK * (b - a)], BF16, "woven%d_%d" % (s, a))
+            cut = GPSIMD_LATE if a == 0 else 0
+            if cut:
+                weave_on_gpsimd(woven[:, : PACK * cut], s, a, a + cut)
+            weave_on_scalar(woven[:, PACK * cut :], s, a + cut, b)
+            quantize_late(woven, a + s * CHUNK)
         far_words1_last = tile([P, CHUNK], U32, "far_words1_last", "halves0%d" % last)
         far_words1.append(far_words1_last[:])
         gather_far_words1(far_words1[last], last)
@@ -210,7 +213,7 @@ def tile_moe_loc_lin_relu_kernel(
         def far_experts(c):
             a, b = c * CHUNK, (c + 1) * CHUNK
             bank = ps.tile([P, CHUNK], F32, name="far%d" % c)
-            experts(a, b, bank, [far_words0[:, a:b], far_words1[c]], [far_scale0[:, a:b], far_scale1[:, a:b]])
+            experts(a, b, bank, [far_words0[:, a:b], far_words1[c]], [far_scale[:, a:b], far_scale[:, S + a : S + b]])
             return bank
 
         far_banks = [far_experts(c) for c in range(last)]

@@ -24,7 +24,8 @@ QUADRANTS = 4
 CHUNK = 512
 CHUNKS = S // CHUNK
 OWN = ((0, 512), (512, 1024), (1024, 1280), (1280, S))
-GPSIMD_LATE = 256
+ON_GPSIMD = ((0, 0), (0, 1), (1, 0))
+HALVES_BYTES = 2 * 4 * CHUNK
 LIST_ROWS = 16
 HALVES = ((0, S // 2), (S // 2, S))
 COMBINE = ((0, 384), (384, 640), (640, T))
@@ -41,6 +42,9 @@ def tile_moe_loc_lin_relu_kernel(
 
         def tile(shape, dtype, name, after=None):
             return sb.tile(shape, dtype, name=name, tag=after or name, align_bytes=64)
+
+        def placed(shape, dtype, name, offset):
+            return heirs.tile(shape, dtype, name=name, offset=offset, align_bytes=64)
 
         def entries(lst, a, b):
             return lst[:, a // LIST_ROWS : b // LIST_ROWS]
@@ -59,8 +63,9 @@ def tile_moe_loc_lin_relu_kernel(
 
         xo_k = xo.rearrange("(s p u e) t -> s u p e t", s=PASSES, u=2, e=2)
         far_table = [tile([P, Q], I32, "far_table%d" % s) for s in range(PASSES)]
-        raw_pair = [tile([P, 2, T], F32, "raw_pair0"), heirs.tile([P, 2, T], F32, name="raw_pair1", offset=6144, align_bytes=64)]
-        raw_single = [tile([P, T], F32, "raw_single%d" % d) for d in range(PACK)]
+        raw_pair = [tile([P, 2, T], F32, "raw_pair%d" % u) for u in range(2)]
+        raw_single = [tile([P, T], F32, "raw_single%d" % d) for d in range(PACK - 1)]
+        raw_single.append(placed([P, T], F32, "raw_single3", 3 * HALVES_BYTES))
 
         def load_far_words(s):
             nc.sync.dma_start(far_table[s][:], x_words[s].rearrange("p t d -> p (t d)").bitcast(I32))
@@ -73,18 +78,16 @@ def tile_moe_loc_lin_relu_kernel(
         load_single(0)
         nc.sync.dma_start(own_list[:], offs)
         load_far_words(0)
-        load_single(1)
-        load_single(2)
-        nc.sync.dma_start(raw_pair[0][:], xo_k[0, 0])
-        load_single(3)
-        nc.sync.dma_start(raw_pair[1][:], xo_k[0, 1])
+        for u in range(2):
+            load_single(u + 1)
+            nc.sync.dma_start(raw_pair[u][:], xo_k[0, u])
+        load_single(PACK - 1)
         load_far_words(1)
-        w_scale_rows = w_scales.bitcast(I32).rearrange("e s (q r) n -> r q (e s) n", r=4)
-        w_scale_words = w_scale[:].bitcast(I32).rearrange("p (g n) -> p g n", n=N // 4)
-        for r in range(4):
-            nc.sync.dma_start(w_scale_words[r:P:32, :, :], w_scale_rows[r])
-        nc.sync.dma_start(pos_list[0][:], pos1)
-        nc.sync.dma_start(pos_list[1][:], pos2)
+        w_scale_rows = tile([P, E * PASSES * N], U8, "w_scale_rows")
+        nc.sync.dma_start(
+            w_scale_rows[:16, :].bitcast(I32).rearrange("b (g n) -> b g n", n=N // 4),
+            w_scales.bitcast(I32).rearrange("e s b n -> b (e s) n"),
+        )
 
         def chunk_entries(lst, c):
             return entries(lst, c * CHUNK, (c + 1) * CHUNK)
@@ -102,6 +105,14 @@ def tile_moe_loc_lin_relu_kernel(
                     far_scale[32 * q : 32 * q + 4, s * S : (s + 1) * S].bitcast(I32), far_scale_rows[row : row + 4, :].bitcast(I32)
                 )
 
+        for q in range(QUADRANTS):
+            nc.sync.dma_start(w_scale[32 * q : 32 * q + 4, :].bitcast(I32), w_scale_rows[4 * q : 4 * q + 4, :].bitcast(I32))
+        w_code = tile([P, E * PASSES * 2 * N], U8, "w_code")
+        nc.sync.dma_start(
+            w_code[:].bitcast(I32).rearrange("p (g n) -> p g n", n=N // 2),
+            w_words.bitcast(I32).rearrange("e s p n -> p (e s) n"),
+        )
+
         singles = [tile([P, T], BF16, "single%d" % d) for d in range(PACK)]
         pairs = [tile([P, 2 * T], BF16, "pair%d" % u) for u in range(2)]
 
@@ -113,26 +124,23 @@ def tile_moe_loc_lin_relu_kernel(
 
         nc.scalar.activation(singles[0][:, : T // 2], raw_single[0][:, : T // 2], ACT.Copy)
         move_on_gpsimd(singles[0][:, T // 2 :], raw_single[0][:, T // 2 :])
-        move_on_gpsimd(singles[1][:], raw_single[1][:])
-        move_on_gpsimd(singles[2][:], raw_single[2][:])
-        round_pair(0)
-        move_on_gpsimd(singles[3][:], raw_single[3][:])
-        round_pair(1)
+        for u in range(2):
+            move_on_gpsimd(singles[u + 1][:], raw_single[u + 1][:])
+            round_pair(u)
+        move_on_gpsimd(singles[PACK - 1][:], raw_single[PACK - 1][:])
 
-        w_code = tile([P, E * PASSES * 2 * N], U8, "w_code", "raw_pair0")
-        nc.sync.dma_start(
-            w_code[:].bitcast(I32).rearrange("p (g n) -> p g n", n=N // 2),
-            w_words.bitcast(I32).rearrange("e s p n -> p (e s) n"),
-        )
+        nc.sync.dma_start(pos_list[0][:], pos1)
+        nc.sync.dma_start(pos_list[1][:], pos2)
         gates = [tile([P, T], F32, "gate%d" % r, "raw_single%d" % (r + 1)) for r in range(2)]
         for r in range(2):
             nc.sync.dma_start(gates[r][:], gate[r])
 
         last = CHUNKS - 1
-        halves = [
-            [tile([P, 2 * CHUNK], U32, "halves0%d" % c) for c in range(CHUNKS)],
-            [tile([P, 2 * CHUNK], U32, "halves1%d" % c, "raw_single3" if c == last else None) for c in range(CHUNKS)],
-        ]
+        halves = [[None] * CHUNKS for s in range(PASSES)]
+        for i, (s, c) in enumerate(ON_GPSIMD):
+            halves[s][c] = placed([P, 2 * CHUNK], U32, "halves%d%d" % (s, c), i * HALVES_BYTES)
+        for s, c in ((1, 1), (1, last), (0, last)):
+            halves[s][c] = tile([P, 2 * CHUNK], U32, "halves%d%d" % (s, c))
 
         def gather_single(d, c):
             at = (d // 2) * CHUNK
@@ -158,39 +166,37 @@ def tile_moe_loc_lin_relu_kernel(
             nc.gpsimd.tensor_copy(dst.bitcast(U32).rearrange("p (j u) -> p j u", u=2), src)
 
         for d in range(PACK):
-            for c in range(last):
+            for c in range(CHUNKS):
                 gather_single(d, c)
-        for d in range(PACK):
-            gather_single(d, last)
         for c in range(CHUNKS):
             gather_pair(0, c)
         for c in range(CHUNKS):
             gather_pair(1, c)
-        far_words1_first = heirs.tile([P, last * CHUNK], U32, name="far_words1_first", offset=8192, align_bytes=64)
+        far_words1_first = tile([P, last * CHUNK], U32, "far_words1_first", "raw_pair1")
         far_words1 = [far_words1_first[:, c * CHUNK : (c + 1) * CHUNK] for c in range(last)]
         for c in range(last):
             gather_far_words1(far_words1[c], c)
 
-        woven_early = heirs.tile([P, PACK * last * CHUNK], BF16, name="woven_early", offset=0, align_bytes=64)
-        for c in range(last):
-            weave_on_gpsimd(woven_early[:, c * PACK * CHUNK : (c + 1) * PACK * CHUNK], 1, c * CHUNK, (c + 1) * CHUNK)
-        early_words = tile([P, last * CHUNK], U32, "early_words")
-        early_scale = tile([P, last * CHUNK], U8, "early_scale")
-        nc.vector.quantize_mx(early_words[:].bitcast(FP8X4), early_scale[:], woven_early[:])
+        woven_early = tile([P, PACK * len(ON_GPSIMD) * CHUNK], BF16, "woven_early")
+        for i, (s, c) in enumerate(ON_GPSIMD):
+            weave_on_gpsimd(woven_early[:, i * PACK * CHUNK : (i + 1) * PACK * CHUNK], s, c * CHUNK, (c + 1) * CHUNK)
+        own_words = placed([P, PASSES * S], U32, "own_words", 0)
+        own_scale = tile([P, PASSES * S], U8, "own_scale")
 
-        late_words = tile([P, S + CHUNK], U32, "late_words", "halves1%d" % (last - 1))
-        late_scale = tile([P, S + CHUNK], U8, "late_scale")
-        def quantize_late(woven, at):
-            end = at + woven.shape[1] // PACK
-            nc.vector.quantize_mx(late_words[:, at:end].bitcast(FP8X4), late_scale[:, at:end], woven[:])
+        def quantize(woven, s, a, b):
+            cols = slice(s * S + a, s * S + b)
+            nc.vector.quantize_mx(own_words[:, cols].bitcast(FP8X4), own_scale[:, cols], woven)
 
-        for s, a, b in [(0, 0, CHUNK), (0, CHUNK, last * CHUNK), (1, last * CHUNK, S)] + [(0, a, b) for a, b in OWN[last:]]:
-            woven = tile([P, PACK * (b - a)], BF16, "woven%d_%d" % (s, a))
-            cut = GPSIMD_LATE if a == 0 else 0
-            if cut:
-                weave_on_gpsimd(woven[:, : PACK * cut], s, a, a + cut)
-            weave_on_scalar(woven[:, PACK * cut :], s, a + cut, b)
-            quantize_late(woven, a + s * CHUNK)
+        quantize(woven_early[:, : PACK * last * CHUNK], 0, 0, last * CHUNK)
+        quantize(woven_early[:, PACK * last * CHUNK :], 1, 0, CHUNK)
+        for c in range(1, CHUNKS):
+            woven = tile([P, PACK * CHUNK], BF16, "woven1%d" % c)
+            weave_on_scalar(woven[:], 1, c * CHUNK, (c + 1) * CHUNK)
+            quantize(woven[:], 1, c * CHUNK, (c + 1) * CHUNK)
+        for i, (a, b) in enumerate(OWN[last:]):
+            woven = placed([P, PACK * (b - a)], BF16, "woven0_%d" % a, 3 * HALVES_BYTES + i * 2 * PACK * (b - a))
+            weave_on_scalar(woven[:], 0, a, b)
+            quantize(woven[:], 0, a, b)
         far_words1_last = tile([P, CHUNK], U32, "far_words1_last", "halves0%d" % last)
         far_words1.append(far_words1_last[:])
         gather_far_words1(far_words1[last], last)
@@ -219,18 +225,15 @@ def tile_moe_loc_lin_relu_kernel(
         far_banks = [far_experts(c) for c in range(last)]
         y = tile([P, S], F32, "y")
         for a, b in OWN:
-            if a < last * CHUNK:
-                words1, scale1 = early_words[:, a:b], early_scale[:, a:b]
-            else:
-                words1, scale1 = late_words[:, a + CHUNK : b + CHUNK], late_scale[:, a + CHUNK : b + CHUNK]
             bank = ps.tile([P, b - a], F32, name="own%d" % a)
-            experts(a, b, bank, [late_words[:, a:b], words1], [late_scale[:, a:b], scale1])
+            cols = [slice(s * S + a, s * S + b) for s in range(PASSES)]
+            experts(a, b, bank, [own_words[:, col] for col in cols], [own_scale[:, col] for col in cols])
             nc.scalar.activation(y[:, a:b], bank[:], ACT.Relu)
 
         far_banks.append(far_experts(last))
         for c, bank in enumerate(far_banks):
             a, b = c * CHUNK, (c + 1) * CHUNK
-            z = tile([P, CHUNK], F32, "z%d" % c, ("halves1%d" % (last - 1), "late_scale", None)[c])
+            z = placed([P, CHUNK], F32, "z%d" % c, 4 * c * CHUNK)
             nc.scalar.activation(z[:], bank[:], ACT.Relu)
             nc.sync.dma_start(out[:, T + a : T + b], z[:])
 

@@ -23,9 +23,15 @@ PACK = 4
 QUADRANTS = 4
 CHUNK = 512
 CHUNKS = S // CHUNK
-OWN = ((0, 512), (512, 1024), (1024, 1280), (1280, S))
+OWN = ((0, 512), (512, 1024), (1024, 1280), (1280, 1408), (1408, S))
+FAR_CUT = 896
+FAR_EARLY = ((0, CHUNK), (CHUNK, FAR_CUT))
+FAR_LATE = ((FAR_CUT, 1280), (1280, S))
 ON_GPSIMD = ((0, 0), (0, 1), (1, 0))
 HALVES_BYTES = 2 * 4 * CHUNK
+WIDE = 2048
+SHIFTED = 128
+GPSIMD_MORE = 256
 LIST_ROWS = 16
 HALVES = ((0, S // 2), (S // 2, S))
 COMBINE = ((0, 384), (384, 640), (640, T))
@@ -58,14 +64,18 @@ def tile_moe_loc_lin_relu_kernel(
         far_scale = tile([P, PASSES * S], U8, "far_scale")
         for a, b in ((32, 64), (64, P)):
             nc.vector.memset(far_scale_table[a:b, :].bitcast(I32), 0)
-        for zeroed in (w_scale, far_scale):
-            nc.gpsimd.memset(zeroed[:].bitcast(I32), 0)
+        singles = tile([P, (PACK - 1) * T + WIDE], BF16, "singles")
+        for zeroed in (singles[:, PACK * T :], w_scale[:], far_scale[:]):
+            nc.gpsimd.memset(zeroed.bitcast(I32), 0)
 
         xo_k = xo.rearrange("(s p u e) t -> s u p e t", s=PASSES, u=2, e=2)
         far_table = [tile([P, Q], I32, "far_table%d" % s) for s in range(PASSES)]
-        raw_pair = [tile([P, 2, T], F32, "raw_pair%d" % u) for u in range(2)]
-        raw_single = [tile([P, T], F32, "raw_single%d" % d) for d in range(PACK - 1)]
-        raw_single.append(placed([P, T], F32, "raw_single3", 3 * HALVES_BYTES))
+        raw_pair = [[tile([P, 2, T // 2], F32, "raw_pair%d%d" % (u, h)) for h in range(2)] for u in range(2)]
+        raw_pair[1][1] = placed([P, 2, T // 2], F32, "raw_pair11", 5 * HALVES_BYTES - 2 * T)
+        raw_first = [tile([P, T // 2], F32, "raw_first%d" % h) for h in range(2)]
+        token_halves = (slice(0, T // 2), slice(T // 2, T))
+        raw_single = [None] + [tile([P, T], F32, "raw_single%d" % d) for d in range(1, PACK - 1)]
+        raw_single.append(placed([P, T], F32, "raw_single3", 4 * HALVES_BYTES - 4 * T))
 
         def load_far_words(s):
             nc.sync.dma_start(far_table[s][:], x_words[s].rearrange("p t d -> p (t d)").bitcast(I32))
@@ -74,13 +84,15 @@ def tile_moe_loc_lin_relu_kernel(
             nc.sync.dma_start(raw_single[d][:], xo_k[1, d // 2, :, d % 2, :])
 
         nc.sync.dma_start(far_list[:], offs2)
-        nc.sync.dma_start(far_scale_table[: PASSES * 16, :].bitcast(I32), x_scales.bitcast(I32).rearrange("s b t -> (s b) t"))
-        load_single(0)
+        nc.scalar.dma_start(far_scale_table[: PASSES * 16, :].bitcast(I32), x_scales.bitcast(I32).rearrange("s b t -> (s b) t"))
+        for h in range(2):
+            nc.sync.dma_start(raw_first[h][:], xo_k[1, 0, :, 0, token_halves[h]])
         nc.sync.dma_start(own_list[:], offs)
         load_far_words(0)
         for u in range(2):
             load_single(u + 1)
-            nc.sync.dma_start(raw_pair[u][:], xo_k[0, u])
+            for h in range(2):
+                nc.sync.dma_start(raw_pair[u][h][:], xo_k[0, u, :, :, token_halves[h]])
         load_single(PACK - 1)
         load_far_words(1)
         w_scale_rows = tile([P, E * PASSES * N], U8, "w_scale_rows")
@@ -113,21 +125,29 @@ def tile_moe_loc_lin_relu_kernel(
             w_words.bitcast(I32).rearrange("e s p n -> p (e s) n"),
         )
 
-        singles = [tile([P, T], BF16, "single%d" % d) for d in range(PACK)]
+        def single(d, width=T):
+            at = (PACK - 1 - d) * T
+            return singles[:, at : at + width]
+
         pairs = [tile([P, 2 * T], BF16, "pair%d" % u) for u in range(2)]
 
         def move_on_gpsimd(dst, src):
             nc.gpsimd.tensor_scalar(dst, src, 1.0, 0.0, ALU.mult, ALU.add)
 
         def round_pair(u):
-            move_on_gpsimd(pairs[u][:].rearrange("p (t e) -> p t e", e=2), raw_pair[u][:].rearrange("p e t -> p t e"))
+            for h in range(2):
+                dst = pairs[u][:].rearrange("p (t e) -> p t e", e=2)[:, token_halves[h], :]
+                move_on_gpsimd(dst, raw_pair[u][h][:].rearrange("p e t -> p t e"))
 
-        nc.scalar.activation(singles[0][:, : T // 2], raw_single[0][:, : T // 2], ACT.Copy)
-        move_on_gpsimd(singles[0][:, T // 2 :], raw_single[0][:, T // 2 :])
+        nc.scalar.activation(single(0)[:, : T // 2], raw_first[0][:], ACT.Copy)
+        move_on_gpsimd(single(0)[:, T // 2 :], raw_first[1][:])
         for u in range(2):
-            move_on_gpsimd(singles[u + 1][:], raw_single[u + 1][:])
+            move_on_gpsimd(single(u + 1), raw_single[u + 1][:])
             round_pair(u)
-        move_on_gpsimd(singles[PACK - 1][:], raw_single[PACK - 1][:])
+        move_on_gpsimd(single(PACK - 1), raw_single[PACK - 1][:])
+        spare = [tile([P, T], BF16, "spare%d" % e) for e in range(2)]
+        for e in range(2):
+            nc.gpsimd.tensor_copy(spare[e][:], pairs[1][:].rearrange("p (t e) -> p e t", e=2)[:, e, :])
 
         nc.sync.dma_start(pos_list[0][:], pos1)
         nc.sync.dma_start(pos_list[1][:], pos2)
@@ -136,46 +156,54 @@ def tile_moe_loc_lin_relu_kernel(
             nc.sync.dma_start(gates[r][:], gate[r])
 
         last = CHUNKS - 1
-        halves = [[None] * CHUNKS for s in range(PASSES)]
-        for i, (s, c) in enumerate(ON_GPSIMD):
-            halves[s][c] = placed([P, 2 * CHUNK], U32, "halves%d%d" % (s, c), i * HALVES_BYTES)
-        for s, c in ((1, 1), (1, last), (0, last)):
-            halves[s][c] = tile([P, 2 * CHUNK], U32, "halves%d%d" % (s, c))
+        halves0 = [placed([P, 2 * CHUNK], U32, "halves0%d" % c, c * HALVES_BYTES) for c in range(last)]
+        halves0.append(placed([P, 2 * CHUNK], U32, "halves0%d" % last, 4 * HALVES_BYTES))
+        halves1 = tile([P, 2 * S], U32, "halves1")
 
-        def gather_single(d, c):
-            at = (d // 2) * CHUNK
-            dst = halves[1][c][:, at : at + CHUNK].bitcast(BF16).rearrange("p (j e) -> p e j", e=2)
-            nc.scalar.activation(dst[:, d % 2, :], singles[d][:].indirect(chunk_entries(own_list, c)), ACT.Copy)
+        def halves(s, a, b):
+            if s == 1:
+                return halves1[:].rearrange("p (u j) -> p j u", u=2)[:, a:b, :]
+            return halves0[a // CHUNK][:].rearrange("p (u j) -> p j u", u=2)[:, a % CHUNK : a % CHUNK + b - a, :]
+
+        def gather_single(d, a, b, width):
+            at = (d // 2) * S
+            dst = halves1[:, at + a : at + b].bitcast(BF16).rearrange("p (j e) -> p e j", e=2)
+            nc.scalar.activation(dst[:, d % 2, :], single(d, width).indirect(entries(own_list, a, b)), ACT.Copy)
 
         def gather_pair(u, c):
+            width = CHUNK - SHIFTED if (u, c) == (1, last) else CHUNK
             nc.vector.tensor_copy(
-                halves[0][c][:, u * CHUNK : (u + 1) * CHUNK], pairs[u][:].bitcast(U32).indirect(chunk_entries(own_list, c))
+                halves0[c][:, u * CHUNK : u * CHUNK + width],
+                pairs[u][:].bitcast(U32).indirect(entries(own_list, c * CHUNK, c * CHUNK + width)),
             )
 
-        def gather_far_words1(dst, c):
-            nc.vector.tensor_copy(dst, far_table[1][:].bitcast(U32).indirect(chunk_entries(far_list, c)))
+        def gather_spare(e):
+            dst = halves0[last][:, 2 * CHUNK - SHIFTED :].bitcast(BF16).rearrange("p (j e) -> p e j", e=2)
+            nc.scalar.activation(dst[:, e, :], spare[e][:].indirect(entries(own_list, S - SHIFTED, S)), ACT.Copy)
+
+        def gather_far_words1(dst, a, b):
+            nc.vector.tensor_copy(dst, far_table[1][:].bitcast(U32).indirect(entries(far_list, a, b)))
 
         def weave_on_scalar(dst, s, a, b):
-            at = a % CHUNK
-            src = halves[s][a // CHUNK][:].rearrange("p (u j) -> p j u", u=2)[:, at : at + b - a, :]
-            nc.scalar.copy(dst.bitcast(U32).rearrange("p (j u) -> p j u", u=2), src)
+            nc.scalar.copy(dst.bitcast(U32).rearrange("p (j u) -> p j u", u=2), halves(s, a, b))
 
         def weave_on_gpsimd(dst, s, a, b):
-            at = a % CHUNK
-            src = halves[s][a // CHUNK][:].rearrange("p (u j) -> p j u", u=2)[:, at : at + b - a, :]
-            nc.gpsimd.tensor_copy(dst.bitcast(U32).rearrange("p (j u) -> p j u", u=2), src)
+            nc.gpsimd.tensor_copy(dst.bitcast(U32).rearrange("p (j u) -> p j u", u=2), halves(s, a, b))
 
-        for d in range(PACK):
-            for c in range(CHUNKS):
-                gather_single(d, c)
+        for d in range(PACK - 1):
+            gather_single(d, 0, S, WIDE)
         for c in range(CHUNKS):
-            gather_pair(0, c)
-        for c in range(CHUNKS):
-            gather_pair(1, c)
-        far_words1_first = tile([P, last * CHUNK], U32, "far_words1_first", "raw_pair1")
-        far_words1 = [far_words1_first[:, c * CHUNK : (c + 1) * CHUNK] for c in range(last)]
-        for c in range(last):
-            gather_far_words1(far_words1[c], c)
+            gather_single(PACK - 1, c * CHUNK, (c + 1) * CHUNK, T)
+        for e in range(2):
+            gather_spare(e)
+        for u in range(2):
+            for c in range(last):
+                gather_pair(u, c)
+        for u in range(2):
+            gather_pair(u, last)
+        far_words1_early = placed([P, FAR_CUT], U32, "far_words1_early", 5 * HALVES_BYTES)
+        for a, b in FAR_EARLY:
+            gather_far_words1(far_words1_early[:, a:b], a, b)
 
         woven_early = tile([P, PACK * len(ON_GPSIMD) * CHUNK], BF16, "woven_early")
         for i, (s, c) in enumerate(ON_GPSIMD):
@@ -191,15 +219,17 @@ def tile_moe_loc_lin_relu_kernel(
         quantize(woven_early[:, PACK * last * CHUNK :], 1, 0, CHUNK)
         for c in range(1, CHUNKS):
             woven = tile([P, PACK * CHUNK], BF16, "woven1%d" % c)
-            weave_on_scalar(woven[:], 1, c * CHUNK, (c + 1) * CHUNK)
+            cut = GPSIMD_MORE if c == 1 else 0
+            if cut:
+                weave_on_gpsimd(woven[:, : PACK * cut], 1, c * CHUNK, c * CHUNK + cut)
+            weave_on_scalar(woven[:, PACK * cut :], 1, c * CHUNK + cut, (c + 1) * CHUNK)
             quantize(woven[:], 1, c * CHUNK, (c + 1) * CHUNK)
-        for i, (a, b) in enumerate(OWN[last:]):
-            woven = placed([P, PACK * (b - a)], BF16, "woven0_%d" % a, 3 * HALVES_BYTES + i * 2 * PACK * (b - a))
+        for a, b in OWN[last:]:
+            woven = placed([P, PACK * (b - a)], BF16, "woven0_%d" % a, 3 * HALVES_BYTES + 2 * PACK * (a - last * CHUNK))
             weave_on_scalar(woven[:], 0, a, b)
             quantize(woven[:], 0, a, b)
-        far_words1_last = tile([P, CHUNK], U32, "far_words1_last", "halves0%d" % last)
-        far_words1.append(far_words1_last[:])
-        gather_far_words1(far_words1[last], last)
+        far_words1_late = placed([P, S - FAR_CUT], U32, "far_words1_late", 4 * HALVES_BYTES)
+        gather_far_words1(far_words1_late[:], FAR_CUT, S)
 
         def experts(a, b, bank, words, scale):
             for j in range((b - a) // C):
@@ -216,13 +246,12 @@ def tile_moe_loc_lin_relu_kernel(
                         stop=(s == PASSES - 1),
                     )
 
-        def far_experts(c):
-            a, b = c * CHUNK, (c + 1) * CHUNK
-            bank = ps.tile([P, CHUNK], F32, name="far%d" % c)
-            experts(a, b, bank, [far_words0[:, a:b], far_words1[c]], [far_scale[:, a:b], far_scale[:, S + a : S + b]])
+        def far_experts(a, b, words1, tag):
+            bank = ps.tile([P, b - a], F32, name="far%d" % a, tag=tag)
+            experts(a, b, bank, [far_words0[:, a:b], words1], [far_scale[:, a:b], far_scale[:, S + a : S + b]])
             return bank
 
-        far_banks = [far_experts(c) for c in range(last)]
+        far_banks = [far_experts(a, b, far_words1_early[:, a:b], "far%d" % a) for a, b in FAR_EARLY]
         y = tile([P, S], F32, "y")
         for a, b in OWN:
             bank = ps.tile([P, b - a], F32, name="own%d" % a)
@@ -230,10 +259,10 @@ def tile_moe_loc_lin_relu_kernel(
             experts(a, b, bank, [own_words[:, col] for col in cols], [own_scale[:, col] for col in cols])
             nc.scalar.activation(y[:, a:b], bank[:], ACT.Relu)
 
-        far_banks.append(far_experts(last))
-        for c, bank in enumerate(far_banks):
-            a, b = c * CHUNK, (c + 1) * CHUNK
-            z = placed([P, CHUNK], F32, "z%d" % c, 4 * c * CHUNK)
+        for i, (a, b) in enumerate(FAR_LATE):
+            far_banks.append(far_experts(a, b, far_words1_late[:, a - FAR_CUT : b - FAR_CUT], "own%d" % OWN[i][0]))
+        for (a, b), bank in zip(FAR_EARLY + FAR_LATE, far_banks):
+            z = placed([P, b - a], F32, "z%d" % a, 4 * a)
             nc.scalar.activation(z[:], bank[:], ACT.Relu)
             nc.sync.dma_start(out[:, T + a : T + b], z[:])
 

@@ -21,19 +21,14 @@ P = 128
 PASSES = K // 512
 PACK = 4
 QUADRANTS = 4
-CHUNK = 512
-CHUNKS = S // CHUNK
-OWN = ((0, 512), (512, 1024), (1024, 1280), (1280, 1408), (1408, S))
-FAR_CUT = 896
-FAR_EARLY = ((0, CHUNK), (CHUNK, FAR_CUT))
-FAR_LATE = ((FAR_CUT, 1280), (1280, S))
-ON_GPSIMD = ((0, 0), (0, 1), (1, 0))
-HALVES_BYTES = 2 * 4 * CHUNK
-WIDE = 2048
-SHIFTED = 128
-GPSIMD_MORE = 256
 LIST_ROWS = 16
-HALVES = ((0, S // 2), (S // 2, S))
+WIDE = 2048
+CHUNK = 512
+OWN = ((0, 512), (512, 1024), (1024, 1280), (1280, S))
+FAR_CUT = 640
+FAR_SPARE = 256
+WOVEN_BYTES = PASSES * PACK * CHUNK * 2
+TOKEN_PARTS = (((0, 512), (512, T)), ((0, T // 2), (T // 2, T)))
 COMBINE = ((0, 384), (384, 640), (640, T))
 
 
@@ -59,64 +54,68 @@ def tile_moe_loc_lin_relu_kernel(
         far_list = tile([P, S // LIST_ROWS], U16, "far_list")
         pos_list = [tile([P, T // LIST_ROWS], U16, "pos_list%d" % r) for r in range(2)]
 
-        far_scale_table = tile([P, Q], U8, "far_scale_table")
+        far_scale_table = tile([P, WIDE], U8, "far_scale_table")
         w_scale = tile([P, E * PASSES * N], U8, "w_scale")
         far_scale = tile([P, PASSES * S], U8, "far_scale")
         for a, b in ((32, 64), (64, P)):
             nc.vector.memset(far_scale_table[a:b, :].bitcast(I32), 0)
-        singles = tile([P, (PACK - 1) * T + WIDE], BF16, "singles")
-        for zeroed in (singles[:, PACK * T :], w_scale[:], far_scale[:]):
+        nc.vector.memset(far_scale_table[:32, Q:].bitcast(I32), 0)
+        singles = tile([P, 2 * T + WIDE], BF16, "singles")
+        for zeroed in (singles[:, 3 * T :], w_scale[:], far_scale[:]):
             nc.gpsimd.memset(zeroed.bitcast(I32), 0)
 
         xo_k = xo.rearrange("(s p u e) t -> s u p e t", s=PASSES, u=2, e=2)
-        far_table = [tile([P, Q], I32, "far_table%d" % s) for s in range(PASSES)]
-        raw_pair = [[tile([P, 2, T // 2], F32, "raw_pair%d%d" % (u, h)) for h in range(2)] for u in range(2)]
-        raw_pair[1][1] = placed([P, 2, T // 2], F32, "raw_pair11", 5 * HALVES_BYTES - 2 * T)
-        raw_first = [tile([P, T // 2], F32, "raw_first%d" % h) for h in range(2)]
-        token_halves = (slice(0, T // 2), slice(T // 2, T))
-        raw_single = [None] + [tile([P, T], F32, "raw_single%d" % d) for d in range(1, PACK - 1)]
-        raw_single.append(placed([P, T], F32, "raw_single3", 4 * HALVES_BYTES - 4 * T))
+        pair_table = tile([P, 4 * T], F32, "pair_table")
+        raw_pair1 = tile([P, 2 * T], F32, "raw_pair1")
 
-        def load_far_words(s):
-            nc.sync.dma_start(far_table[s][:], x_words[s].rearrange("p t d -> p (t d)").bitcast(I32))
+        def raw_pair(u, a, b):
+            rows = pair_table[:, 2 * T :] if u == 0 else raw_pair1[:]
+            return rows[:, 2 * a : 2 * b].rearrange("p (e t) -> p e t", e=2)
+
+        def pair_words(u, width):
+            at = (1 - u) * T
+            return pair_table[:, at : at + width]
+
+        raw_first = [tile([P, T // 2], F32, "raw_first%d" % h) for h in range(2)]
+        raw_single = [None] + [tile([P, T], F32, "raw_single%d" % d) for d in range(1, PACK)]
+        far_table = tile([P, PASSES * Q + FAR_SPARE], I32, "far_table")
+        nc.vector.memset(far_table[:, PASSES * Q :], 0)
 
         def load_single(d):
             nc.sync.dma_start(raw_single[d][:], xo_k[1, d // 2, :, d % 2, :])
 
+        def load_pair(u, h):
+            a, b = TOKEN_PARTS[u][h]
+            nc.sync.dma_start(raw_pair(u, a, b), xo_k[0, u, :, :, a:b])
+
         nc.sync.dma_start(far_list[:], offs2)
-        nc.scalar.dma_start(far_scale_table[: PASSES * 16, :].bitcast(I32), x_scales.bitcast(I32).rearrange("s b t -> (s b) t"))
+        nc.scalar.dma_start(far_scale_table[: PASSES * 16, :Q].bitcast(I32), x_scales.bitcast(I32).rearrange("s b t -> (s b) t"))
+        load_pair(0, 0)
         for h in range(2):
-            nc.sync.dma_start(raw_first[h][:], xo_k[1, 0, :, 0, token_halves[h]])
+            nc.sync.dma_start(raw_first[h][:], xo_k[1, 0, :, 0, h * T // 2 : (h + 1) * T // 2])
         nc.sync.dma_start(own_list[:], offs)
-        load_far_words(0)
-        for u in range(2):
-            load_single(u + 1)
-            for h in range(2):
-                nc.sync.dma_start(raw_pair[u][h][:], xo_k[0, u, :, :, token_halves[h]])
-        load_single(PACK - 1)
-        load_far_words(1)
+        load_pair(0, 1)
+        load_single(1)
+        load_pair(1, 0)
+        load_pair(1, 1)
+        load_single(2)
+        load_single(3)
         w_scale_rows = tile([P, E * PASSES * N], U8, "w_scale_rows")
         nc.sync.dma_start(
             w_scale_rows[:16, :].bitcast(I32).rearrange("b (g n) -> b g n", n=N // 4),
             w_scales.bitcast(I32).rearrange("e s b n -> b (e s) n"),
         )
-
-        def chunk_entries(lst, c):
-            return entries(lst, c * CHUNK, (c + 1) * CHUNK)
+        for s in range(PASSES):
+            nc.sync.dma_start(far_table[:, s * Q : (s + 1) * Q], x_words[s].rearrange("p t d -> p (t d)").bitcast(I32))
 
         far_scale_rows = tile([P, S], U8, "far_scale_rows")
-        for a, b in HALVES:
-            nc.vector.tensor_copy(far_scale_rows[:, a:b], far_scale_table[:].indirect(entries(far_list, a, b)))
-        far_words0 = tile([P, S], U32, "far_words0")
-        for a, b in HALVES:
-            nc.vector.tensor_copy(far_words0[:, a:b], far_table[0][:].bitcast(U32).indirect(entries(far_list, a, b)))
+        nc.vector.tensor_copy(far_scale_rows[:], far_scale_table[:].indirect(far_list[:]))
         for s in range(PASSES):
             for q in range(QUADRANTS):
                 row = 16 * s + 4 * q
                 nc.sync.dma_start(
                     far_scale[32 * q : 32 * q + 4, s * S : (s + 1) * S].bitcast(I32), far_scale_rows[row : row + 4, :].bitcast(I32)
                 )
-
         for q in range(QUADRANTS):
             nc.sync.dma_start(w_scale[32 * q : 32 * q + 4, :].bitcast(I32), w_scale_rows[4 * q : 4 * q + 4, :].bitcast(I32))
         w_code = tile([P, E * PASSES * 2 * N], U8, "w_code")
@@ -124,111 +123,93 @@ def tile_moe_loc_lin_relu_kernel(
             w_code[:].bitcast(I32).rearrange("p (g n) -> p g n", n=N // 2),
             w_words.bitcast(I32).rearrange("e s p n -> p (e s) n"),
         )
+        nc.sync.dma_start(pos_list[0][:], pos1)
+        nc.sync.dma_start(pos_list[1][:], pos2)
+
+        last_single = tile([P, T], BF16, "last_single")
 
         def single(d, width=T):
-            at = (PACK - 1 - d) * T
+            if d == PACK - 1:
+                return last_single[:]
+            at = (PACK - 2 - d) * T
             return singles[:, at : at + width]
 
-        pairs = [tile([P, 2 * T], BF16, "pair%d" % u) for u in range(2)]
-
-        def move_on_gpsimd(dst, src):
+        def round_on_gpsimd(dst, src):
             nc.gpsimd.tensor_scalar(dst, src, 1.0, 0.0, ALU.mult, ALU.add)
 
         def round_pair(u):
-            for h in range(2):
-                dst = pairs[u][:].rearrange("p (t e) -> p t e", e=2)[:, token_halves[h], :]
-                move_on_gpsimd(dst, raw_pair[u][h][:].rearrange("p e t -> p t e"))
+            for a, b in TOKEN_PARTS[u]:
+                dst = pair_words(u, T)[:, a:b].bitcast(BF16).rearrange("p (t e) -> p t e", e=2)
+                round_on_gpsimd(dst, raw_pair(u, a, b).rearrange("p e t -> p t e"))
 
-        nc.scalar.activation(single(0)[:, : T // 2], raw_first[0][:], ACT.Copy)
-        move_on_gpsimd(single(0)[:, T // 2 :], raw_first[1][:])
-        for u in range(2):
-            move_on_gpsimd(single(u + 1), raw_single[u + 1][:])
-            round_pair(u)
-        move_on_gpsimd(single(PACK - 1), raw_single[PACK - 1][:])
-        spare = [tile([P, T], BF16, "spare%d" % e) for e in range(2)]
-        for e in range(2):
-            nc.gpsimd.tensor_copy(spare[e][:], pairs[1][:].rearrange("p (t e) -> p e t", e=2)[:, e, :])
+        for h in range(2):
+            nc.scalar.activation(single(0)[:, h * T // 2 : (h + 1) * T // 2], raw_first[h][:], ACT.Copy)
+        round_pair(0)
+        round_on_gpsimd(single(1), raw_single[1][:])
+        round_pair(1)
+        round_on_gpsimd(single(2), raw_single[2][:])
+        round_on_gpsimd(single(3), raw_single[3][:])
 
-        nc.sync.dma_start(pos_list[0][:], pos1)
-        nc.sync.dma_start(pos_list[1][:], pos2)
         gates = [tile([P, T], F32, "gate%d" % r, "raw_single%d" % (r + 1)) for r in range(2)]
         for r in range(2):
             nc.sync.dma_start(gates[r][:], gate[r])
 
-        last = CHUNKS - 1
-        halves0 = [placed([P, 2 * CHUNK], U32, "halves0%d" % c, c * HALVES_BYTES) for c in range(last)]
-        halves0.append(placed([P, 2 * CHUNK], U32, "halves0%d" % last, 4 * HALVES_BYTES))
-        halves1 = tile([P, 2 * S], U32, "halves1")
-
-        def halves(s, a, b):
-            if s == 1:
-                return halves1[:].rearrange("p (u j) -> p j u", u=2)[:, a:b, :]
-            return halves0[a // CHUNK][:].rearrange("p (u j) -> p j u", u=2)[:, a % CHUNK : a % CHUNK + b - a, :]
+        halves = [tile([P, 2 * S], U32, "halves%d" % s) for s in range(PASSES)]
 
         def gather_single(d, a, b, width):
             at = (d // 2) * S
-            dst = halves1[:, at + a : at + b].bitcast(BF16).rearrange("p (j e) -> p e j", e=2)
+            dst = halves[1][:, at + a : at + b].bitcast(BF16).rearrange("p (j e) -> p e j", e=2)
             nc.scalar.activation(dst[:, d % 2, :], single(d, width).indirect(entries(own_list, a, b)), ACT.Copy)
 
-        def gather_pair(u, c):
-            width = CHUNK - SHIFTED if (u, c) == (1, last) else CHUNK
-            nc.vector.tensor_copy(
-                halves0[c][:, u * CHUNK : u * CHUNK + width],
-                pairs[u][:].bitcast(U32).indirect(entries(own_list, c * CHUNK, c * CHUNK + width)),
-            )
+        def gather_pair(u, a, b, width):
+            nc.vector.tensor_copy(halves[0][:, u * S + a : u * S + b], pair_words(u, width).bitcast(U32).indirect(entries(own_list, a, b)))
 
-        def gather_spare(e):
-            dst = halves0[last][:, 2 * CHUNK - SHIFTED :].bitcast(BF16).rearrange("p (j e) -> p e j", e=2)
-            nc.scalar.activation(dst[:, e, :], spare[e][:].indirect(entries(own_list, S - SHIFTED, S)), ACT.Copy)
+        gather_single(0, 0, S, WIDE)
+        gather_single(1, 0, 2 * CHUNK, 2 * T)
+        gather_single(2, 0, 2 * CHUNK, 2 * T)
+        gather_single(3, 0, CHUNK, T)
+        gather_single(3, CHUNK, 2 * CHUNK, T)
+        for d in range(1, PACK):
+            gather_single(d, 2 * CHUNK, S, T)
+        gather_pair(0, 0, S, WIDE)
+        for c in range(S // CHUNK):
+            gather_pair(1, c * CHUNK, (c + 1) * CHUNK, T)
+
+        far_words0 = tile([P, S], U32, "far_words0")
+        nc.vector.tensor_copy(far_words0[:], far_table[:, :WIDE].bitcast(U32).indirect(far_list[:]))
 
         def gather_far_words1(dst, a, b):
-            nc.vector.tensor_copy(dst, far_table[1][:].bitcast(U32).indirect(entries(far_list, a, b)))
+            nc.vector.tensor_copy(dst, far_table[:, Q:].bitcast(U32).indirect(entries(far_list, a, b)))
 
-        def weave_on_scalar(dst, s, a, b):
-            nc.scalar.copy(dst.bitcast(U32).rearrange("p (j u) -> p j u", u=2), halves(s, a, b))
+        far_words1_early = tile([P, FAR_CUT], U32, "far_words1_early")
+        gather_far_words1(far_words1_early[:], 0, FAR_CUT)
 
-        def weave_on_gpsimd(dst, s, a, b):
-            nc.gpsimd.tensor_copy(dst.bitcast(U32).rearrange("p (j u) -> p j u", u=2), halves(s, a, b))
+        woven = [placed([P, PASSES * PACK * CHUNK], BF16, "woven%d" % c, c * WOVEN_BYTES) for c in range(S // CHUNK)]
 
-        for d in range(PACK - 1):
-            gather_single(d, 0, S, WIDE)
-        for c in range(CHUNKS):
-            gather_single(PACK - 1, c * CHUNK, (c + 1) * CHUNK, T)
-        for e in range(2):
-            gather_spare(e)
-        for u in range(2):
-            for c in range(last):
-                gather_pair(u, c)
-        for u in range(2):
-            gather_pair(u, last)
-        far_words1_early = placed([P, FAR_CUT], U32, "far_words1_early", 5 * HALVES_BYTES)
-        for a, b in FAR_EARLY:
-            gather_far_words1(far_words1_early[:, a:b], a, b)
+        def woven_range(i):
+            a, b = OWN[i]
+            at = PASSES * PACK * (a % CHUNK)
+            return woven[a // CHUNK][:, at : at + PASSES * PACK * (b - a)]
 
-        woven_early = tile([P, PACK * len(ON_GPSIMD) * CHUNK], BF16, "woven_early")
-        for i, (s, c) in enumerate(ON_GPSIMD):
-            weave_on_gpsimd(woven_early[:, i * PACK * CHUNK : (i + 1) * PACK * CHUNK], s, c * CHUNK, (c + 1) * CHUNK)
-        own_words = placed([P, PASSES * S], U32, "own_words", 0)
-        own_scale = tile([P, PASSES * S], U8, "own_scale")
+        def slot_words(s, a, b):
+            return halves[s][:].rearrange("p (u j) -> p j u", u=2)[:, a:b, :]
 
-        def quantize(woven, s, a, b):
-            cols = slice(s * S + a, s * S + b)
-            nc.vector.quantize_mx(own_words[:, cols].bitcast(FP8X4), own_scale[:, cols], woven)
+        def weave(copy, s, i):
+            a, b = OWN[i]
+            dst = woven_range(i)[:, s * PACK * (b - a) : (s + 1) * PACK * (b - a)].bitcast(U32).rearrange("p (j u) -> p j u", u=2)
+            copy(dst, slot_words(s, a, b))
 
-        quantize(woven_early[:, : PACK * last * CHUNK], 0, 0, last * CHUNK)
-        quantize(woven_early[:, PACK * last * CHUNK :], 1, 0, CHUNK)
-        for c in range(1, CHUNKS):
-            woven = tile([P, PACK * CHUNK], BF16, "woven1%d" % c)
-            cut = GPSIMD_MORE if c == 1 else 0
-            if cut:
-                weave_on_gpsimd(woven[:, : PACK * cut], 1, c * CHUNK, c * CHUNK + cut)
-            weave_on_scalar(woven[:, PACK * cut :], 1, c * CHUNK + cut, (c + 1) * CHUNK)
-            quantize(woven[:], 1, c * CHUNK, (c + 1) * CHUNK)
-        for a, b in OWN[last:]:
-            woven = placed([P, PACK * (b - a)], BF16, "woven0_%d" % a, 3 * HALVES_BYTES + 2 * PACK * (a - last * CHUNK))
-            weave_on_scalar(woven[:], 0, a, b)
-            quantize(woven[:], 0, a, b)
-        far_words1_late = placed([P, S - FAR_CUT], U32, "far_words1_late", 4 * HALVES_BYTES)
+        for s, i in ((0, 0), (0, 1), (0, 2), (1, 0), (1, 1)):
+            weave(nc.gpsimd.tensor_copy, s, i)
+        for s, i in ((1, 2), (0, 3), (1, 3)):
+            weave(nc.scalar.copy, s, i)
+
+        own_words = [tile([P, PASSES * (b - a)], U32, "own_words%d" % a) for a, b in OWN[:2]]
+        own_words += [placed([P, PASSES * (b - a)], U32, "own_words%d" % a, WOVEN_BYTES + 4 * PASSES * (a % CHUNK)) for a, b in OWN[2:]]
+        own_scale = [tile([P, PASSES * (b - a)], U8, "own_scale%d" % a) for a, b in OWN]
+        for i in range(len(OWN)):
+            nc.vector.quantize_mx(own_words[i][:].bitcast(FP8X4), own_scale[i][:], woven_range(i))
+        far_words1_late = placed([P, S - FAR_CUT], U32, "far_words1_late", 2 * WOVEN_BYTES)
         gather_far_words1(far_words1_late[:], FAR_CUT, S)
 
         def experts(a, b, bank, words, scale):
@@ -246,25 +227,23 @@ def tile_moe_loc_lin_relu_kernel(
                         stop=(s == PASSES - 1),
                     )
 
-        def far_experts(a, b, words1, tag):
-            bank = ps.tile([P, b - a], F32, name="far%d" % a, tag=tag)
-            experts(a, b, bank, [far_words0[:, a:b], words1], [far_scale[:, a:b], far_scale[:, S + a : S + b]])
-            return bank
+        def far_experts(a, b, words1, z):
+            for lo, hi in ((a, a + CHUNK), (a + CHUNK, b)):
+                bank = ps.tile([P, hi - lo], F32, name="far%d" % lo)
+                experts(lo, hi, bank, [far_words0[:, lo:hi], words1[:, lo - a : hi - a]], [far_scale[:, lo:hi], far_scale[:, S + lo : S + hi]])
+                nc.scalar.activation(z[:, lo - a : hi - a], bank[:], ACT.Relu)
+                nc.sync.dma_start(out[:, T + lo : T + hi], z[:, lo - a : hi - a])
 
-        far_banks = [far_experts(a, b, far_words1_early[:, a:b], "far%d" % a) for a, b in FAR_EARLY]
+        z_early = tile([P, FAR_CUT], F32, "z_early", "halves1")
+        far_experts(0, FAR_CUT, far_words1_early, z_early)
         y = tile([P, S], F32, "y")
-        for a, b in OWN:
+        for i, (a, b) in enumerate(OWN):
             bank = ps.tile([P, b - a], F32, name="own%d" % a)
-            cols = [slice(s * S + a, s * S + b) for s in range(PASSES)]
-            experts(a, b, bank, [own_words[:, col] for col in cols], [own_scale[:, col] for col in cols])
+            cols = [slice(s * (b - a), (s + 1) * (b - a)) for s in range(PASSES)]
+            experts(a, b, bank, [own_words[i][:, col] for col in cols], [own_scale[i][:, col] for col in cols])
             nc.scalar.activation(y[:, a:b], bank[:], ACT.Relu)
-
-        for i, (a, b) in enumerate(FAR_LATE):
-            far_banks.append(far_experts(a, b, far_words1_late[:, a - FAR_CUT : b - FAR_CUT], "own%d" % OWN[i][0]))
-        for (a, b), bank in zip(FAR_EARLY + FAR_LATE, far_banks):
-            z = placed([P, b - a], F32, "z%d" % a, 4 * a)
-            nc.scalar.activation(z[:], bank[:], ACT.Relu)
-            nc.sync.dma_start(out[:, T + a : T + b], z[:])
+        z_late = tile([P, S - FAR_CUT], F32, "z_late")
+        far_experts(FAR_CUT, S, far_words1_late, z_late)
 
         first = tile([P, T], F32, "first")
         nc.vector.tensor_tensor(first[:], y[:].indirect(pos_list[0][:]), gates[0][:], ALU.mult)

@@ -25,10 +25,11 @@ LIST_ROWS = 16
 WIDE = 2048
 CHUNK = 512
 OWN = ((0, 512), (512, 1024), (1024, 1280), (1280, S))
-FAR_CUT = 640
-FAR_SPARE = 256
+FAR_CUT = 768
+SCALE_ROWS = P - PASSES * 16
+GPSIMD_MORE = 256
 WOVEN_BYTES = PASSES * PACK * CHUNK * 2
-TOKEN_PARTS = (((0, 512), (512, T)), ((0, T // 2), (T // 2, T)))
+TOKEN_PARTS = (((0, T // 2), (T // 2, T)), ((0, T),))
 COMBINE = ((0, 384), (384, 640), (640, T))
 
 
@@ -57,11 +58,10 @@ def tile_moe_loc_lin_relu_kernel(
         far_scale_table = tile([P, WIDE], U8, "far_scale_table")
         w_scale = tile([P, E * PASSES * N], U8, "w_scale")
         far_scale = tile([P, PASSES * S], U8, "far_scale")
-        for a, b in ((32, 64), (64, P)):
-            nc.vector.memset(far_scale_table[a:b, :].bitcast(I32), 0)
-        nc.vector.memset(far_scale_table[:32, Q:].bitcast(I32), 0)
-        singles = tile([P, 2 * T + WIDE], BF16, "singles")
-        for zeroed in (singles[:, 3 * T :], w_scale[:], far_scale[:]):
+        nc.vector.memset(far_scale_table[:SCALE_ROWS, :].bitcast(I32), 0)
+        nc.vector.memset(far_scale_table[SCALE_ROWS:, Q:].bitcast(I32), 0)
+        singles = tile([P, T + WIDE], BF16, "singles")
+        for zeroed in (singles[:, 2 * T :], far_scale[:], w_scale[:]):
             nc.gpsimd.memset(zeroed.bitcast(I32), 0)
 
         xo_k = xo.rearrange("(s p u e) t -> s u p e t", s=PASSES, u=2, e=2)
@@ -77,61 +77,63 @@ def tile_moe_loc_lin_relu_kernel(
             return pair_table[:, at : at + width]
 
         raw_first = [tile([P, T // 2], F32, "raw_first%d" % h) for h in range(2)]
-        raw_single = [None] + [tile([P, T], F32, "raw_single%d" % d) for d in range(1, PACK)]
-        far_table = tile([P, PASSES * Q + FAR_SPARE], I32, "far_table")
-        nc.vector.memset(far_table[:, PASSES * Q :], 0)
+        raw_second = tile([P, T], F32, "raw_second")
+        raw_last = tile([P, 2 * T], F32, "raw_last")
+        far_table = [tile([P, Q], I32, "far_table%d" % s) for s in range(PASSES)]
 
-        def load_single(d):
-            nc.sync.dma_start(raw_single[d][:], xo_k[1, d // 2, :, d % 2, :])
+        def load_pair(u):
+            for a, b in TOKEN_PARTS[u]:
+                nc.sync.dma_start(raw_pair(u, a, b), xo_k[0, u, :, :, a:b])
 
-        def load_pair(u, h):
-            a, b = TOKEN_PARTS[u][h]
-            nc.sync.dma_start(raw_pair(u, a, b), xo_k[0, u, :, :, a:b])
+        def load_far_words(s):
+            nc.sync.dma_start(far_table[s][:], x_words[s].rearrange("p t d -> p (t d)").bitcast(I32))
 
         nc.sync.dma_start(far_list[:], offs2)
-        nc.scalar.dma_start(far_scale_table[: PASSES * 16, :Q].bitcast(I32), x_scales.bitcast(I32).rearrange("s b t -> (s b) t"))
-        load_pair(0, 0)
+        nc.scalar.dma_start(far_scale_table[SCALE_ROWS:, :Q].bitcast(I32), x_scales.bitcast(I32).rearrange("s b t -> (s b) t"))
         for h in range(2):
             nc.sync.dma_start(raw_first[h][:], xo_k[1, 0, :, 0, h * T // 2 : (h + 1) * T // 2])
         nc.sync.dma_start(own_list[:], offs)
-        load_pair(0, 1)
-        load_single(1)
-        load_pair(1, 0)
-        load_pair(1, 1)
-        load_single(2)
-        load_single(3)
+        load_far_words(0)
+        nc.sync.dma_start(raw_second[:], xo_k[1, 0, :, 1, :])
+        load_pair(0)
+        nc.sync.dma_start(raw_last[:].rearrange("p (e t) -> p e t", e=2), xo_k[1, 1])
+        load_pair(1)
+        load_far_words(1)
         w_scale_rows = tile([P, E * PASSES * N], U8, "w_scale_rows")
         nc.sync.dma_start(
             w_scale_rows[:16, :].bitcast(I32).rearrange("b (g n) -> b g n", n=N // 4),
             w_scales.bitcast(I32).rearrange("e s b n -> b (e s) n"),
         )
-        for s in range(PASSES):
-            nc.sync.dma_start(far_table[:, s * Q : (s + 1) * Q], x_words[s].rearrange("p t d -> p (t d)").bitcast(I32))
 
         far_scale_rows = tile([P, S], U8, "far_scale_rows")
         nc.vector.tensor_copy(far_scale_rows[:], far_scale_table[:].indirect(far_list[:]))
         for s in range(PASSES):
             for q in range(QUADRANTS):
-                row = 16 * s + 4 * q
+                row = SCALE_ROWS + 16 * s + 4 * q
                 nc.sync.dma_start(
                     far_scale[32 * q : 32 * q + 4, s * S : (s + 1) * S].bitcast(I32), far_scale_rows[row : row + 4, :].bitcast(I32)
                 )
+        w_code = [tile([P, E * N * 2], U8, "w_code%d" % h) for h in range(2)]
+
+        def load_w_code(h):
+            nc.sync.dma_start(
+                w_code[h][:].bitcast(I32).rearrange("p (g n) -> p g n", n=N // 2),
+                w_words[h * E // 2 : (h + 1) * E // 2].bitcast(I32).rearrange("e s p n -> p (e s) n"),
+            )
+
+        load_w_code(0)
         for q in range(QUADRANTS):
             nc.sync.dma_start(w_scale[32 * q : 32 * q + 4, :].bitcast(I32), w_scale_rows[4 * q : 4 * q + 4, :].bitcast(I32))
-        w_code = tile([P, E * PASSES * 2 * N], U8, "w_code")
-        nc.sync.dma_start(
-            w_code[:].bitcast(I32).rearrange("p (g n) -> p g n", n=N // 2),
-            w_words.bitcast(I32).rearrange("e s p n -> p (e s) n"),
-        )
+        load_w_code(1)
         nc.sync.dma_start(pos_list[0][:], pos1)
         nc.sync.dma_start(pos_list[1][:], pos2)
 
-        last_single = tile([P, T], BF16, "last_single")
+        last_singles = tile([P, 2 * T], BF16, "last_singles")
 
         def single(d, width=T):
-            if d == PACK - 1:
-                return last_single[:]
-            at = (PACK - 2 - d) * T
+            if d >= 2:
+                return last_singles[:, (d - 2) * T : (d - 1) * T]
+            at = (1 - d) * T
             return singles[:, at : at + width]
 
         def round_on_gpsimd(dst, src):
@@ -142,15 +144,14 @@ def tile_moe_loc_lin_relu_kernel(
                 dst = pair_words(u, T)[:, a:b].bitcast(BF16).rearrange("p (t e) -> p t e", e=2)
                 round_on_gpsimd(dst, raw_pair(u, a, b).rearrange("p e t -> p t e"))
 
-        for h in range(2):
-            nc.scalar.activation(single(0)[:, h * T // 2 : (h + 1) * T // 2], raw_first[h][:], ACT.Copy)
+        nc.scalar.activation(single(0)[:, : T // 2], raw_first[0][:], ACT.Copy)
+        round_on_gpsimd(single(0)[:, T // 2 :], raw_first[1][:])
+        round_on_gpsimd(single(1), raw_second[:])
         round_pair(0)
-        round_on_gpsimd(single(1), raw_single[1][:])
+        round_on_gpsimd(last_singles[:], raw_last[:])
         round_pair(1)
-        round_on_gpsimd(single(2), raw_single[2][:])
-        round_on_gpsimd(single(3), raw_single[3][:])
 
-        gates = [tile([P, T], F32, "gate%d" % r, "raw_single%d" % (r + 1)) for r in range(2)]
+        gates = [tile([P, T], F32, "gate%d" % r, ("raw_last", "raw_second")[r]) for r in range(2)]
         for r in range(2):
             nc.sync.dma_start(gates[r][:], gate[r])
 
@@ -165,24 +166,23 @@ def tile_moe_loc_lin_relu_kernel(
             nc.vector.tensor_copy(halves[0][:, u * S + a : u * S + b], pair_words(u, width).bitcast(U32).indirect(entries(own_list, a, b)))
 
         gather_single(0, 0, S, WIDE)
-        gather_single(1, 0, 2 * CHUNK, 2 * T)
-        gather_single(2, 0, 2 * CHUNK, 2 * T)
-        gather_single(3, 0, CHUNK, T)
-        gather_single(3, CHUNK, 2 * CHUNK, T)
-        for d in range(1, PACK):
-            gather_single(d, 2 * CHUNK, S, T)
-        gather_pair(0, 0, S, WIDE)
+        gather_single(1, 0, S, WIDE)
         for c in range(S // CHUNK):
-            gather_pair(1, c * CHUNK, (c + 1) * CHUNK, T)
+            for d in (2, 3):
+                gather_single(d, c * CHUNK, (c + 1) * CHUNK, T)
+
+        def gather_far_words(dst, s, a, b):
+            nc.vector.tensor_copy(dst, far_table[s][:].bitcast(U32).indirect(entries(far_list, a, b)))
 
         far_words0 = tile([P, S], U32, "far_words0")
-        nc.vector.tensor_copy(far_words0[:], far_table[:, :WIDE].bitcast(U32).indirect(far_list[:]))
-
-        def gather_far_words1(dst, a, b):
-            nc.vector.tensor_copy(dst, far_table[:, Q:].bitcast(U32).indirect(entries(far_list, a, b)))
-
-        far_words1_early = tile([P, FAR_CUT], U32, "far_words1_early")
-        gather_far_words1(far_words1_early[:], 0, FAR_CUT)
+        for a in (0, S // 2):
+            gather_far_words(far_words0[:, a : a + S // 2], 0, a, a + S // 2)
+        gather_pair(0, 0, S, WIDE)
+        gather_pair(1, 0, CHUNK, T)
+        gather_pair(1, CHUNK, 2 * CHUNK, T)
+        far_words1_early = tile([P, FAR_CUT], U32, "far_words1_early", "raw_pair1")
+        gather_far_words(far_words1_early[:], 1, 0, FAR_CUT)
+        gather_pair(1, 2 * CHUNK, S, T)
 
         woven = [placed([P, PASSES * PACK * CHUNK], BF16, "woven%d" % c, c * WOVEN_BYTES) for c in range(S // CHUNK)]
 
@@ -194,15 +194,19 @@ def tile_moe_loc_lin_relu_kernel(
         def slot_words(s, a, b):
             return halves[s][:].rearrange("p (u j) -> p j u", u=2)[:, a:b, :]
 
-        def weave(copy, s, i):
+        def weave(copy, s, i, lo=0, hi=None):
             a, b = OWN[i]
-            dst = woven_range(i)[:, s * PACK * (b - a) : (s + 1) * PACK * (b - a)].bitcast(U32).rearrange("p (j u) -> p j u", u=2)
-            copy(dst, slot_words(s, a, b))
+            hi = hi or b - a
+            dst = woven_range(i)[:, PACK * (s * (b - a) + lo) : PACK * (s * (b - a) + hi)].bitcast(U32).rearrange("p (j u) -> p j u", u=2)
+            copy(dst, slot_words(s, a + lo, a + hi))
 
-        for s, i in ((0, 0), (0, 1), (0, 2), (1, 0), (1, 1)):
+        for s, i in ((1, 0), (0, 0), (0, 1)):
             weave(nc.gpsimd.tensor_copy, s, i)
-        for s, i in ((1, 2), (0, 3), (1, 3)):
-            weave(nc.scalar.copy, s, i)
+        weave(nc.gpsimd.tensor_copy, 1, 1, 0, GPSIMD_MORE)
+        weave(nc.scalar.copy, 1, 1, GPSIMD_MORE)
+        for i in (2, 3):
+            for s in (1, 0):
+                weave(nc.scalar.copy, s, i)
 
         own_words = [tile([P, PASSES * (b - a)], U32, "own_words%d" % a) for a, b in OWN[:2]]
         own_words += [placed([P, PASSES * (b - a)], U32, "own_words%d" % a, WOVEN_BYTES + 4 * PASSES * (a % CHUNK)) for a, b in OWN[2:]]
@@ -210,7 +214,7 @@ def tile_moe_loc_lin_relu_kernel(
         for i in range(len(OWN)):
             nc.vector.quantize_mx(own_words[i][:].bitcast(FP8X4), own_scale[i][:], woven_range(i))
         far_words1_late = placed([P, S - FAR_CUT], U32, "far_words1_late", 2 * WOVEN_BYTES)
-        gather_far_words1(far_words1_late[:], FAR_CUT, S)
+        gather_far_words(far_words1_late[:], 1, FAR_CUT, S)
 
         def experts(a, b, bank, words, scale):
             for j in range((b - a) // C):
@@ -219,7 +223,7 @@ def tile_moe_loc_lin_relu_kernel(
                     i = (a // C + j) * PASSES + s
                     nc.tensor.matmul_mx(
                         bank[:, slots],
-                        lhsT=w_code[:, i * 2 * N : (i + 1) * 2 * N].bitcast(FP4X4),
+                        lhsT=w_code[i // E][:, i % E * 2 * N : (i % E + 1) * 2 * N].bitcast(FP4X4),
                         lhsT_scale=w_scale[:, i * N : (i + 1) * N],
                         rhs=words[s][:, slots].bitcast(FP8X4),
                         rhs_scale=scale[s][:, slots],
@@ -227,23 +231,26 @@ def tile_moe_loc_lin_relu_kernel(
                         stop=(s == PASSES - 1),
                     )
 
-        def far_experts(a, b, words1, z):
+        def far_experts(a, b, words1):
+            banks = []
             for lo, hi in ((a, a + CHUNK), (a + CHUNK, b)):
                 bank = ps.tile([P, hi - lo], F32, name="far%d" % lo)
                 experts(lo, hi, bank, [far_words0[:, lo:hi], words1[:, lo - a : hi - a]], [far_scale[:, lo:hi], far_scale[:, S + lo : S + hi]])
-                nc.scalar.activation(z[:, lo - a : hi - a], bank[:], ACT.Relu)
-                nc.sync.dma_start(out[:, T + lo : T + hi], z[:, lo - a : hi - a])
+                banks.append((lo, hi, bank))
+            return banks
 
-        z_early = tile([P, FAR_CUT], F32, "z_early", "halves1")
-        far_experts(0, FAR_CUT, far_words1_early, z_early)
+        far_banks = far_experts(0, FAR_CUT, far_words1_early)
         y = tile([P, S], F32, "y")
         for i, (a, b) in enumerate(OWN):
             bank = ps.tile([P, b - a], F32, name="own%d" % a)
             cols = [slice(s * (b - a), (s + 1) * (b - a)) for s in range(PASSES)]
             experts(a, b, bank, [own_words[i][:, col] for col in cols], [own_scale[i][:, col] for col in cols])
             nc.scalar.activation(y[:, a:b], bank[:], ACT.Relu)
-        z_late = tile([P, S - FAR_CUT], F32, "z_late")
-        far_experts(FAR_CUT, S, far_words1_late, z_late)
+        far_banks.extend(far_experts(FAR_CUT, S, far_words1_late))
+        z = placed([P, S], F32, "z", WOVEN_BYTES)
+        for lo, hi, bank in far_banks:
+            nc.scalar.activation(z[:, lo:hi], bank[:], ACT.Relu)
+            nc.sync.dma_start(out[:, T + lo : T + hi], z[:, lo:hi])
 
         first = tile([P, T], F32, "first")
         nc.vector.tensor_tensor(first[:], y[:].indirect(pos_list[0][:]), gates[0][:], ALU.mult)

@@ -25,11 +25,11 @@ LIST_ROWS = 16
 WIDE = 2048
 CHUNK = 512
 OWN = ((0, 512), (512, 1024), (1024, 1280), (1280, S))
-FAR_CUT = 768
+FAR_CUT = 896
+FAR_SPARE = 256
 SCALE_ROWS = P - PASSES * 16
-GPSIMD_MORE = 256
 WOVEN_BYTES = PASSES * PACK * CHUNK * 2
-TOKEN_PARTS = (((0, T // 2), (T // 2, T)), ((0, T),))
+TOKEN_PARTS = ((0, T // 2), (T // 2, T))
 COMBINE = ((0, 384), (384, 640), (640, T))
 
 
@@ -60,8 +60,9 @@ def tile_moe_loc_lin_relu_kernel(
         far_scale = tile([P, PASSES * S], U8, "far_scale")
         nc.vector.memset(far_scale_table[:SCALE_ROWS, :].bitcast(I32), 0)
         nc.vector.memset(far_scale_table[SCALE_ROWS:, Q:].bitcast(I32), 0)
-        singles = tile([P, T + WIDE], BF16, "singles")
-        for zeroed in (singles[:, 2 * T :], far_scale[:], w_scale[:]):
+        singles = tile([P, 2 * T + WIDE], BF16, "singles")
+        far_table = [tile([P, Q + s * FAR_SPARE], I32, "far_table%d" % s) for s in range(PASSES)]
+        for zeroed in (singles[:, 3 * T :], far_scale[:], w_scale[:], far_table[1][:, Q:]):
             nc.gpsimd.memset(zeroed.bitcast(I32), 0)
 
         xo_k = xo.rearrange("(s p u e) t -> s u p e t", s=PASSES, u=2, e=2)
@@ -77,16 +78,17 @@ def tile_moe_loc_lin_relu_kernel(
             return pair_table[:, at : at + width]
 
         raw_first = [tile([P, T // 2], F32, "raw_first%d" % h) for h in range(2)]
-        raw_second = tile([P, T], F32, "raw_second")
-        raw_last = tile([P, 2 * T], F32, "raw_last")
-        far_table = [tile([P, Q], I32, "far_table%d" % s) for s in range(PASSES)]
+        raw_single = [None] + [tile([P, T], F32, "raw_single%d" % d) for d in range(1, PACK)]
+
+        def load_single(d):
+            nc.sync.dma_start(raw_single[d][:], xo_k[1, d // 2, :, d % 2, :])
 
         def load_pair(u):
-            for a, b in TOKEN_PARTS[u]:
+            for a, b in TOKEN_PARTS:
                 nc.sync.dma_start(raw_pair(u, a, b), xo_k[0, u, :, :, a:b])
 
         def load_far_words(s):
-            nc.sync.dma_start(far_table[s][:], x_words[s].rearrange("p t d -> p (t d)").bitcast(I32))
+            nc.sync.dma_start(far_table[s][:, :Q], x_words[s].rearrange("p t d -> p (t d)").bitcast(I32))
 
         nc.sync.dma_start(far_list[:], offs2)
         nc.scalar.dma_start(far_scale_table[SCALE_ROWS:, :Q].bitcast(I32), x_scales.bitcast(I32).rearrange("s b t -> (s b) t"))
@@ -94,10 +96,10 @@ def tile_moe_loc_lin_relu_kernel(
             nc.sync.dma_start(raw_first[h][:], xo_k[1, 0, :, 0, h * T // 2 : (h + 1) * T // 2])
         nc.sync.dma_start(own_list[:], offs)
         load_far_words(0)
-        nc.sync.dma_start(raw_second[:], xo_k[1, 0, :, 1, :])
-        load_pair(0)
-        nc.sync.dma_start(raw_last[:].rearrange("p (e t) -> p e t", e=2), xo_k[1, 1])
-        load_pair(1)
+        for u in range(2):
+            load_single(u + 1)
+            load_pair(u)
+        load_single(3)
         load_far_words(1)
         w_scale_rows = tile([P, E * PASSES * N], U8, "w_scale_rows")
         nc.sync.dma_start(
@@ -128,30 +130,30 @@ def tile_moe_loc_lin_relu_kernel(
         nc.sync.dma_start(pos_list[0][:], pos1)
         nc.sync.dma_start(pos_list[1][:], pos2)
 
-        last_singles = tile([P, 2 * T], BF16, "last_singles")
+        last_single = placed([P, T], BF16, "last_single", 2 * WOVEN_BYTES)
 
         def single(d, width=T):
-            if d >= 2:
-                return last_singles[:, (d - 2) * T : (d - 1) * T]
-            at = (1 - d) * T
+            if d == PACK - 1:
+                return last_single[:]
+            at = (PACK - 2 - d) * T
             return singles[:, at : at + width]
 
         def round_on_gpsimd(dst, src):
             nc.gpsimd.tensor_scalar(dst, src, 1.0, 0.0, ALU.mult, ALU.add)
 
         def round_pair(u):
-            for a, b in TOKEN_PARTS[u]:
+            for a, b in TOKEN_PARTS:
                 dst = pair_words(u, T)[:, a:b].bitcast(BF16).rearrange("p (t e) -> p t e", e=2)
                 round_on_gpsimd(dst, raw_pair(u, a, b).rearrange("p e t -> p t e"))
 
         nc.scalar.activation(single(0)[:, : T // 2], raw_first[0][:], ACT.Copy)
         round_on_gpsimd(single(0)[:, T // 2 :], raw_first[1][:])
-        round_on_gpsimd(single(1), raw_second[:])
-        round_pair(0)
-        round_on_gpsimd(last_singles[:], raw_last[:])
-        round_pair(1)
+        for u in range(2):
+            round_on_gpsimd(single(u + 1), raw_single[u + 1][:])
+            round_pair(u)
+        round_on_gpsimd(single(3), raw_single[3][:])
 
-        gates = [tile([P, T], F32, "gate%d" % r, ("raw_last", "raw_second")[r]) for r in range(2)]
+        gates = [tile([P, T], F32, "gate%d" % r, "raw_single%d" % (r + 1)) for r in range(2)]
         for r in range(2):
             nc.sync.dma_start(gates[r][:], gate[r])
 
@@ -165,11 +167,10 @@ def tile_moe_loc_lin_relu_kernel(
         def gather_pair(u, a, b, width):
             nc.vector.tensor_copy(halves[0][:, u * S + a : u * S + b], pair_words(u, width).bitcast(U32).indirect(entries(own_list, a, b)))
 
-        gather_single(0, 0, S, WIDE)
-        gather_single(1, 0, S, WIDE)
+        for d in range(PACK - 1):
+            gather_single(d, 0, S, WIDE)
         for c in range(S // CHUNK):
-            for d in (2, 3):
-                gather_single(d, c * CHUNK, (c + 1) * CHUNK, T)
+            gather_single(PACK - 1, c * CHUNK, (c + 1) * CHUNK, T)
 
         def gather_far_words(dst, s, a, b):
             nc.vector.tensor_copy(dst, far_table[s][:].bitcast(U32).indirect(entries(far_list, a, b)))
@@ -200,15 +201,15 @@ def tile_moe_loc_lin_relu_kernel(
             dst = woven_range(i)[:, PACK * (s * (b - a) + lo) : PACK * (s * (b - a) + hi)].bitcast(U32).rearrange("p (j u) -> p j u", u=2)
             copy(dst, slot_words(s, a + lo, a + hi))
 
-        for s, i in ((1, 0), (0, 0), (0, 1)):
+        for s, i in ((0, 0), (0, 1), (1, 0)):
             weave(nc.gpsimd.tensor_copy, s, i)
-        weave(nc.gpsimd.tensor_copy, 1, 1, 0, GPSIMD_MORE)
-        weave(nc.scalar.copy, 1, 1, GPSIMD_MORE)
+        weave(nc.scalar.copy, 1, 1)
         for i in (2, 3):
             for s in (1, 0):
                 weave(nc.scalar.copy, s, i)
 
-        own_words = [tile([P, PASSES * (b - a)], U32, "own_words%d" % a) for a, b in OWN[:2]]
+        own_words = [tile([P, PASSES * (b - a)], U32, "own_words%d" % a) for a, b in OWN[:1]]
+        own_words.append(placed([P, PASSES * CHUNK], U32, "own_words%d" % CHUNK, 0))
         own_words += [placed([P, PASSES * (b - a)], U32, "own_words%d" % a, WOVEN_BYTES + 4 * PASSES * (a % CHUNK)) for a, b in OWN[2:]]
         own_scale = [tile([P, PASSES * (b - a)], U8, "own_scale%d" % a) for a, b in OWN]
         for i in range(len(OWN)):
@@ -233,7 +234,7 @@ def tile_moe_loc_lin_relu_kernel(
 
         def far_experts(a, b, words1):
             banks = []
-            for lo, hi in ((a, a + CHUNK), (a + CHUNK, b)):
+            for lo, hi in ((a, b - CHUNK), (b - CHUNK, b)) if a else ((a, a + CHUNK), (a + CHUNK, b)):
                 bank = ps.tile([P, hi - lo], F32, name="far%d" % lo)
                 experts(lo, hi, bank, [far_words0[:, lo:hi], words1[:, lo - a : hi - a]], [far_scale[:, lo:hi], far_scale[:, S + lo : S + hi]])
                 banks.append((lo, hi, bank))

@@ -26,7 +26,7 @@ WIDE = 2048
 CHUNK = 512
 OWN = ((0, 512), (512, 1024), (1024, 1280), (1280, S))
 FAR_CUT = 896
-FAR_SPARE = 256
+FAR_WINDOW = 1280
 SCALE_ROWS = P - PASSES * 16
 WOVEN_BYTES = PASSES * PACK * CHUNK * 2
 TOKEN_PARTS = ((0, T // 2), (T // 2, T))
@@ -56,14 +56,13 @@ def tile_moe_loc_lin_relu_kernel(
         pos_list = [tile([P, T // LIST_ROWS], U16, "pos_list%d" % r) for r in range(2)]
 
         far_scale_table = tile([P, WIDE], U8, "far_scale_table")
-        w_scale = tile([P, E * PASSES * N], U8, "w_scale")
         far_scale = tile([P, PASSES * S], U8, "far_scale")
         nc.vector.memset(far_scale_table[:SCALE_ROWS, :].bitcast(I32), 0)
         nc.vector.memset(far_scale_table[SCALE_ROWS:, Q:].bitcast(I32), 0)
+        nc.vector.memset(far_scale[:].bitcast(I32), 0)
         singles = tile([P, 2 * T + WIDE], BF16, "singles")
-        far_table = [tile([P, Q + s * FAR_SPARE], I32, "far_table%d" % s) for s in range(PASSES)]
-        for zeroed in (singles[:, 3 * T :], far_scale[:], w_scale[:], far_table[1][:, Q:]):
-            nc.gpsimd.memset(zeroed.bitcast(I32), 0)
+        nc.gpsimd.memset(singles[:, 3 * T :].bitcast(I32), 0)
+        far_table = tile([P, PASSES * Q], I32, "far_table")
 
         xo_k = xo.rearrange("(s p u e) t -> s u p e t", s=PASSES, u=2, e=2)
         pair_table = tile([P, 4 * T], F32, "pair_table")
@@ -88,7 +87,7 @@ def tile_moe_loc_lin_relu_kernel(
                 nc.sync.dma_start(raw_pair(u, a, b), xo_k[0, u, :, :, a:b])
 
         def load_far_words(s):
-            nc.sync.dma_start(far_table[s][:, :Q], x_words[s].rearrange("p t d -> p (t d)").bitcast(I32))
+            nc.sync.dma_start(far_table[:, (1 - s) * Q : (2 - s) * Q], x_words[s].rearrange("p t d -> p (t d)").bitcast(I32))
 
         nc.sync.dma_start(far_list[:], offs2)
         nc.scalar.dma_start(far_scale_table[SCALE_ROWS:, :Q].bitcast(I32), x_scales.bitcast(I32).rearrange("s b t -> (s b) t"))
@@ -106,6 +105,22 @@ def tile_moe_loc_lin_relu_kernel(
             w_scale_rows[:16, :].bitcast(I32).rearrange("b (g n) -> b g n", n=N // 4),
             w_scales.bitcast(I32).rearrange("e s b n -> b (e s) n"),
         )
+
+        last_single = tile([P, T], BF16, "last_single")
+
+        def single(d, width=T):
+            if d == PACK - 1:
+                return last_single[:]
+            at = (PACK - 2 - d) * T
+            return singles[:, at : at + width]
+
+        def round_on_gpsimd(dst, src):
+            nc.gpsimd.tensor_scalar(dst, src, 1.0, 0.0, ALU.mult, ALU.add)
+
+        nc.scalar.activation(single(0)[:, : T // 2], raw_first[0][:], ACT.Copy)
+        round_on_gpsimd(single(0)[:, T // 2 :], raw_first[1][:])
+        w_scale = tile([P, E * PASSES * N], U8, "w_scale", "raw_first1")
+        nc.gpsimd.memset(w_scale[:].bitcast(I32), 0)
 
         far_scale_rows = tile([P, S], U8, "far_scale_rows")
         nc.vector.tensor_copy(far_scale_rows[:], far_scale_table[:].indirect(far_list[:]))
@@ -130,24 +145,11 @@ def tile_moe_loc_lin_relu_kernel(
         nc.sync.dma_start(pos_list[0][:], pos1)
         nc.sync.dma_start(pos_list[1][:], pos2)
 
-        last_single = placed([P, T], BF16, "last_single", 2 * WOVEN_BYTES)
-
-        def single(d, width=T):
-            if d == PACK - 1:
-                return last_single[:]
-            at = (PACK - 2 - d) * T
-            return singles[:, at : at + width]
-
-        def round_on_gpsimd(dst, src):
-            nc.gpsimd.tensor_scalar(dst, src, 1.0, 0.0, ALU.mult, ALU.add)
-
         def round_pair(u):
             for a, b in TOKEN_PARTS:
                 dst = pair_words(u, T)[:, a:b].bitcast(BF16).rearrange("p (t e) -> p t e", e=2)
                 round_on_gpsimd(dst, raw_pair(u, a, b).rearrange("p e t -> p t e"))
 
-        nc.scalar.activation(single(0)[:, : T // 2], raw_first[0][:], ACT.Copy)
-        round_on_gpsimd(single(0)[:, T // 2 :], raw_first[1][:])
         for u in range(2):
             round_on_gpsimd(single(u + 1), raw_single[u + 1][:])
             round_pair(u)
@@ -157,15 +159,22 @@ def tile_moe_loc_lin_relu_kernel(
         for r in range(2):
             nc.sync.dma_start(gates[r][:], gate[r])
 
-        halves = [tile([P, 2 * S], U32, "halves%d" % s) for s in range(PASSES)]
+        cut = 2 * CHUNK
+        halves0 = [placed([P, 2 * (b - a)], U32, "halves0_%d" % a, at) for a, b, at in ((0, cut, 2 * WOVEN_BYTES), (cut, S, 3 * WOVEN_BYTES))]
+        halves1 = tile([P, 2 * S], U32, "halves1")
+
+        def slot_words(s, a, b):
+            if s:
+                return halves1[:].rearrange("p (u j) -> p j u", u=2)[:, a:b, :]
+            return halves0[a // cut][:].rearrange("p (u j) -> p j u", u=2)[:, a % cut : a % cut + b - a, :]
 
         def gather_single(d, a, b, width):
             at = (d // 2) * S
-            dst = halves[1][:, at + a : at + b].bitcast(BF16).rearrange("p (j e) -> p e j", e=2)
+            dst = halves1[:, at + a : at + b].bitcast(BF16).rearrange("p (j e) -> p e j", e=2)
             nc.scalar.activation(dst[:, d % 2, :], single(d, width).indirect(entries(own_list, a, b)), ACT.Copy)
 
         def gather_pair(u, a, b, width):
-            nc.vector.tensor_copy(halves[0][:, u * S + a : u * S + b], pair_words(u, width).bitcast(U32).indirect(entries(own_list, a, b)))
+            nc.vector.tensor_copy(slot_words(0, a, b)[:, :, u], pair_words(u, width).bitcast(U32).indirect(entries(own_list, a, b)))
 
         for d in range(PACK - 1):
             gather_single(d, 0, S, WIDE)
@@ -173,12 +182,14 @@ def tile_moe_loc_lin_relu_kernel(
             gather_single(PACK - 1, c * CHUNK, (c + 1) * CHUNK, T)
 
         def gather_far_words(dst, s, a, b):
-            nc.vector.tensor_copy(dst, far_table[s][:].bitcast(U32).indirect(entries(far_list, a, b)))
+            window = far_table[:, :FAR_WINDOW] if s else far_table[:, Q:]
+            nc.vector.tensor_copy(dst, window.bitcast(U32).indirect(entries(far_list, a, b)))
 
         far_words0 = tile([P, S], U32, "far_words0")
         for a in (0, S // 2):
             gather_far_words(far_words0[:, a : a + S // 2], 0, a, a + S // 2)
-        gather_pair(0, 0, S, WIDE)
+        gather_pair(0, 0, cut, cut + CHUNK)
+        gather_pair(0, cut, S, T)
         gather_pair(1, 0, CHUNK, T)
         gather_pair(1, CHUNK, 2 * CHUNK, T)
         far_words1_early = tile([P, FAR_CUT], U32, "far_words1_early", "raw_pair1")
@@ -192,29 +203,24 @@ def tile_moe_loc_lin_relu_kernel(
             at = PASSES * PACK * (a % CHUNK)
             return woven[a // CHUNK][:, at : at + PASSES * PACK * (b - a)]
 
-        def slot_words(s, a, b):
-            return halves[s][:].rearrange("p (u j) -> p j u", u=2)[:, a:b, :]
-
         def weave(copy, s, i, lo=0, hi=None):
             a, b = OWN[i]
             hi = hi or b - a
             dst = woven_range(i)[:, PACK * (s * (b - a) + lo) : PACK * (s * (b - a) + hi)].bitcast(U32).rearrange("p (j u) -> p j u", u=2)
             copy(dst, slot_words(s, a + lo, a + hi))
 
-        for s, i in ((0, 0), (0, 1), (1, 0)):
+        for s, i in ((0, 0), (1, 0), (0, 1)):
             weave(nc.gpsimd.tensor_copy, s, i)
         weave(nc.scalar.copy, 1, 1)
         for i in (2, 3):
             for s in (1, 0):
                 weave(nc.scalar.copy, s, i)
 
-        own_words = [tile([P, PASSES * (b - a)], U32, "own_words%d" % a) for a, b in OWN[:1]]
-        own_words.append(placed([P, PASSES * CHUNK], U32, "own_words%d" % CHUNK, 0))
-        own_words += [placed([P, PASSES * (b - a)], U32, "own_words%d" % a, WOVEN_BYTES + 4 * PASSES * (a % CHUNK)) for a, b in OWN[2:]]
+        own_words = [placed([P, PASSES * (b - a)], U32, "own_words%d" % a, 4 * WOVEN_BYTES + 4 * PASSES * a) for a, b in OWN]
         own_scale = [tile([P, PASSES * (b - a)], U8, "own_scale%d" % a) for a, b in OWN]
         for i in range(len(OWN)):
             nc.vector.quantize_mx(own_words[i][:].bitcast(FP8X4), own_scale[i][:], woven_range(i))
-        far_words1_late = placed([P, S - FAR_CUT], U32, "far_words1_late", 2 * WOVEN_BYTES)
+        far_words1_late = placed([P, S - FAR_CUT], U32, "far_words1_late", 3 * WOVEN_BYTES)
         gather_far_words(far_words1_late[:], 1, FAR_CUT, S)
 
         def experts(a, b, bank, words, scale):
@@ -248,7 +254,7 @@ def tile_moe_loc_lin_relu_kernel(
             experts(a, b, bank, [own_words[i][:, col] for col in cols], [own_scale[i][:, col] for col in cols])
             nc.scalar.activation(y[:, a:b], bank[:], ACT.Relu)
         far_banks.extend(far_experts(FAR_CUT, S, far_words1_late))
-        z = placed([P, S], F32, "z", WOVEN_BYTES)
+        z = placed([P, S], F32, "z", 4 * WOVEN_BYTES + 4 * S)
         for lo, hi, bank in far_banks:
             nc.scalar.activation(z[:, lo:hi], bank[:], ACT.Relu)
             nc.sync.dma_start(out[:, T + lo : T + hi], z[:, lo:hi])

@@ -25,8 +25,9 @@ LIST_ROWS = 16
 WIDE = 2048
 CHUNK = 512
 OWN = ((0, 512), (512, 1024), (1024, 1280), (1280, S))
-FAR_CUT = 896
-FAR_WINDOW = 1280
+FAR_CUT = 1152
+FAR_WINDOW = 1536
+GPSIMD_MORE = 256
 SCALE_ROWS = P - PASSES * 16
 WOVEN_BYTES = PASSES * PACK * CHUNK * 2
 TOKEN_PARTS = ((0, T // 2), (T // 2, T))
@@ -59,14 +60,14 @@ def tile_moe_loc_lin_relu_kernel(
         far_scale = tile([P, PASSES * S], U8, "far_scale")
         nc.vector.memset(far_scale_table[:SCALE_ROWS, :].bitcast(I32), 0)
         nc.vector.memset(far_scale_table[SCALE_ROWS:, Q:].bitcast(I32), 0)
-        nc.vector.memset(far_scale[:].bitcast(I32), 0)
+        far_table = tile([P, Q + FAR_WINDOW], I32, "far_table")
+        nc.vector.memset(far_table[:, PASSES * Q :], 0)
         singles = tile([P, 2 * T + WIDE], BF16, "singles")
         nc.gpsimd.memset(singles[:, 3 * T :].bitcast(I32), 0)
-        far_table = tile([P, PASSES * Q], I32, "far_table")
 
         xo_k = xo.rearrange("(s p u e) t -> s u p e t", s=PASSES, u=2, e=2)
         pair_table = tile([P, 4 * T], F32, "pair_table")
-        raw_pair1 = tile([P, 2 * T], F32, "raw_pair1")
+        raw_pair1 = placed([P, 2 * T], F32, "raw_pair1", 5 * WOVEN_BYTES)
 
         def raw_pair(u, a, b):
             rows = pair_table[:, 2 * T :] if u == 0 else raw_pair1[:]
@@ -76,11 +77,11 @@ def tile_moe_loc_lin_relu_kernel(
             at = (1 - u) * T
             return pair_table[:, at : at + width]
 
-        raw_first = [tile([P, T // 2], F32, "raw_first%d" % h) for h in range(2)]
+        raw_first = [tile([P, T // 2], F32, "raw_first%d" % h)[:] for h in range(2)]
         raw_single = [None] + [tile([P, T], F32, "raw_single%d" % d) for d in range(1, PACK)]
 
         def load_single(d):
-            nc.sync.dma_start(raw_single[d][:], xo_k[1, d // 2, :, d % 2, :])
+            nc.sync.dma_start(raw_single[d][:], xo_k[1, d % 2, :, d // 2, :])
 
         def load_pair(u):
             for a, b in TOKEN_PARTS:
@@ -92,12 +93,13 @@ def tile_moe_loc_lin_relu_kernel(
         nc.sync.dma_start(far_list[:], offs2)
         nc.scalar.dma_start(far_scale_table[SCALE_ROWS:, :Q].bitcast(I32), x_scales.bitcast(I32).rearrange("s b t -> (s b) t"))
         for h in range(2):
-            nc.sync.dma_start(raw_first[h][:], xo_k[1, 0, :, 0, h * T // 2 : (h + 1) * T // 2])
+            nc.sync.dma_start(raw_first[h], xo_k[1, 0, :, 0, h * T // 2 : (h + 1) * T // 2])
         nc.sync.dma_start(own_list[:], offs)
+        load_single(1)
         load_far_words(0)
-        for u in range(2):
-            load_single(u + 1)
-            load_pair(u)
+        load_pair(0)
+        load_single(2)
+        load_pair(1)
         load_single(3)
         load_far_words(1)
         w_scale_rows = tile([P, E * PASSES * N], U8, "w_scale_rows")
@@ -106,7 +108,7 @@ def tile_moe_loc_lin_relu_kernel(
             w_scales.bitcast(I32).rearrange("e s b n -> b (e s) n"),
         )
 
-        last_single = tile([P, T], BF16, "last_single")
+        last_single = placed([P, T], BF16, "last_single", 2 * WOVEN_BYTES)
 
         def single(d, width=T):
             if d == PACK - 1:
@@ -117,10 +119,11 @@ def tile_moe_loc_lin_relu_kernel(
         def round_on_gpsimd(dst, src):
             nc.gpsimd.tensor_scalar(dst, src, 1.0, 0.0, ALU.mult, ALU.add)
 
-        nc.scalar.activation(single(0)[:, : T // 2], raw_first[0][:], ACT.Copy)
-        round_on_gpsimd(single(0)[:, T // 2 :], raw_first[1][:])
-        w_scale = tile([P, E * PASSES * N], U8, "w_scale", "raw_first1")
-        nc.gpsimd.memset(w_scale[:].bitcast(I32), 0)
+        nc.scalar.activation(single(0)[:, : T // 2], raw_first[0], ACT.Copy)
+        round_on_gpsimd(single(0)[:, T // 2 :], raw_first[1])
+
+        round_on_gpsimd(single(1), raw_single[1][:])
+        w_scale = tile([P, E * PASSES * N], U8, "w_scale")
 
         far_scale_rows = tile([P, S], U8, "far_scale_rows")
         nc.vector.tensor_copy(far_scale_rows[:], far_scale_table[:].indirect(far_list[:]))
@@ -151,27 +154,22 @@ def tile_moe_loc_lin_relu_kernel(
                 round_on_gpsimd(dst, raw_pair(u, a, b).rearrange("p e t -> p t e"))
 
         for u in range(2):
-            round_on_gpsimd(single(u + 1), raw_single[u + 1][:])
             round_pair(u)
-        round_on_gpsimd(single(3), raw_single[3][:])
+            round_on_gpsimd(single(u + 2), raw_single[u + 2][:])
 
-        gates = [tile([P, T], F32, "gate%d" % r, "raw_single%d" % (r + 1)) for r in range(2)]
+        gates = [tile([P, T], F32, "gate%d" % r, "raw_single%d" % (r + 2)) for r in range(2)]
         for r in range(2):
             nc.sync.dma_start(gates[r][:], gate[r])
 
-        cut = 2 * CHUNK
-        halves0 = [placed([P, 2 * (b - a)], U32, "halves0_%d" % a, at) for a, b, at in ((0, cut, 2 * WOVEN_BYTES), (cut, S, 3 * WOVEN_BYTES))]
-        halves1 = tile([P, 2 * S], U32, "halves1")
+        halves = [tile([P, 2 * S], U32, "halves%d" % s) for s in range(PASSES)]
 
         def slot_words(s, a, b):
-            if s:
-                return halves1[:].rearrange("p (u j) -> p j u", u=2)[:, a:b, :]
-            return halves0[a // cut][:].rearrange("p (u j) -> p j u", u=2)[:, a % cut : a % cut + b - a, :]
+            return halves[s][:].rearrange("p (u j) -> p j u", u=2)[:, a:b, :]
 
         def gather_single(d, a, b, width):
-            at = (d // 2) * S
-            dst = halves1[:, at + a : at + b].bitcast(BF16).rearrange("p (j e) -> p e j", e=2)
-            nc.scalar.activation(dst[:, d % 2, :], single(d, width).indirect(entries(own_list, a, b)), ACT.Copy)
+            at = (d % 2) * S
+            dst = halves[1][:, at + a : at + b].bitcast(BF16).rearrange("p (j e) -> p e j", e=2)
+            nc.scalar.activation(dst[:, d // 2, :], single(d, width).indirect(entries(own_list, a, b)), ACT.Copy)
 
         def gather_pair(u, a, b, width):
             nc.vector.tensor_copy(slot_words(0, a, b)[:, :, u], pair_words(u, width).bitcast(U32).indirect(entries(own_list, a, b)))
@@ -182,18 +180,16 @@ def tile_moe_loc_lin_relu_kernel(
             gather_single(PACK - 1, c * CHUNK, (c + 1) * CHUNK, T)
 
         def gather_far_words(dst, s, a, b):
-            window = far_table[:, :FAR_WINDOW] if s else far_table[:, Q:]
+            at = (1 - s) * Q
+            window = far_table[:, at : at + (Q if a else FAR_WINDOW)]
             nc.vector.tensor_copy(dst, window.bitcast(U32).indirect(entries(far_list, a, b)))
 
-        far_words0 = tile([P, S], U32, "far_words0")
-        for a in (0, S // 2):
-            gather_far_words(far_words0[:, a : a + S // 2], 0, a, a + S // 2)
-        gather_pair(0, 0, cut, cut + CHUNK)
-        gather_pair(0, cut, S, T)
+        far_early = [tile([P, FAR_CUT], U32, "far_early0"), placed([P, FAR_CUT], U32, "far_early1", 5 * WOVEN_BYTES)]
+        gather_far_words(far_early[0][:], 0, 0, FAR_CUT)
+        gather_pair(0, 0, S, WIDE)
         gather_pair(1, 0, CHUNK, T)
         gather_pair(1, CHUNK, 2 * CHUNK, T)
-        far_words1_early = tile([P, FAR_CUT], U32, "far_words1_early", "raw_pair1")
-        gather_far_words(far_words1_early[:], 1, 0, FAR_CUT)
+        gather_far_words(far_early[1][:], 1, 0, FAR_CUT)
         gather_pair(1, 2 * CHUNK, S, T)
 
         woven = [placed([P, PASSES * PACK * CHUNK], BF16, "woven%d" % c, c * WOVEN_BYTES) for c in range(S // CHUNK)]
@@ -209,19 +205,22 @@ def tile_moe_loc_lin_relu_kernel(
             dst = woven_range(i)[:, PACK * (s * (b - a) + lo) : PACK * (s * (b - a) + hi)].bitcast(U32).rearrange("p (j u) -> p j u", u=2)
             copy(dst, slot_words(s, a + lo, a + hi))
 
-        for s, i in ((0, 0), (1, 0), (0, 1)):
+        for s, i in ((0, 0), (0, 1), (1, 0)):
             weave(nc.gpsimd.tensor_copy, s, i)
-        weave(nc.scalar.copy, 1, 1)
+        weave(nc.gpsimd.tensor_copy, 1, 1, 0, GPSIMD_MORE)
+        weave(nc.scalar.copy, 1, 1, GPSIMD_MORE)
         for i in (2, 3):
             for s in (1, 0):
                 weave(nc.scalar.copy, s, i)
 
-        own_words = [placed([P, PASSES * (b - a)], U32, "own_words%d" % a, 4 * WOVEN_BYTES + 4 * PASSES * a) for a, b in OWN]
+        own_words = [tile([P, PASSES * (b - a)], U32, "own_words%d" % a) for a, b in OWN[:2]]
+        own_words += [placed([P, PASSES * (b - a)], U32, "own_words%d" % a, 4 * PASSES * (a % CHUNK)) for a, b in OWN[2:]]
         own_scale = [tile([P, PASSES * (b - a)], U8, "own_scale%d" % a) for a, b in OWN]
         for i in range(len(OWN)):
             nc.vector.quantize_mx(own_words[i][:].bitcast(FP8X4), own_scale[i][:], woven_range(i))
-        far_words1_late = placed([P, S - FAR_CUT], U32, "far_words1_late", 3 * WOVEN_BYTES)
-        gather_far_words(far_words1_late[:], 1, FAR_CUT, S)
+        far_late = [placed([P, S - FAR_CUT], U32, "far_late%d" % s, WOVEN_BYTES + s * WOVEN_BYTES // 2) for s in range(PASSES)]
+        for s in range(PASSES):
+            gather_far_words(far_late[s][:], s, FAR_CUT, S)
 
         def experts(a, b, bank, words, scale):
             for j in range((b - a) // C):
@@ -238,23 +237,24 @@ def tile_moe_loc_lin_relu_kernel(
                         stop=(s == PASSES - 1),
                     )
 
-        def far_experts(a, b, words1):
+        def far_experts(a, b, words):
             banks = []
-            for lo, hi in ((a, b - CHUNK), (b - CHUNK, b)) if a else ((a, a + CHUNK), (a + CHUNK, b)):
+            for lo in range(a, b, CHUNK):
+                hi = min(lo + CHUNK, b)
                 bank = ps.tile([P, hi - lo], F32, name="far%d" % lo)
-                experts(lo, hi, bank, [far_words0[:, lo:hi], words1[:, lo - a : hi - a]], [far_scale[:, lo:hi], far_scale[:, S + lo : S + hi]])
+                experts(lo, hi, bank, [w[:, lo - a : hi - a] for w in words], [far_scale[:, lo:hi], far_scale[:, S + lo : S + hi]])
                 banks.append((lo, hi, bank))
             return banks
 
-        far_banks = far_experts(0, FAR_CUT, far_words1_early)
+        far_banks = far_experts(0, FAR_CUT, far_early)
         y = tile([P, S], F32, "y")
         for i, (a, b) in enumerate(OWN):
             bank = ps.tile([P, b - a], F32, name="own%d" % a)
             cols = [slice(s * (b - a), (s + 1) * (b - a)) for s in range(PASSES)]
             experts(a, b, bank, [own_words[i][:, col] for col in cols], [own_scale[i][:, col] for col in cols])
             nc.scalar.activation(y[:, a:b], bank[:], ACT.Relu)
-        far_banks.extend(far_experts(FAR_CUT, S, far_words1_late))
-        z = placed([P, S], F32, "z", 4 * WOVEN_BYTES + 4 * S)
+        far_banks.extend(far_experts(FAR_CUT, S, far_late))
+        z = placed([P, S], F32, "z", 0)
         for lo, hi, bank in far_banks:
             nc.scalar.activation(z[:, lo:hi], bank[:], ACT.Relu)
             nc.sync.dma_start(out[:, T + lo : T + hi], z[:, lo:hi])

@@ -25,13 +25,12 @@ LIST_ROWS = 16
 WIDE = 2048
 CHUNK = 512
 OWN = ((0, 512), (512, 1024), (1024, 1280), (1280, S))
-FAR_CUT = 1152
-FAR_WINDOW = 1536
-GPSIMD_MORE = 256
+FAR_CUT = 896
 SCALE_ROWS = P - PASSES * 16
 WOVEN_BYTES = PASSES * PACK * CHUNK * 2
 TOKEN_PARTS = ((0, T // 2), (T // 2, T))
-COMBINE = ((0, 384), (384, 640), (640, T))
+SECOND = ((0, 512), (512, T))
+SUM = 256
 
 
 def tile_moe_loc_lin_relu_kernel(
@@ -60,7 +59,7 @@ def tile_moe_loc_lin_relu_kernel(
         far_scale = tile([P, PASSES * S], U8, "far_scale")
         nc.vector.memset(far_scale_table[:SCALE_ROWS, :].bitcast(I32), 0)
         nc.vector.memset(far_scale_table[SCALE_ROWS:, Q:].bitcast(I32), 0)
-        far_table = tile([P, Q + FAR_WINDOW], I32, "far_table")
+        far_table = tile([P, Q + WIDE], I32, "far_table")
         nc.vector.memset(far_table[:, PASSES * Q :], 0)
         singles = tile([P, 2 * T + WIDE], BF16, "singles")
         nc.gpsimd.memset(singles[:, 3 * T :].bitcast(I32), 0)
@@ -181,16 +180,16 @@ def tile_moe_loc_lin_relu_kernel(
 
         def gather_far_words(dst, s, a, b):
             at = (1 - s) * Q
-            window = far_table[:, at : at + (Q if a else FAR_WINDOW)]
+            window = far_table[:, at : at + (Q if a else WIDE)]
             nc.vector.tensor_copy(dst, window.bitcast(U32).indirect(entries(far_list, a, b)))
 
-        far_early = [tile([P, FAR_CUT], U32, "far_early0"), placed([P, FAR_CUT], U32, "far_early1", 5 * WOVEN_BYTES)]
-        gather_far_words(far_early[0][:], 0, 0, FAR_CUT)
+        far_words0 = tile([P, S], U32, "far_words0")
+        gather_far_words(far_words0[:], 0, 0, S)
         gather_pair(0, 0, S, WIDE)
         gather_pair(1, 0, CHUNK, T)
-        gather_pair(1, CHUNK, 2 * CHUNK, T)
-        gather_far_words(far_early[1][:], 1, 0, FAR_CUT)
-        gather_pair(1, 2 * CHUNK, S, T)
+        gather_pair(1, CHUNK, S, 2 * T)
+        far_early = placed([P, FAR_CUT], U32, "far_early", 5 * WOVEN_BYTES)
+        gather_far_words(far_early[:], 1, 0, FAR_CUT)
 
         woven = [placed([P, PASSES * PACK * CHUNK], BF16, "woven%d" % c, c * WOVEN_BYTES) for c in range(S // CHUNK)]
 
@@ -205,10 +204,9 @@ def tile_moe_loc_lin_relu_kernel(
             dst = woven_range(i)[:, PACK * (s * (b - a) + lo) : PACK * (s * (b - a) + hi)].bitcast(U32).rearrange("p (j u) -> p j u", u=2)
             copy(dst, slot_words(s, a + lo, a + hi))
 
-        for s, i in ((0, 0), (0, 1), (1, 0)):
+        for s, i in ((0, 0), (1, 0), (0, 1)):
             weave(nc.gpsimd.tensor_copy, s, i)
-        weave(nc.gpsimd.tensor_copy, 1, 1, 0, GPSIMD_MORE)
-        weave(nc.scalar.copy, 1, 1, GPSIMD_MORE)
+        weave(nc.scalar.copy, 1, 1)
         for i in (2, 3):
             for s in (1, 0):
                 weave(nc.scalar.copy, s, i)
@@ -218,9 +216,8 @@ def tile_moe_loc_lin_relu_kernel(
         own_scale = [tile([P, PASSES * (b - a)], U8, "own_scale%d" % a) for a, b in OWN]
         for i in range(len(OWN)):
             nc.vector.quantize_mx(own_words[i][:].bitcast(FP8X4), own_scale[i][:], woven_range(i))
-        far_late = [placed([P, S - FAR_CUT], U32, "far_late%d" % s, WOVEN_BYTES + s * WOVEN_BYTES // 2) for s in range(PASSES)]
-        for s in range(PASSES):
-            gather_far_words(far_late[s][:], s, FAR_CUT, S)
+        far_late = placed([P, S - FAR_CUT], U32, "far_late", WOVEN_BYTES)
+        gather_far_words(far_late[:], 1, FAR_CUT, S)
 
         def experts(a, b, bank, words, scale):
             for j in range((b - a) // C):
@@ -242,7 +239,7 @@ def tile_moe_loc_lin_relu_kernel(
             for lo in range(a, b, CHUNK):
                 hi = min(lo + CHUNK, b)
                 bank = ps.tile([P, hi - lo], F32, name="far%d" % lo)
-                experts(lo, hi, bank, [w[:, lo - a : hi - a] for w in words], [far_scale[:, lo:hi], far_scale[:, S + lo : S + hi]])
+                experts(lo, hi, bank, [far_words0[:, lo:hi], words[:, lo - a : hi - a]], [far_scale[:, lo:hi], far_scale[:, S + lo : S + hi]])
                 banks.append((lo, hi, bank))
             return banks
 
@@ -261,16 +258,11 @@ def tile_moe_loc_lin_relu_kernel(
 
         first = tile([P, T], F32, "first")
         nc.vector.tensor_tensor(first[:], y[:].indirect(pos_list[0][:]), gates[0][:], ALU.mult)
-        second = [tile([P, b - a], F32, "second%d" % a) for a, b in COMBINE]
-
-        def second_product(i):
-            a, b = COMBINE[i]
-            nc.vector.tensor_tensor(second[i][:], y[:].indirect(entries(pos_list[1], a, b)), gates[1][:, a:b], ALU.mult)
-
-        second_product(0)
-        for i, (a, b) in enumerate(COMBINE):
-            if i + 1 < len(COMBINE):
-                second_product(i + 1)
-            total = tile([P, b - a], F32, "total%d" % a)
-            nc.vector.tensor_tensor(total[:], first[:, a:b], second[i][:], ALU.add)
-            nc.sync.dma_start(out[:, a:b], total[:])
+        second = [tile([P, b - a], F32, "second%d" % a) for a, b in SECOND]
+        for part, (a, b) in zip(second, SECOND):
+            nc.vector.tensor_tensor(part[:], y[:].indirect(entries(pos_list[1], a, b)), gates[1][:, a:b], ALU.mult)
+        for a in range(0, T, SUM):
+            at = a % SECOND[1][0]
+            total = tile([P, SUM], F32, "total%d" % a)
+            nc.vector.tensor_tensor(total[:], first[:, a : a + SUM], second[a // SECOND[1][0]][:, at : at + SUM], ALU.add)
+            nc.sync.dma_start(out[:, a : a + SUM], total[:])

@@ -1,6 +1,7 @@
 from contextlib import ExitStack
 
 import concourse.mybir as mybir
+from concourse.masks import make_identity
 
 K, T, Q, E, C, N = 1024, 768, 1024, 12, 128, 128
 S = E * C
@@ -29,7 +30,7 @@ FAR_CUT = 896
 SCALE_ROWS = P - PASSES * 16
 WOVEN_BYTES = PASSES * PACK * CHUNK * 2
 TOKEN_PARTS = ((0, T // 2), (T // 2, T))
-SECOND = ((0, 512), (512, T))
+TURNED = 256
 SUM = 256
 
 
@@ -156,9 +157,9 @@ def tile_moe_loc_lin_relu_kernel(
             round_pair(u)
             round_on_gpsimd(single(u + 2), raw_single[u + 2][:])
 
-        gates = [tile([P, T], F32, "gate%d" % r, "raw_single%d" % (r + 2)) for r in range(2)]
-        for r in range(2):
-            nc.sync.dma_start(gates[r][:], gate[r])
+        gate_pair = tile([P, 2 * T], F32, "gate_pair", "raw_single1")
+        nc.sync.dma_start(gate_pair[:].rearrange("p (r t) -> p r t", r=2), gate.rearrange("r p t -> p r t"))
+        gates = [gate_pair[:, r * T : (r + 1) * T] for r in range(2)]
 
         halves = [tile([P, 2 * S], U32, "halves%d" % s) for s in range(PASSES)]
 
@@ -216,6 +217,8 @@ def tile_moe_loc_lin_relu_kernel(
         own_scale = [tile([P, PASSES * (b - a)], U8, "own_scale%d" % a) for a, b in OWN]
         for i in range(len(OWN)):
             nc.vector.quantize_mx(own_words[i][:].bitcast(FP8X4), own_scale[i][:], woven_range(i))
+        identity = placed([P, P], F32, "identity", 2 * WOVEN_BYTES)
+        make_identity(nc, identity[:])
         far_late = placed([P, S - FAR_CUT], U32, "far_late", WOVEN_BYTES)
         gather_far_words(far_late[:], 1, FAR_CUT, S)
 
@@ -256,13 +259,28 @@ def tile_moe_loc_lin_relu_kernel(
             nc.scalar.activation(z[:, lo:hi], bank[:], ACT.Relu)
             nc.sync.dma_start(out[:, T + lo : T + hi], z[:, lo:hi])
 
-        first = tile([P, T], F32, "first")
-        nc.vector.tensor_tensor(first[:], y[:].indirect(pos_list[0][:]), gates[0][:], ALU.mult)
-        second = [tile([P, b - a], F32, "second%d" % a) for a, b in SECOND]
-        for part, (a, b) in zip(second, SECOND):
-            nc.vector.tensor_tensor(part[:], y[:].indirect(entries(pos_list[1], a, b)), gates[1][:, a:b], ALU.mult)
-        for a in range(0, T, SUM):
-            at = a % SECOND[1][0]
+        def product(r, a, b):
+            part = tile([P, b - a], F32, "product%d_%d" % (r, a))
+            nc.vector.tensor_tensor(part[:], y[:].indirect(entries(pos_list[r], a, b)), gates[r][:, a:b], ALU.mult)
+            return part
+
+        early = [product(r, 0, TURNED) for r in range(2)]
+        first = product(0, TURNED, T)
+        second = [product(1, a, a + SUM) for a in range(TURNED, T, SUM)]
+        early_total = tile([P, TURNED], F32, "early_total")
+        turned = []
+        for i, a in enumerate(range(0, TURNED, P)):
+            turned_bank = ps.tile([P, P], F32, name="turned_bank%d" % a, tag="own%d" % OWN[i][0])
+            for r in range(2):
+                nc.tensor.matmul(turned_bank[:], early[r][:, a : a + P], identity[:], start=(r == 0), stop=(r == 1), is_transpose=True)
+            turned.append(tile([P, P], F32, "turned%d" % a))
+            nc.scalar.copy(turned[i][:], turned_bank[:])
+        for i, a in enumerate(range(0, TURNED, P)):
+            back_bank = ps.tile([P, P], F32, name="back_bank%d" % a, tag="own%d" % OWN[i + 2][0])
+            nc.tensor.transpose(back_bank[:], turned[i][:], identity[:])
+            nc.scalar.copy(early_total[:, a : a + P], back_bank[:])
+        nc.scalar.dma_start(out[:, :TURNED], early_total[:])
+        for part, a in zip(second, range(TURNED, T, SUM)):
             total = tile([P, SUM], F32, "total%d" % a)
-            nc.vector.tensor_tensor(total[:], first[:, a : a + SUM], second[a // SECOND[1][0]][:, at : at + SUM], ALU.add)
+            nc.vector.tensor_tensor(total[:], first[:, a - TURNED : a - TURNED + SUM], part[:], ALU.add)
             nc.sync.dma_start(out[:, a : a + SUM], total[:])

@@ -30,6 +30,7 @@ FAR_CUT = 896
 SCALE_ROWS = P - PASSES * 16
 WOVEN_BYTES = PASSES * PACK * CHUNK * 2
 TOKEN_PARTS = ((0, T // 2), (T // 2, T))
+V_IN, V_OUT, SHARED, S_IN, S_OUT = 0, 28672, 65536, 131072, 147456
 TURNED = 256
 SUM = 256
 
@@ -39,15 +40,22 @@ def tile_moe_loc_lin_relu_kernel(
 ):
     nc = tc.nc
     with ExitStack() as ctx:
-        sb = ctx.enter_context(tc.tile_pool(name="sb", bufs=1))
         heirs = ctx.enter_context(tc.tile_pool(name="heirs", bufs=1))
+        sb = ctx.enter_context(tc.tile_pool(name="sb", bufs=1))
         ps = ctx.enter_context(tc.psum_pool(name="ps", bufs=1))
 
         def tile(shape, dtype, name, after=None):
             return sb.tile(shape, dtype, name=name, tag=after or name, align_bytes=64)
 
         def placed(shape, dtype, name, offset):
-            return heirs.tile(shape, dtype, name=name, offset=offset, align_bytes=64)
+            return heirs.tile(shape, dtype, name=name, offset=SHARED + offset, align_bytes=64)
+
+        used = {V_IN: 0, V_OUT: 0, S_IN: 0, S_OUT: 0}
+
+        def in_region(region, shape, dtype, name, size):
+            at = region + used[region]
+            used[region] = used[region] + size
+            return heirs.tile(shape, dtype, name=name, offset=at, align_bytes=64)
 
         def entries(lst, a, b):
             return lst[:, a // LIST_ROWS : b // LIST_ROWS]
@@ -56,17 +64,17 @@ def tile_moe_loc_lin_relu_kernel(
         far_list = tile([P, S // LIST_ROWS], U16, "far_list")
         pos_list = [tile([P, T // LIST_ROWS], U16, "pos_list%d" % r) for r in range(2)]
 
-        far_scale_table = tile([P, WIDE], U8, "far_scale_table")
+        far_scale_table = in_region(V_IN, [P, WIDE], U8, "far_scale_table", WIDE)
         far_scale = tile([P, PASSES * S], U8, "far_scale")
         nc.vector.memset(far_scale_table[:SCALE_ROWS, :].bitcast(I32), 0)
         nc.vector.memset(far_scale_table[SCALE_ROWS:, Q:].bitcast(I32), 0)
-        far_table = tile([P, Q + WIDE], I32, "far_table")
+        far_table = in_region(V_IN, [P, Q + WIDE], I32, "far_table", 4 * (Q + WIDE))
         nc.vector.memset(far_table[:, PASSES * Q :], 0)
-        singles = tile([P, 2 * T + WIDE], BF16, "singles")
+        singles = in_region(S_IN, [P, 2 * T + WIDE], BF16, "singles", 2 * (2 * T + WIDE))
         nc.gpsimd.memset(singles[:, 3 * T :].bitcast(I32), 0)
 
         xo_k = xo.rearrange("(s p u e) t -> s u p e t", s=PASSES, u=2, e=2)
-        pair_table = tile([P, 4 * T], F32, "pair_table")
+        pair_table = in_region(V_IN, [P, 4 * T], F32, "pair_table", 16 * T)
         raw_pair1 = placed([P, 2 * T], F32, "raw_pair1", 5 * WOVEN_BYTES)
 
         def raw_pair(u, a, b):
@@ -125,7 +133,7 @@ def tile_moe_loc_lin_relu_kernel(
         round_on_gpsimd(single(1), raw_single[1][:])
         w_scale = tile([P, E * PASSES * N], U8, "w_scale")
 
-        far_scale_rows = tile([P, S], U8, "far_scale_rows")
+        far_scale_rows = in_region(V_OUT, [P, S], U8, "far_scale_rows", S)
         nc.vector.tensor_copy(far_scale_rows[:], far_scale_table[:].indirect(far_list[:]))
         for s in range(PASSES):
             for q in range(QUADRANTS):
@@ -161,7 +169,7 @@ def tile_moe_loc_lin_relu_kernel(
         nc.sync.dma_start(gate_pair[:].rearrange("p (r t) -> p r t", r=2), gate.rearrange("r p t -> p r t"))
         gates = [gate_pair[:, r * T : (r + 1) * T] for r in range(2)]
 
-        halves = [tile([P, 2 * S], U32, "halves%d" % s) for s in range(PASSES)]
+        halves = [in_region((V_OUT, S_OUT)[s], [P, 2 * S], U32, "halves%d" % s, 8 * S) for s in range(PASSES)]
 
         def slot_words(s, a, b):
             return halves[s][:].rearrange("p (u j) -> p j u", u=2)[:, a:b, :]
@@ -184,7 +192,7 @@ def tile_moe_loc_lin_relu_kernel(
             window = far_table[:, at : at + (Q if a else WIDE)]
             nc.vector.tensor_copy(dst, window.bitcast(U32).indirect(entries(far_list, a, b)))
 
-        far_words0 = tile([P, S], U32, "far_words0")
+        far_words0 = in_region(V_OUT, [P, S], U32, "far_words0", 4 * S)
         gather_far_words(far_words0[:], 0, 0, S)
         gather_pair(0, 0, S, WIDE)
         gather_pair(1, 0, CHUNK, T)

@@ -1,7 +1,6 @@
 from contextlib import ExitStack
 
 import concourse.mybir as mybir
-from concourse.masks import make_identity
 
 K, T, Q, E, C, N = 1024, 768, 1024, 12, 128, 128
 S = E * C
@@ -25,13 +24,11 @@ QUADRANTS = 4
 LIST_ROWS = 16
 WIDE = 2048
 CHUNK = 512
-OWN = ((0, 512), (512, 1024), (1024, 1280), (1280, S))
-FAR_CUT = 896
+CHUNKS = S // CHUNK
+OWN = ((0, 512), (512, 768), (768, 1024), (1024, 1280), (1280, S))
+FAR_CUT = 1024
 SCALE_ROWS = P - PASSES * 16
-WOVEN_BYTES = PASSES * PACK * CHUNK * 2
 TOKEN_PARTS = ((0, T // 2), (T // 2, T))
-V_IN, V_OUT, SHARED, S_IN, S_OUT = 0, 28672, 65536, 131072, 147456
-TURNED = 256
 SUM = 256
 
 
@@ -48,14 +45,11 @@ def tile_moe_loc_lin_relu_kernel(
             return sb.tile(shape, dtype, name=name, tag=after or name, align_bytes=64)
 
         def placed(shape, dtype, name, offset):
-            return heirs.tile(shape, dtype, name=name, offset=SHARED + offset, align_bytes=64)
+            return heirs.tile(shape, dtype, name=name, offset=offset, align_bytes=64)
 
-        used = {V_IN: 0, V_OUT: 0, S_IN: 0, S_OUT: 0}
-
-        def in_region(region, shape, dtype, name, size):
-            at = region + used[region]
-            used[region] = used[region] + size
-            return heirs.tile(shape, dtype, name=name, offset=at, align_bytes=64)
+        woven_bytes = 2 * PASSES * PACK * S
+        far_early_at = woven_bytes
+        halves0_at = far_early_at + 4 * FAR_CUT
 
         def entries(lst, a, b):
             return lst[:, a // LIST_ROWS : b // LIST_ROWS]
@@ -64,32 +58,32 @@ def tile_moe_loc_lin_relu_kernel(
         far_list = tile([P, S // LIST_ROWS], U16, "far_list")
         pos_list = [tile([P, T // LIST_ROWS], U16, "pos_list%d" % r) for r in range(2)]
 
-        far_scale_table = in_region(V_IN, [P, WIDE], U8, "far_scale_table", WIDE)
+        far_scale_table = tile([P, WIDE], U8, "far_scale_table")
         far_scale = tile([P, PASSES * S], U8, "far_scale")
         nc.vector.memset(far_scale_table[:SCALE_ROWS, :].bitcast(I32), 0)
         nc.vector.memset(far_scale_table[SCALE_ROWS:, Q:].bitcast(I32), 0)
-        far_table = in_region(V_IN, [P, Q + WIDE], I32, "far_table", 4 * (Q + WIDE))
+        far_table = tile([P, Q + WIDE], I32, "far_table")
         nc.vector.memset(far_table[:, PASSES * Q :], 0)
-        singles = in_region(S_IN, [P, 2 * T + WIDE], BF16, "singles", 2 * (2 * T + WIDE))
-        nc.gpsimd.memset(singles[:, 3 * T :].bitcast(I32), 0)
+        singles = tile([P, 3 * T + WIDE], BF16, "singles")
+        nc.gpsimd.memset(singles[:, PACK * T :].bitcast(I32), 0)
 
         xo_k = xo.rearrange("(s p u e) t -> s u p e t", s=PASSES, u=2, e=2)
-        pair_table = in_region(V_IN, [P, 4 * T], F32, "pair_table", 16 * T)
-        raw_pair1 = placed([P, 2 * T], F32, "raw_pair1", 5 * WOVEN_BYTES)
+        pair_table = tile([P, 4 * T], F32, "pair_table")
+        raw_pair1 = placed([P, 2 * T], F32, "raw_pair1", far_early_at - 4 * T)
+        raw_late = tile([P, 2 * T], F32, "raw_late")
+
+        def two_rows(rows, a, b):
+            return rows[:, 2 * a : 2 * b].rearrange("p (e t) -> p e t", e=2)
 
         def raw_pair(u, a, b):
-            rows = pair_table[:, 2 * T :] if u == 0 else raw_pair1[:]
-            return rows[:, 2 * a : 2 * b].rearrange("p (e t) -> p e t", e=2)
+            return two_rows(pair_table[:, 2 * T :] if u == 0 else raw_pair1[:], a, b)
 
         def pair_words(u, width):
             at = (1 - u) * T
             return pair_table[:, at : at + width]
 
         raw_first = [tile([P, T // 2], F32, "raw_first%d" % h)[:] for h in range(2)]
-        raw_single = [None] + [tile([P, T], F32, "raw_single%d" % d) for d in range(1, PACK)]
-
-        def load_single(d):
-            nc.sync.dma_start(raw_single[d][:], xo_k[1, d % 2, :, d // 2, :])
+        raw_second = tile([P, T], F32, "raw_second")
 
         def load_pair(u):
             for a, b in TOKEN_PARTS:
@@ -103,12 +97,12 @@ def tile_moe_loc_lin_relu_kernel(
         for h in range(2):
             nc.sync.dma_start(raw_first[h], xo_k[1, 0, :, 0, h * T // 2 : (h + 1) * T // 2])
         nc.sync.dma_start(own_list[:], offs)
-        load_single(1)
+        nc.sync.dma_start(raw_second[:], xo_k[1, 1, :, 0, :])
         load_far_words(0)
         load_pair(0)
-        load_single(2)
+        for a, b in TOKEN_PARTS:
+            nc.sync.dma_start(two_rows(raw_late[:], a, b), xo_k[1, :, :, 1, a:b].rearrange("u p t -> p u t"))
         load_pair(1)
-        load_single(3)
         load_far_words(1)
         w_scale_rows = tile([P, E * PASSES * N], U8, "w_scale_rows")
         nc.sync.dma_start(
@@ -116,24 +110,19 @@ def tile_moe_loc_lin_relu_kernel(
             w_scales.bitcast(I32).rearrange("e s b n -> b (e s) n"),
         )
 
-        last_single = placed([P, T], BF16, "last_single", 2 * WOVEN_BYTES)
-
-        def single(d, width=T):
-            if d == PACK - 1:
-                return last_single[:]
-            at = (PACK - 2 - d) * T
+        def single(u, e, width=T):
+            at = (u if e else PACK - 1 - u) * T
             return singles[:, at : at + width]
 
         def round_on_gpsimd(dst, src):
             nc.gpsimd.tensor_scalar(dst, src, 1.0, 0.0, ALU.mult, ALU.add)
 
-        nc.scalar.activation(single(0)[:, : T // 2], raw_first[0], ACT.Copy)
-        round_on_gpsimd(single(0)[:, T // 2 :], raw_first[1])
-
-        round_on_gpsimd(single(1), raw_single[1][:])
+        round_on_gpsimd(single(0, 0)[:, : T // 2], raw_first[0])
+        nc.scalar.activation(single(0, 0)[:, T // 2 :], raw_first[1], ACT.Copy)
+        round_on_gpsimd(single(1, 0), raw_second[:])
         w_scale = tile([P, E * PASSES * N], U8, "w_scale")
 
-        far_scale_rows = in_region(V_OUT, [P, S], U8, "far_scale_rows", S)
+        far_scale_rows = tile([P, S], U8, "far_scale_rows")
         nc.vector.tensor_copy(far_scale_rows[:], far_scale_table[:].indirect(far_list[:]))
         for s in range(PASSES):
             for q in range(QUADRANTS):
@@ -161,134 +150,134 @@ def tile_moe_loc_lin_relu_kernel(
                 dst = pair_words(u, T)[:, a:b].bitcast(BF16).rearrange("p (t e) -> p t e", e=2)
                 round_on_gpsimd(dst, raw_pair(u, a, b).rearrange("p e t -> p t e"))
 
-        for u in range(2):
-            round_pair(u)
-            round_on_gpsimd(single(u + 2), raw_single[u + 2][:])
+        round_pair(0)
+        for a, b in TOKEN_PARTS:
+            round_on_gpsimd(singles[:, : 2 * T].rearrange("p (v t) -> p v t", v=2)[:, :, a:b], two_rows(raw_late[:], a, b))
+        round_pair(1)
 
-        gate_pair = tile([P, 2 * T], F32, "gate_pair", "raw_single1")
+        gate_pair = tile([P, 2 * T], F32, "gate_pair", "raw_second")
         nc.sync.dma_start(gate_pair[:].rearrange("p (r t) -> p r t", r=2), gate.rearrange("r p t -> p r t"))
-        gates = [gate_pair[:, r * T : (r + 1) * T] for r in range(2)]
+        gates = gate_pair[:].rearrange("p (r t) -> p r t", r=2)
 
-        halves = [in_region((V_OUT, S_OUT)[s], [P, 2 * S], U32, "halves%d" % s, 8 * S) for s in range(PASSES)]
+        halves = [placed([P, 2 * S], U32, "halves0", halves0_at), tile([P, 2 * S], U32, "halves1")]
 
         def slot_words(s, a, b):
             return halves[s][:].rearrange("p (u j) -> p j u", u=2)[:, a:b, :]
 
-        def gather_single(d, a, b, width):
-            at = (d % 2) * S
-            dst = halves[1][:, at + a : at + b].bitcast(BF16).rearrange("p (j e) -> p e j", e=2)
-            nc.scalar.activation(dst[:, d // 2, :], single(d, width).indirect(entries(own_list, a, b)), ACT.Copy)
+        def gather_single(u, e, a, b, window):
+            dst = halves[1][:, u * S + a : u * S + b].bitcast(BF16).rearrange("p (j e) -> p e j", e=2)
+            nc.scalar.activation(dst[:, e, :], window.indirect(entries(own_list, a, b)), ACT.Copy)
 
         def gather_pair(u, a, b, width):
             nc.vector.tensor_copy(slot_words(0, a, b)[:, :, u], pair_words(u, width).bitcast(U32).indirect(entries(own_list, a, b)))
 
-        for d in range(PACK - 1):
-            gather_single(d, 0, S, WIDE)
-        for c in range(S // CHUNK):
-            gather_single(PACK - 1, c * CHUNK, (c + 1) * CHUNK, T)
+        for u in range(2):
+            gather_single(u, 0, 0, S, single(u, 0, WIDE))
+        for a, b, width in ((0, CHUNK, T), (CHUNK, S, WIDE)):
+            for u in range(2):
+                gather_single(u, 1, a, b, single(u, 1, width))
 
         def gather_far_words(dst, s, a, b):
             at = (1 - s) * Q
-            window = far_table[:, at : at + (Q if a else WIDE)]
+            window = far_table[:, at : at + (WIDE if b - a > CHUNK else Q)]
             nc.vector.tensor_copy(dst, window.bitcast(U32).indirect(entries(far_list, a, b)))
 
-        far_words0 = in_region(V_OUT, [P, S], U32, "far_words0", 4 * S)
+        far_words0 = tile([P, S], U32, "far_words0")
         gather_far_words(far_words0[:], 0, 0, S)
         gather_pair(0, 0, S, WIDE)
-        gather_pair(1, 0, CHUNK, T)
-        gather_pair(1, CHUNK, S, 2 * T)
-        far_early = placed([P, FAR_CUT], U32, "far_early", 5 * WOVEN_BYTES)
-        gather_far_words(far_early[:], 1, 0, FAR_CUT)
+        for a in (0, S // 2):
+            gather_pair(1, a, a + S // 2, 2 * T)
+        far_early = placed([P, FAR_CUT], U32, "far_early", far_early_at)
+        for lo in range(0, FAR_CUT, CHUNK):
+            gather_far_words(far_early[:, lo : lo + CHUNK], 1, lo, lo + CHUNK)
 
-        woven = [placed([P, PASSES * PACK * CHUNK], BF16, "woven%d" % c, c * WOVEN_BYTES) for c in range(S // CHUNK)]
+        woven = placed([P, PASSES * PACK * S], BF16, "woven", 0)
 
-        def woven_range(i):
-            a, b = OWN[i]
-            at = PASSES * PACK * (a % CHUNK)
-            return woven[a // CHUNK][:, at : at + PASSES * PACK * (b - a)]
+        def weave(copy, s, a, b):
+            dst = woven[:].bitcast(U32).rearrange("p (e s j u) -> p s e j u", s=PASSES, j=C, u=2)[:, s, a // C : b // C]
+            copy(dst, slot_words(s, a, b).rearrange("p (e j) u -> p e j u", j=C))
 
-        def weave(copy, s, i, lo=0, hi=None):
-            a, b = OWN[i]
-            hi = hi or b - a
-            dst = woven_range(i)[:, PACK * (s * (b - a) + lo) : PACK * (s * (b - a) + hi)].bitcast(U32).rearrange("p (j u) -> p j u", u=2)
-            copy(dst, slot_words(s, a + lo, a + hi))
+        for s, a, b in ((1, 0, CHUNK), (0, 0, S // 2), (0, S // 2, S)):
+            weave(nc.gpsimd.tensor_copy, s, a, b)
+        for a in (CHUNK, 2 * CHUNK):
+            weave(nc.scalar.copy, 1, a, a + CHUNK)
 
-        for s, i in ((0, 0), (1, 0), (0, 1)):
-            weave(nc.gpsimd.tensor_copy, s, i)
-        weave(nc.scalar.copy, 1, 1)
-        for i in (2, 3):
-            for s in (1, 0):
-                weave(nc.scalar.copy, s, i)
-
-        own_words = [tile([P, PASSES * (b - a)], U32, "own_words%d" % a) for a, b in OWN[:2]]
-        own_words += [placed([P, PASSES * (b - a)], U32, "own_words%d" % a, 4 * PASSES * (a % CHUNK)) for a, b in OWN[2:]]
+        own_words = [tile([P, PASSES * (b - a)], U32, "own_words%d" % a) for a, b in OWN]
         own_scale = [tile([P, PASSES * (b - a)], U8, "own_scale%d" % a) for a, b in OWN]
-        for i in range(len(OWN)):
-            nc.vector.quantize_mx(own_words[i][:].bitcast(FP8X4), own_scale[i][:], woven_range(i))
-        identity = placed([P, P], F32, "identity", 2 * WOVEN_BYTES)
-        make_identity(nc, identity[:])
-        far_late = placed([P, S - FAR_CUT], U32, "far_late", WOVEN_BYTES)
-        gather_far_words(far_late[:], 1, FAR_CUT, S)
+        for i, (a, b) in enumerate(OWN):
+            nc.vector.quantize_mx(own_words[i][:].bitcast(FP8X4), own_scale[i][:], woven[:, PASSES * PACK * a : PASSES * PACK * b])
+        far_late = placed([P, S - FAR_CUT], U32, "far_late", halves0_at)
+        late_ranges = [(lo, min(lo + CHUNK, S)) for lo in range(FAR_CUT, S, CHUNK)]
+        for lo, hi in late_ranges:
+            gather_far_words(far_late[:, lo - FAR_CUT : hi - FAR_CUT], 1, lo, hi)
 
-        def experts(a, b, bank, words, scale):
-            for j in range((b - a) // C):
-                slots = slice(j * C, (j + 1) * C)
-                for s in range(PASSES):
+        def experts(a, b, bank, words, scale, order=(0, 1)):
+            count = (b - a) // C
+            for s in order:
+                for j in range(count):
+                    slots = slice(j * C, (j + 1) * C)
                     i = (a // C + j) * PASSES + s
                     nc.tensor.matmul_mx(
                         bank[:, slots],
                         lhsT=w_code[i // E][:, i % E * 2 * N : (i % E + 1) * 2 * N].bitcast(FP4X4),
                         lhsT_scale=w_scale[:, i * N : (i + 1) * N],
-                        rhs=words[s][:, slots].bitcast(FP8X4),
-                        rhs_scale=scale[s][:, slots],
-                        start=(s == 0),
-                        stop=(s == PASSES - 1),
+                        rhs=words(s, j).bitcast(FP8X4),
+                        rhs_scale=scale(s, j),
+                        start=(s == order[0] and j == 0),
+                        stop=(s == order[-1] and j == count - 1),
                     )
 
-        def far_experts(a, b, words):
-            banks = []
-            for lo in range(a, b, CHUNK):
-                hi = min(lo + CHUNK, b)
-                bank = ps.tile([P, hi - lo], F32, name="far%d" % lo)
-                experts(lo, hi, bank, [far_words0[:, lo:hi], words[:, lo - a : hi - a]], [far_scale[:, lo:hi], far_scale[:, S + lo : S + hi]])
-                banks.append((lo, hi, bank))
-            return banks
+        def far_experts(lo, hi, words, tag, order):
+            bank = ps.tile([P, hi - lo], F32, name="far%d" % lo, tag=tag)
+            tables = (far_words0[:, lo:hi], words)
+            experts(
+                lo, hi, bank,
+                lambda s, j: tables[s][:, j * C : (j + 1) * C],
+                lambda s, j: far_scale[:, s * S + lo + j * C : s * S + lo + (j + 1) * C],
+                order,
+            )
+            return bank
 
-        far_banks = far_experts(0, FAR_CUT, far_early)
+        def far_out(lo, hi, bank, z):
+            nc.scalar.activation(z, bank, ACT.Relu)
+            nc.sync.dma_start(out[:, T + lo : T + hi], z)
+
+        for lo in range(0, FAR_CUT, CHUNK):
+            hi = min(lo + CHUNK, FAR_CUT)
+            far_out(lo, hi, far_experts(lo, hi, far_early[:, lo:hi], "far%d" % lo, (1, 0))[:], tile([P, hi - lo], F32, "z%d" % lo)[:])
         y = tile([P, S], F32, "y")
         for i, (a, b) in enumerate(OWN):
             bank = ps.tile([P, b - a], F32, name="own%d" % a)
-            cols = [slice(s * (b - a), (s + 1) * (b - a)) for s in range(PASSES)]
-            experts(a, b, bank, [own_words[i][:, col] for col in cols], [own_scale[i][:, col] for col in cols])
+            experts(
+                a, b, bank,
+                lambda s, j: own_words[i][:, (j * PASSES + s) * C : (j * PASSES + s + 1) * C],
+                lambda s, j: own_scale[i][:, (j * PASSES + s) * C : (j * PASSES + s + 1) * C],
+            )
             nc.scalar.activation(y[:, a:b], bank[:], ACT.Relu)
-        far_banks.extend(far_experts(FAR_CUT, S, far_late))
-        z = placed([P, S], F32, "z", 0)
-        for lo, hi, bank in far_banks:
-            nc.scalar.activation(z[:, lo:hi], bank[:], ACT.Relu)
-            nc.sync.dma_start(out[:, T + lo : T + hi], z[:, lo:hi])
+        late_bank = far_experts(FAR_CUT, S, far_late[:], "own%d" % OWN[-1][0], (0, 1))
 
-        def product(r, a, b):
-            part = tile([P, b - a], F32, "product%d_%d" % (r, a))
-            nc.vector.tensor_tensor(part[:], y[:].indirect(entries(pos_list[r], a, b)), gates[r][:, a:b], ALU.mult)
-            return part
+        def fetch(r, a, b):
+            got = tile([P, b - a], F32, "got%d_%d" % (r, a))
+            nc.scalar.activation(got[:], y[:].indirect(entries(pos_list[r], a, b)), ACT.Copy)
+            return got
 
-        early = [product(r, 0, TURNED) for r in range(2)]
-        first = product(0, TURNED, T)
-        second = [product(1, a, a + SUM) for a in range(TURNED, T, SUM)]
-        early_total = tile([P, TURNED], F32, "early_total")
-        turned = []
-        for i, a in enumerate(range(0, TURNED, P)):
-            turned_bank = ps.tile([P, P], F32, name="turned_bank%d" % a, tag="own%d" % OWN[i][0])
-            for r in range(2):
-                nc.tensor.matmul(turned_bank[:], early[r][:, a : a + P], identity[:], start=(r == 0), stop=(r == 1), is_transpose=True)
-            turned.append(tile([P, P], F32, "turned%d" % a))
-            nc.scalar.copy(turned[i][:], turned_bank[:])
-        for i, a in enumerate(range(0, TURNED, P)):
-            back_bank = ps.tile([P, P], F32, name="back_bank%d" % a, tag="own%d" % OWN[i + 2][0])
-            nc.tensor.transpose(back_bank[:], turned[i][:], identity[:])
-            nc.scalar.copy(early_total[:, a : a + P], back_bank[:])
-        nc.scalar.dma_start(out[:, :TURNED], early_total[:])
-        for part, a in zip(second, range(TURNED, T, SUM)):
-            total = tile([P, SUM], F32, "total%d" % a)
-            nc.vector.tensor_tensor(total[:], first[:, a - TURNED : a - TURNED + SUM], part[:], ALU.add)
-            nc.sync.dma_start(out[:, a : a + SUM], total[:])
+        def weigh(got, r, a, b):
+            weighed = tile([P, b - a], F32, "weighed%d_%d" % (r, a))
+            nc.vector.tensor_tensor(weighed[:], got[:], gates[:, r, a:b], ALU.mult)
+            return weighed
+
+        def add(first, second, a, b):
+            total = tile([P, b - a], F32, "total%d" % a)
+            nc.vector.tensor_tensor(total[:], first, second, ALU.add)
+            nc.sync.dma_start(out[:, a:b], total[:])
+
+        got = [fetch(1, 0, 2 * SUM), fetch(1, 2 * SUM, T)]
+        for lo in range(FAR_CUT, S, SUM):
+            far_out(lo, lo + SUM, late_bank[:, lo - FAR_CUT : lo - FAR_CUT + SUM], tile([P, SUM], F32, "z%d" % lo)[:])
+        first = tile([P, T], F32, "first")
+        nc.vector.tensor_tensor(first[:], y[:].indirect(pos_list[0][:]), gates[:, 0, :], ALU.mult)
+        second = weigh(got[0], 1, 0, 2 * SUM)
+        second_rest = weigh(got[1], 1, 2 * SUM, T)
+        add(first[:, :SUM], second[:, :SUM], 0, SUM)
+        add(first[:, SUM : 2 * SUM], second[:, SUM:], SUM, 2 * SUM)
+        add(first[:, 2 * SUM :], second_rest[:], 2 * SUM, T)

@@ -256,8 +256,8 @@ def tile_moe_loc_lin_relu_kernel(
             nc.scalar.activation(y[:, a:b], bank[:], ACT.Relu)
         late_bank = far_experts(FAR_CUT, S, far_late[:], "own%d" % OWN[-1][0], (0, 1))
 
-        def fetch(r, a, b):
-            got = tile([P, b - a], F32, "got%d_%d" % (r, a))
+        def fetch(r, a, b, got=None):
+            got = got if got is not None else tile([P, b - a], F32, "got%d_%d" % (r, a))
             nc.scalar.activation(got[:], y[:].indirect(entries(pos_list[r], a, b)), ACT.Copy)
             return got
 
@@ -271,13 +271,17 @@ def tile_moe_loc_lin_relu_kernel(
             nc.vector.tensor_tensor(total[:], first, second, ALU.add)
             nc.sync.dma_start(out[:, a:b], total[:])
 
-        got = [fetch(1, 0, 2 * SUM), fetch(1, 2 * SUM, T)]
-        for lo in range(FAR_CUT, S, SUM):
+        def late_out(lo):
             far_out(lo, lo + SUM, late_bank[:, lo - FAR_CUT : lo - FAR_CUT + SUM], tile([P, SUM], F32, "z%d" % lo)[:])
+
+        got = fetch(1, 0, 2 * SUM)
+        late_out(FAR_CUT)
+        got_rest = fetch(1, 2 * SUM, T, placed([P, T - 2 * SUM], F32, "got_rest", halves0_at))
+        late_out(FAR_CUT + SUM)
         first = tile([P, T], F32, "first")
         nc.vector.tensor_tensor(first[:], y[:].indirect(pos_list[0][:]), gates[:, 0, :], ALU.mult)
-        second = weigh(got[0], 1, 0, 2 * SUM)
-        second_rest = weigh(got[1], 1, 2 * SUM, T)
+        second = weigh(got, 1, 0, 2 * SUM)
         add(first[:, :SUM], second[:, :SUM], 0, SUM)
+        second_rest = weigh(got_rest, 1, 2 * SUM, T)
         add(first[:, SUM : 2 * SUM], second[:, SUM:], SUM, 2 * SUM)
         add(first[:, 2 * SUM :], second_rest[:], 2 * SUM, T)

@@ -93,7 +93,7 @@ def tile_moe_loc_lin_relu_kernel(
             nc.sync.dma_start(far_table[:, (1 - s) * Q : (2 - s) * Q], x_words[s].rearrange("p t d -> p (t d)").bitcast(I32))
 
         nc.sync.dma_start(far_list[:], offs2)
-        nc.scalar.dma_start(far_scale_table[SCALE_ROWS:, :Q].bitcast(I32), x_scales.bitcast(I32).rearrange("s b t -> (s b) t"))
+        nc.sync.dma_start(far_scale_table[SCALE_ROWS:, :Q].bitcast(I32), x_scales.bitcast(I32).rearrange("s b t -> (s b) t"))
         for h in range(2):
             nc.sync.dma_start(raw_first[h], xo_k[1, 0, :, 0, h * T // 2 : (h + 1) * T // 2])
         nc.sync.dma_start(own_list[:], offs)
@@ -282,6 +282,6 @@ def tile_moe_loc_lin_relu_kernel(
         nc.vector.tensor_tensor(first[:], y[:].indirect(pos_list[0][:]), gates[:, 0, :], ALU.mult)
         second = weigh(got, 1, 0, 2 * SUM)
         add(first[:, :SUM], second[:, :SUM], 0, SUM)
-        second_rest = weigh(got_rest, 1, 2 * SUM, T)
         add(first[:, SUM : 2 * SUM], second[:, SUM:], SUM, 2 * SUM)
+        second_rest = weigh(got_rest, 1, 2 * SUM, T)
         add(first[:, 2 * SUM :], second_rest[:], 2 * SUM, T)

@@ -97,8 +97,9 @@ def tile_moe_loc_lin_relu_kernel(
         for h in range(2):
             nc.sync.dma_start(raw_first[h], xo_k[1, 0, :, 0, h * T // 2 : (h + 1) * T // 2])
         nc.sync.dma_start(own_list[:], offs)
-        nc.sync.dma_start(raw_second[:], xo_k[1, 1, :, 0, :])
+        nc.sync.dma_start(raw_second[:, : T // 2], xo_k[1, 1, :, 0, : T // 2])
         load_far_words(0)
+        nc.sync.dma_start(raw_second[:, T // 2 :], xo_k[1, 1, :, 0, T // 2 :])
         load_pair(0)
         for a, b in TOKEN_PARTS:
             nc.sync.dma_start(two_rows(raw_late[:], a, b), xo_k[1, :, :, 1, a:b].rearrange("u p t -> p u t"))
@@ -119,7 +120,8 @@ def tile_moe_loc_lin_relu_kernel(
 
         round_on_gpsimd(single(0, 0)[:, : T // 2], raw_first[0])
         nc.scalar.activation(single(0, 0)[:, T // 2 :], raw_first[1], ACT.Copy)
-        round_on_gpsimd(single(1, 0), raw_second[:])
+        for a, b in TOKEN_PARTS:
+            round_on_gpsimd(single(1, 0)[:, a:b], raw_second[:, a:b])
         w_scale = tile([P, E * PASSES * N], U8, "w_scale")
 
         far_scale_rows = tile([P, S], U8, "far_scale_rows")

@@ -30,6 +30,7 @@ FAR_CUT = 1024
 SCALE_ROWS = P - PASSES * 16
 TOKEN_PARTS = ((0, T // 2), (T // 2, T))
 SUM = 256
+IN_FLIGHT = 8
 
 
 def tile_moe_loc_lin_relu_kernel(
@@ -97,19 +98,18 @@ def tile_moe_loc_lin_relu_kernel(
         for h in range(2):
             nc.sync.dma_start(raw_first[h], xo_k[1, 0, :, 0, h * T // 2 : (h + 1) * T // 2])
         nc.sync.dma_start(own_list[:], offs)
-        nc.sync.dma_start(raw_second[:, : T // 2], xo_k[1, 1, :, 0, : T // 2])
+        nc.sync.dma_start(raw_second[:], xo_k[1, 1, :, 0, :])
         load_far_words(0)
-        nc.sync.dma_start(raw_second[:, T // 2 :], xo_k[1, 1, :, 0, T // 2 :])
         load_pair(0)
         for a, b in TOKEN_PARTS:
             nc.sync.dma_start(two_rows(raw_late[:], a, b), xo_k[1, :, :, 1, a:b].rearrange("u p t -> p u t"))
         load_pair(1)
-        load_far_words(1)
         w_scale_rows = tile([P, E * PASSES * N], U8, "w_scale_rows")
         nc.sync.dma_start(
             w_scale_rows[:16, :].bitcast(I32).rearrange("b (g n) -> b g n", n=N // 4),
             w_scales.bitcast(I32).rearrange("e s b n -> b (e s) n"),
         )
+        load_far_words(1)
 
         def single(u, e, width=T):
             at = (u if e else PACK - 1 - u) * T
@@ -120,30 +120,25 @@ def tile_moe_loc_lin_relu_kernel(
 
         round_on_gpsimd(single(0, 0)[:, : T // 2], raw_first[0])
         nc.scalar.activation(single(0, 0)[:, T // 2 :], raw_first[1], ACT.Copy)
-        for a, b in TOKEN_PARTS:
-            round_on_gpsimd(single(1, 0)[:, a:b], raw_second[:, a:b])
+        round_on_gpsimd(single(1, 0), raw_second[:])
         w_scale = tile([P, E * PASSES * N], U8, "w_scale")
+
 
         far_scale_rows = tile([P, S], U8, "far_scale_rows")
         nc.vector.tensor_copy(far_scale_rows[:], far_scale_table[:].indirect(far_list[:]))
-        for s in range(PASSES):
-            for q in range(QUADRANTS):
-                row = SCALE_ROWS + 16 * s + 4 * q
+        moves = [
+            (far_scale[32 * q : 32 * q + 4, s * S : (s + 1) * S], far_scale_rows[SCALE_ROWS + 16 * s + 4 * q : SCALE_ROWS + 16 * s + 4 * q + 4, :])
+            for s in range(PASSES)
+            for q in range(QUADRANTS)
+        ]
+        moves += [(w_scale[32 * q : 32 * q + 4, :], w_scale_rows[4 * q : 4 * q + 4, :]) for q in range(QUADRANTS)]
+        w_code = tile([P, E * PASSES * N * 2], U8, "w_code")
+        for i, (dst, src) in enumerate(moves):
+            if i == len(moves) - (IN_FLIGHT - 1):
                 nc.sync.dma_start(
-                    far_scale[32 * q : 32 * q + 4, s * S : (s + 1) * S].bitcast(I32), far_scale_rows[row : row + 4, :].bitcast(I32)
+                    w_code[:].bitcast(I32).rearrange("p (g n) -> p g n", n=N // 2), w_words.bitcast(I32).rearrange("e s p n -> p (e s) n")
                 )
-        w_code = [tile([P, E * N * 2], U8, "w_code%d" % h) for h in range(2)]
-
-        def load_w_code(h):
-            nc.sync.dma_start(
-                w_code[h][:].bitcast(I32).rearrange("p (g n) -> p g n", n=N // 2),
-                w_words[h * E // 2 : (h + 1) * E // 2].bitcast(I32).rearrange("e s p n -> p (e s) n"),
-            )
-
-        load_w_code(0)
-        for q in range(QUADRANTS):
-            nc.sync.dma_start(w_scale[32 * q : 32 * q + 4, :].bitcast(I32), w_scale_rows[4 * q : 4 * q + 4, :].bitcast(I32))
-        load_w_code(1)
+            nc.sync.dma_start(dst.bitcast(I32), src.bitcast(I32))
         nc.sync.dma_start(pos_list[0][:], pos1)
         nc.sync.dma_start(pos_list[1][:], pos2)
 
@@ -221,7 +216,7 @@ def tile_moe_loc_lin_relu_kernel(
                     i = (a // C + j) * PASSES + s
                     nc.tensor.matmul_mx(
                         bank[:, slots],
-                        lhsT=w_code[i // E][:, i % E * 2 * N : (i % E + 1) * 2 * N].bitcast(FP4X4),
+                        lhsT=w_code[:, i * 2 * N : (i + 1) * 2 * N].bitcast(FP4X4),
                         lhsT_scale=w_scale[:, i * N : (i + 1) * N],
                         rhs=words(s, j).bitcast(FP8X4),
                         rhs_scale=scale(s, j),

@@ -260,7 +260,7 @@ def tile_moe_loc_lin_relu_kernel(
 
         def weigh(got, r, a, b):
             weighed = tile([P, b - a], F32, "weighed%d_%d" % (r, a))
-            nc.vector.tensor_tensor(weighed[:], got[:], gates[:, r, a:b], ALU.mult)
+            nc.vector.tensor_tensor(weighed[:], got, gates[:, r, a:b], ALU.mult)
             return weighed
 
         def add(first, second, a, b):
@@ -277,8 +277,8 @@ def tile_moe_loc_lin_relu_kernel(
         late_out(FAR_CUT + SUM)
         first = tile([P, T], F32, "first")
         nc.vector.tensor_tensor(first[:], y[:].indirect(pos_list[0][:]), gates[:, 0, :], ALU.mult)
-        second = weigh(got, 1, 0, 2 * SUM)
-        add(first[:, :SUM], second[:, :SUM], 0, SUM)
-        add(first[:, SUM : 2 * SUM], second[:, SUM:], SUM, 2 * SUM)
-        second_rest = weigh(got_rest, 1, 2 * SUM, T)
+        second = [weigh(got[:, a : a + SUM], 1, a, a + SUM) for a in (0, SUM)]
+        add(first[:, :SUM], second[0][:], 0, SUM)
+        second_rest = weigh(got_rest[:], 1, 2 * SUM, T)
+        add(first[:, SUM : 2 * SUM], second[1][:], SUM, 2 * SUM)
         add(first[:, 2 * SUM :], second_rest[:], 2 * SUM, T)

@@ -98,11 +98,12 @@ def tile_moe_loc_lin_relu_kernel(
         for h in range(2):
             nc.sync.dma_start(raw_first[h], xo_k[1, 0, :, 0, h * T // 2 : (h + 1) * T // 2])
         nc.sync.dma_start(own_list[:], offs)
-        nc.sync.dma_start(raw_second[:], xo_k[1, 1, :, 0, :])
+        nc.sync.dma_start(raw_second[:, : T // 2], xo_k[1, 1, :, 0, : T // 2])
         load_far_words(0)
+        nc.sync.dma_start(raw_second[:, T // 2 :], xo_k[1, 1, :, 0, T // 2 :])
         load_pair(0)
-        for a, b in TOKEN_PARTS:
-            nc.sync.dma_start(two_rows(raw_late[:], a, b), xo_k[1, :, :, 1, a:b].rearrange("u p t -> p u t"))
+        for u in range(2):
+            nc.sync.dma_start(raw_late[:, u * T : (u + 1) * T], xo_k[1, u, :, 1, :])
         load_pair(1)
         w_scale_rows = tile([P, E * PASSES * N], U8, "w_scale_rows")
         nc.sync.dma_start(
@@ -120,7 +121,8 @@ def tile_moe_loc_lin_relu_kernel(
 
         round_on_gpsimd(single(0, 0)[:, : T // 2], raw_first[0])
         nc.scalar.activation(single(0, 0)[:, T // 2 :], raw_first[1], ACT.Copy)
-        round_on_gpsimd(single(1, 0), raw_second[:])
+        for a, b in TOKEN_PARTS:
+            round_on_gpsimd(single(1, 0)[:, a:b], raw_second[:, a:b])
         w_scale = tile([P, E * PASSES * N], U8, "w_scale")
 
 
@@ -148,8 +150,8 @@ def tile_moe_loc_lin_relu_kernel(
                 round_on_gpsimd(dst, raw_pair(u, a, b).rearrange("p e t -> p t e"))
 
         round_pair(0)
-        for a, b in TOKEN_PARTS:
-            round_on_gpsimd(singles[:, : 2 * T].rearrange("p (v t) -> p v t", v=2)[:, :, a:b], two_rows(raw_late[:], a, b))
+        for u in range(2):
+            round_on_gpsimd(single(u, 1), raw_late[:, u * T : (u + 1) * T])
         round_pair(1)
 
         gate_pair = tile([P, 2 * T], F32, "gate_pair", "raw_second")
@@ -260,7 +262,7 @@ def tile_moe_loc_lin_relu_kernel(
 
         def weigh(got, r, a, b):
             weighed = tile([P, b - a], F32, "weighed%d_%d" % (r, a))
-            nc.vector.tensor_tensor(weighed[:], got, gates[:, r, a:b], ALU.mult)
+            nc.vector.tensor_tensor(weighed[:], got[:], gates[:, r, a:b], ALU.mult)
             return weighed
 
         def add(first, second, a, b):
@@ -277,8 +279,8 @@ def tile_moe_loc_lin_relu_kernel(
         late_out(FAR_CUT + SUM)
         first = tile([P, T], F32, "first")
         nc.vector.tensor_tensor(first[:], y[:].indirect(pos_list[0][:]), gates[:, 0, :], ALU.mult)
-        second = [weigh(got[:, a : a + SUM], 1, a, a + SUM) for a in (0, SUM)]
-        add(first[:, :SUM], second[0][:], 0, SUM)
-        second_rest = weigh(got_rest[:], 1, 2 * SUM, T)
-        add(first[:, SUM : 2 * SUM], second[1][:], SUM, 2 * SUM)
+        second = weigh(got, 1, 0, 2 * SUM)
+        add(first[:, :SUM], second[:, :SUM], 0, SUM)
+        add(first[:, SUM : 2 * SUM], second[:, SUM:], SUM, 2 * SUM)
+        second_rest = weigh(got_rest, 1, 2 * SUM, T)
         add(first[:, 2 * SUM :], second_rest[:], 2 * SUM, T)

@@ -26,9 +26,12 @@ WIDE = 2048
 CHUNK = 512
 CHUNKS = S // CHUNK
 OWN = ((0, 512), (512, 768), (768, 1024), (1024, 1280), (1280, S))
+OWN_BANKS = ((0, 512), (512, 1024), (1024, 1280), (1280, S))
 FAR_CUT = 1024
 SCALE_ROWS = P - PASSES * 16
 TOKEN_PARTS = ((0, T // 2), (T // 2, T))
+FIRST_CUT = 448
+FIRST_PARTS = ((0, FIRST_CUT), (FIRST_CUT, T))
 SUM = 256
 IN_FLIGHT = 8
 
@@ -83,7 +86,7 @@ def tile_moe_loc_lin_relu_kernel(
             at = (1 - u) * T
             return pair_table[:, at : at + width]
 
-        raw_first = [tile([P, T // 2], F32, "raw_first%d" % h)[:] for h in range(2)]
+        raw_first = [tile([P, b - a], F32, "raw_first%d" % a)[:] for a, b in FIRST_PARTS]
         raw_second = tile([P, T], F32, "raw_second")
 
         def load_pair(u):
@@ -95,8 +98,8 @@ def tile_moe_loc_lin_relu_kernel(
 
         nc.sync.dma_start(far_list[:], offs2)
         nc.sync.dma_start(far_scale_table[SCALE_ROWS:, :Q].bitcast(I32), x_scales.bitcast(I32).rearrange("s b t -> (s b) t"))
-        for h in range(2):
-            nc.sync.dma_start(raw_first[h], xo_k[1, 0, :, 0, h * T // 2 : (h + 1) * T // 2])
+        for h, (a, b) in enumerate(FIRST_PARTS):
+            nc.sync.dma_start(raw_first[h], xo_k[1, 0, :, 0, a:b])
         nc.sync.dma_start(own_list[:], offs)
         nc.sync.dma_start(raw_second[:, : T // 2], xo_k[1, 1, :, 0, : T // 2])
         load_far_words(0)
@@ -119,8 +122,8 @@ def tile_moe_loc_lin_relu_kernel(
         def round_on_gpsimd(dst, src):
             nc.gpsimd.tensor_scalar(dst, src, 1.0, 0.0, ALU.mult, ALU.add)
 
-        round_on_gpsimd(single(0, 0)[:, : T // 2], raw_first[0])
-        nc.scalar.activation(single(0, 0)[:, T // 2 :], raw_first[1], ACT.Copy)
+        round_on_gpsimd(single(0, 0)[:, :FIRST_CUT], raw_first[0])
+        nc.scalar.activation(single(0, 0)[:, FIRST_CUT:], raw_first[1], ACT.Copy)
         for a, b in TOKEN_PARTS:
             round_on_gpsimd(single(1, 0)[:, a:b], raw_second[:, a:b])
         w_scale = tile([P, E * PASSES * N], U8, "w_scale")
@@ -210,7 +213,7 @@ def tile_moe_loc_lin_relu_kernel(
         for lo, hi in late_ranges:
             gather_far_words(far_late[:, lo - FAR_CUT : hi - FAR_CUT], 1, lo, hi)
 
-        def experts(a, b, bank, words, scale, order=(0, 1)):
+        def experts(a, b, bank, words, scale, order=(0, 1), opens=True, closes=True):
             count = (b - a) // C
             for s in order:
                 for j in range(count):
@@ -222,8 +225,8 @@ def tile_moe_loc_lin_relu_kernel(
                         lhsT_scale=w_scale[:, i * N : (i + 1) * N],
                         rhs=words(s, j).bitcast(FP8X4),
                         rhs_scale=scale(s, j),
-                        start=(s == order[0] and j == 0),
-                        stop=(s == order[-1] and j == count - 1),
+                        start=(opens and s == order[0] and j == 0),
+                        stop=(closes and s == order[-1] and j == count - 1),
                     )
 
         def far_experts(lo, hi, words, tag, order):
@@ -245,14 +248,18 @@ def tile_moe_loc_lin_relu_kernel(
             hi = min(lo + CHUNK, FAR_CUT)
             far_out(lo, hi, far_experts(lo, hi, far_early[:, lo:hi], "far%d" % lo, (1, 0))[:], tile([P, hi - lo], F32, "z%d" % lo)[:])
         y = tile([P, S], F32, "y")
-        for i, (a, b) in enumerate(OWN):
-            bank = ps.tile([P, b - a], F32, name="own%d" % a)
-            experts(
-                a, b, bank,
-                lambda s, j: own_words[i][:, (j * PASSES + s) * C : (j * PASSES + s + 1) * C],
-                lambda s, j: own_scale[i][:, (j * PASSES + s) * C : (j * PASSES + s + 1) * C],
-            )
-            nc.scalar.activation(y[:, a:b], bank[:], ACT.Relu)
+        for lo, hi in OWN_BANKS:
+            bank = ps.tile([P, hi - lo], F32, name="own%d" % lo)
+            for i, (a, b) in enumerate(OWN):
+                if lo <= a < hi:
+                    experts(
+                        a, b, bank[:, a - lo : b - lo],
+                        lambda s, j: own_words[i][:, (j * PASSES + s) * C : (j * PASSES + s + 1) * C],
+                        lambda s, j: own_scale[i][:, (j * PASSES + s) * C : (j * PASSES + s + 1) * C],
+                        opens=(a == lo),
+                        closes=(b == hi),
+                    )
+            nc.scalar.activation(y[:, lo:hi], bank[:], ACT.Relu)
         late_bank = far_experts(FAR_CUT, S, far_late[:], "own%d" % OWN[-1][0], (0, 1))
 
         def fetch(r, a, b, got=None):

@@ -32,7 +32,7 @@ SCALE_ROWS = P - PASSES * 16
 TOKEN_PARTS = ((0, T // 2), (T // 2, T))
 FIRST_CUT = 448
 FIRST_PARTS = ((0, FIRST_CUT), (FIRST_CUT, T))
-SUM = 256
+SUMS = ((0, 384), (384, 576), (576, T))
 IN_FLIGHT = 8
 
 
@@ -260,7 +260,7 @@ def tile_moe_loc_lin_relu_kernel(
                         closes=(b == hi),
                     )
             nc.scalar.activation(y[:, lo:hi], bank[:], ACT.Relu)
-        late_bank = far_experts(FAR_CUT, S, far_late[:], "own%d" % OWN[-1][0], (0, 1))
+        late_bank = far_experts(FAR_CUT, S, far_late[:], "own%d" % OWN[-2][0], (0, 1))
 
         def fetch(r, a, b, got=None):
             got = got if got is not None else tile([P, b - a], F32, "got%d_%d" % (r, a))
@@ -269,7 +269,7 @@ def tile_moe_loc_lin_relu_kernel(
 
         def weigh(got, r, a, b):
             weighed = tile([P, b - a], F32, "weighed%d_%d" % (r, a))
-            nc.vector.tensor_tensor(weighed[:], got[:], gates[:, r, a:b], ALU.mult)
+            nc.vector.tensor_tensor(weighed[:], got, gates[:, r, a:b], ALU.mult)
             return weighed
 
         def add(first, second, a, b):
@@ -277,17 +277,14 @@ def tile_moe_loc_lin_relu_kernel(
             nc.vector.tensor_tensor(total[:], first, second, ALU.add)
             nc.sync.dma_start(out[:, a:b], total[:])
 
-        def late_out(lo):
-            far_out(lo, lo + SUM, late_bank[:, lo - FAR_CUT : lo - FAR_CUT + SUM], tile([P, SUM], F32, "z%d" % lo)[:])
-
-        got = fetch(1, 0, 2 * SUM)
-        late_out(FAR_CUT)
-        got_rest = fetch(1, 2 * SUM, T, placed([P, T - 2 * SUM], F32, "got_rest", halves0_at))
-        late_out(FAR_CUT + SUM)
+        cut = SUMS[-1][0]
+        got = fetch(1, 0, cut)
+        far_out(FAR_CUT, S, late_bank[:], tile([P, S - FAR_CUT], F32, "z_late")[:])
+        got_rest = fetch(1, cut, T, placed([P, T - cut], F32, "got_rest", halves0_at))
         first = tile([P, T], F32, "first")
         nc.vector.tensor_tensor(first[:], y[:].indirect(pos_list[0][:]), gates[:, 0, :], ALU.mult)
-        second = weigh(got, 1, 0, 2 * SUM)
-        add(first[:, :SUM], second[:, :SUM], 0, SUM)
-        add(first[:, SUM : 2 * SUM], second[:, SUM:], SUM, 2 * SUM)
-        second_rest = weigh(got_rest, 1, 2 * SUM, T)
-        add(first[:, 2 * SUM :], second_rest[:], 2 * SUM, T)
+        second = [weigh(got[:, a:b], 1, a, b) for a, b in SUMS[:-1]]
+        add(first[:, : SUMS[0][1]], second[0][:], *SUMS[0])
+        second.append(weigh(got_rest[:], 1, cut, T))
+        for (a, b), weighed in zip(SUMS[1:], second[1:]):
+            add(first[:, a:b], weighed[:], a, b)

@@ -32,7 +32,7 @@ SCALE_ROWS = P - PASSES * 16
 TOKEN_PARTS = ((0, T // 2), (T // 2, T))
 FIRST_CUT = 448
 FIRST_PARTS = ((0, FIRST_CUT), (FIRST_CUT, T))
-SUMS = ((0, 384), (384, 576), (576, T))
+SUMS = ((0, 320), (320, 576), (576, T))
 IN_FLIGHT = 8
 
 

from contextlib import ExitStack

import concourse.mybir as mybir

K, T, Q, E, C, N = 1024, 768, 1024, 12, 128, 128
S = E * C
FLOPS = 2 * K * N * 2 * S

F32 = mybir.dt.float32
BF16 = mybir.dt.bfloat16
I32 = mybir.dt.int32
U32 = mybir.dt.uint32
U16 = mybir.dt.uint16
U8 = mybir.dt.uint8
FP8X4 = mybir.dt.float8_e4m3fn_x4
FP4X4 = mybir.dt.float4_e2m1fn_x4
ACT = mybir.ActivationFunctionType
ALU = mybir.AluOpType

P = 128
PASSES = K // 512
PACK = 4
QUADRANTS = 4
LIST_ROWS = 16
WIDE = 2048
CHUNK = 512
CHUNKS = S // CHUNK
OWN = ((0, 512), (512, 768), (768, 1024), (1024, 1280), (1280, S))
OWN_BANKS = ((0, 512), (512, 1024), (1024, 1280), (1280, S))
FAR_CUT = 1024
SCALE_ROWS = P - PASSES * 16
TOKEN_PARTS = ((0, T // 2), (T // 2, T))
FIRST_CUT = 448
FIRST_PARTS = ((0, FIRST_CUT), (FIRST_CUT, T))
SUMS = ((0, 320), (320, 576), (576, T))
IN_FLIGHT = 8


def tile_moe_loc_lin_relu_kernel(
    tc, x_words, x_scales, xo, w_words, w_scales, gate, offs, pos1, pos2, offs2, out
):
    nc = tc.nc
    with ExitStack() as ctx:
        heirs = ctx.enter_context(tc.tile_pool(name="heirs", bufs=1))
        sb = ctx.enter_context(tc.tile_pool(name="sb", bufs=1))
        ps = ctx.enter_context(tc.psum_pool(name="ps", bufs=1))

        def tile(shape, dtype, name, after=None):
            return sb.tile(shape, dtype, name=name, tag=after or name, align_bytes=64)

        def placed(shape, dtype, name, offset):
            return heirs.tile(shape, dtype, name=name, offset=offset, align_bytes=64)

        woven_bytes = 2 * PASSES * PACK * S
        far_early_at = woven_bytes
        halves0_at = far_early_at + 4 * FAR_CUT

        def entries(lst, a, b):
            return lst[:, a // LIST_ROWS : b // LIST_ROWS]

        own_list = tile([P, S // LIST_ROWS], U16, "own_list")
        far_list = tile([P, S // LIST_ROWS], U16, "far_list")
        pos_list = [tile([P, T // LIST_ROWS], U16, "pos_list%d" % r) for r in range(2)]

        far_scale_table = tile([P, WIDE], U8, "far_scale_table")
        far_scale = tile([P, PASSES * S], U8, "far_scale")
        nc.vector.memset(far_scale_table[:SCALE_ROWS, :].bitcast(I32), 0)
        nc.vector.memset(far_scale_table[SCALE_ROWS:, Q:].bitcast(I32), 0)
        far_table = tile([P, Q + WIDE], I32, "far_table")
        nc.vector.memset(far_table[:, PASSES * Q :], 0)
        singles = tile([P, 3 * T + WIDE], BF16, "singles")
        nc.gpsimd.memset(singles[:, PACK * T :].bitcast(I32), 0)

        xo_k = xo.rearrange("(s p u e) t -> s u p e t", s=PASSES, u=2, e=2)
        pair_table = tile([P, 4 * T], F32, "pair_table")
        raw_pair1 = placed([P, 2 * T], F32, "raw_pair1", far_early_at - 4 * T)
        raw_late = tile([P, 2 * T], F32, "raw_late")

        def two_rows(rows, a, b):
            return rows[:, 2 * a : 2 * b].rearrange("p (e t) -> p e t", e=2)

        def raw_pair(u, a, b):
            return two_rows(pair_table[:, 2 * T :] if u == 0 else raw_pair1[:], a, b)

        def pair_words(u, width):
            at = (1 - u) * T
            return pair_table[:, at : at + width]

        raw_first = [tile([P, b - a], F32, "raw_first%d" % a)[:] for a, b in FIRST_PARTS]
        raw_second = tile([P, T], F32, "raw_second")

        def load_pair(u):
            for a, b in TOKEN_PARTS:
                nc.sync.dma_start(raw_pair(u, a, b), xo_k[0, u, :, :, a:b])

        def load_far_words(s):
            nc.sync.dma_start(far_table[:, (1 - s) * Q : (2 - s) * Q], x_words[s].rearrange("p t d -> p (t d)").bitcast(I32))

        nc.sync.dma_start(far_list[:], offs2)
        nc.sync.dma_start(far_scale_table[SCALE_ROWS:, :Q].bitcast(I32), x_scales.bitcast(I32).rearrange("s b t -> (s b) t"))
        for h, (a, b) in enumerate(FIRST_PARTS):
            nc.sync.dma_start(raw_first[h], xo_k[1, 0, :, 0, a:b])
        nc.sync.dma_start(own_list[:], offs)
        nc.sync.dma_start(raw_second[:, : T // 2], xo_k[1, 1, :, 0, : T // 2])
        load_far_words(0)
        nc.sync.dma_start(raw_second[:, T // 2 :], xo_k[1, 1, :, 0, T // 2 :])
        load_pair(0)
        for u in range(2):
            nc.sync.dma_start(raw_late[:, u * T : (u + 1) * T], xo_k[1, u, :, 1, :])
        load_pair(1)
        w_scale_rows = tile([P, E * PASSES * N], U8, "w_scale_rows")
        nc.sync.dma_start(
            w_scale_rows[:16, :].bitcast(I32).rearrange("b (g n) -> b g n", n=N // 4),
            w_scales.bitcast(I32).rearrange("e s b n -> b (e s) n"),
        )
        load_far_words(1)

        def single(u, e, width=T):
            at = (u if e else PACK - 1 - u) * T
            return singles[:, at : at + width]

        def round_on_gpsimd(dst, src):
            nc.gpsimd.tensor_scalar(dst, src, 1.0, 0.0, ALU.mult, ALU.add)

        round_on_gpsimd(single(0, 0)[:, :FIRST_CUT], raw_first[0])
        nc.scalar.activation(single(0, 0)[:, FIRST_CUT:], raw_first[1], ACT.Copy)
        for a, b in TOKEN_PARTS:
            round_on_gpsimd(single(1, 0)[:, a:b], raw_second[:, a:b])
        w_scale = tile([P, E * PASSES * N], U8, "w_scale")


        far_scale_rows = tile([P, S], U8, "far_scale_rows")
        nc.vector.tensor_copy(far_scale_rows[:], far_scale_table[:].indirect(far_list[:]))
        moves = [
            (far_scale[32 * q : 32 * q + 4, s * S : (s + 1) * S], far_scale_rows[SCALE_ROWS + 16 * s + 4 * q : SCALE_ROWS + 16 * s + 4 * q + 4, :])
            for s in range(PASSES)
            for q in range(QUADRANTS)
        ]
        moves += [(w_scale[32 * q : 32 * q + 4, :], w_scale_rows[4 * q : 4 * q + 4, :]) for q in range(QUADRANTS)]
        w_code = tile([P, E * PASSES * N * 2], U8, "w_code")
        for i, (dst, src) in enumerate(moves):
            if i == len(moves) - (IN_FLIGHT - 1):
                nc.sync.dma_start(
                    w_code[:].bitcast(I32).rearrange("p (g n) -> p g n", n=N // 2), w_words.bitcast(I32).rearrange("e s p n -> p (e s) n")
                )
            nc.sync.dma_start(dst.bitcast(I32), src.bitcast(I32))
        nc.sync.dma_start(pos_list[0][:], pos1)
        nc.sync.dma_start(pos_list[1][:], pos2)

        def round_pair(u):
            for a, b in TOKEN_PARTS:
                dst = pair_words(u, T)[:, a:b].bitcast(BF16).rearrange("p (t e) -> p t e", e=2)
                round_on_gpsimd(dst, raw_pair(u, a, b).rearrange("p e t -> p t e"))

        round_pair(0)
        for u in range(2):
            round_on_gpsimd(single(u, 1), raw_late[:, u * T : (u + 1) * T])
        round_pair(1)

        gate_pair = tile([P, 2 * T], F32, "gate_pair", "raw_second")
        nc.sync.dma_start(gate_pair[:].rearrange("p (r t) -> p r t", r=2), gate.rearrange("r p t -> p r t"))
        gates = gate_pair[:].rearrange("p (r t) -> p r t", r=2)

        halves = [placed([P, 2 * S], U32, "halves0", halves0_at), tile([P, 2 * S], U32, "halves1")]

        def slot_words(s, a, b):
            return halves[s][:].rearrange("p (u j) -> p j u", u=2)[:, a:b, :]

        def gather_single(u, e, a, b, window):
            dst = halves[1][:, u * S + a : u * S + b].bitcast(BF16).rearrange("p (j e) -> p e j", e=2)
            nc.scalar.activation(dst[:, e, :], window.indirect(entries(own_list, a, b)), ACT.Copy)

        def gather_pair(u, a, b, width):
            nc.vector.tensor_copy(slot_words(0, a, b)[:, :, u], pair_words(u, width).bitcast(U32).indirect(entries(own_list, a, b)))

        for u in range(2):
            gather_single(u, 0, 0, S, single(u, 0, WIDE))
        for a, b, width in ((0, CHUNK, T), (CHUNK, S, WIDE)):
            for u in range(2):
                gather_single(u, 1, a, b, single(u, 1, width))

        def gather_far_words(dst, s, a, b):
            at = (1 - s) * Q
            window = far_table[:, at : at + (WIDE if b - a > CHUNK else Q)]
            nc.vector.tensor_copy(dst, window.bitcast(U32).indirect(entries(far_list, a, b)))

        far_words0 = tile([P, S], U32, "far_words0")
        gather_far_words(far_words0[:], 0, 0, S)
        gather_pair(0, 0, S, WIDE)
        for a in (0, S // 2):
            gather_pair(1, a, a + S // 2, 2 * T)
        far_early = placed([P, FAR_CUT], U32, "far_early", far_early_at)
        for lo in range(0, FAR_CUT, CHUNK):
            gather_far_words(far_early[:, lo : lo + CHUNK], 1, lo, lo + CHUNK)

        woven = placed([P, PASSES * PACK * S], BF16, "woven", 0)

        def weave(copy, s, a, b):
            dst = woven[:].bitcast(U32).rearrange("p (e s j u) -> p s e j u", s=PASSES, j=C, u=2)[:, s, a // C : b // C]
            copy(dst, slot_words(s, a, b).rearrange("p (e j) u -> p e j u", j=C))

        for s, a, b in ((1, 0, CHUNK), (0, 0, S // 2), (0, S // 2, S)):
            weave(nc.gpsimd.tensor_copy, s, a, b)
        for a in (CHUNK, 2 * CHUNK):
            weave(nc.scalar.copy, 1, a, a + CHUNK)

        own_words = [tile([P, PASSES * (b - a)], U32, "own_words%d" % a) for a, b in OWN]
        own_scale = [tile([P, PASSES * (b - a)], U8, "own_scale%d" % a) for a, b in OWN]
        for i, (a, b) in enumerate(OWN):
            nc.vector.quantize_mx(own_words[i][:].bitcast(FP8X4), own_scale[i][:], woven[:, PASSES * PACK * a : PASSES * PACK * b])
        far_late = placed([P, S - FAR_CUT], U32, "far_late", halves0_at)
        late_ranges = [(lo, min(lo + CHUNK, S)) for lo in range(FAR_CUT, S, CHUNK)]
        for lo, hi in late_ranges:
            gather_far_words(far_late[:, lo - FAR_CUT : hi - FAR_CUT], 1, lo, hi)

        def experts(a, b, bank, words, scale, order=(0, 1), opens=True, closes=True):
            count = (b - a) // C
            for s in order:
                for j in range(count):
                    slots = slice(j * C, (j + 1) * C)
                    i = (a // C + j) * PASSES + s
                    nc.tensor.matmul_mx(
                        bank[:, slots],
                        lhsT=w_code[:, i * 2 * N : (i + 1) * 2 * N].bitcast(FP4X4),
                        lhsT_scale=w_scale[:, i * N : (i + 1) * N],
                        rhs=words(s, j).bitcast(FP8X4),
                        rhs_scale=scale(s, j),
                        start=(opens and s == order[0] and j == 0),
                        stop=(closes and s == order[-1] and j == count - 1),
                    )

        def far_experts(lo, hi, words, tag, order):
            bank = ps.tile([P, hi - lo], F32, name="far%d" % lo, tag=tag)
            tables = (far_words0[:, lo:hi], words)
            experts(
                lo, hi, bank,
                lambda s, j: tables[s][:, j * C : (j + 1) * C],
                lambda s, j: far_scale[:, s * S + lo + j * C : s * S + lo + (j + 1) * C],
                order,
            )
            return bank

        def far_out(lo, hi, bank, z):
            nc.scalar.activation(z, bank, ACT.Relu)
            nc.sync.dma_start(out[:, T + lo : T + hi], z)

        for lo in range(0, FAR_CUT, CHUNK):
            hi = min(lo + CHUNK, FAR_CUT)
            far_out(lo, hi, far_experts(lo, hi, far_early[:, lo:hi], "far%d" % lo, (1, 0))[:], tile([P, hi - lo], F32, "z%d" % lo)[:])
        y = tile([P, S], F32, "y")
        for lo, hi in OWN_BANKS:
            bank = ps.tile([P, hi - lo], F32, name="own%d" % lo)
            for i, (a, b) in enumerate(OWN):
                if lo <= a < hi:
                    experts(
                        a, b, bank[:, a - lo : b - lo],
                        lambda s, j: own_words[i][:, (j * PASSES + s) * C : (j * PASSES + s + 1) * C],
                        lambda s, j: own_scale[i][:, (j * PASSES + s) * C : (j * PASSES + s + 1) * C],
                        opens=(a == lo),
                        closes=(b == hi),
                    )
            nc.scalar.activation(y[:, lo:hi], bank[:], ACT.Relu)
        late_bank = far_experts(FAR_CUT, S, far_late[:], "own%d" % OWN[-2][0], (0, 1))

        def fetch(r, a, b, got=None):
            got = got if got is not None else tile([P, b - a], F32, "got%d_%d" % (r, a))
            nc.scalar.activation(got[:], y[:].indirect(entries(pos_list[r], a, b)), ACT.Copy)
            return got

        def weigh(got, r, a, b):
            weighed = tile([P, b - a], F32, "weighed%d_%d" % (r, a))
            nc.vector.tensor_tensor(weighed[:], got, gates[:, r, a:b], ALU.mult)
            return weighed

        def add(first, second, a, b):
            total = tile([P, b - a], F32, "total%d" % a)
            nc.vector.tensor_tensor(total[:], first, second, ALU.add)
            nc.sync.dma_start(out[:, a:b], total[:])

        cut = SUMS[-1][0]
        got = fetch(1, 0, cut)
        far_out(FAR_CUT, S, late_bank[:], tile([P, S - FAR_CUT], F32, "z_late")[:])
        got_rest = fetch(1, cut, T, placed([P, T - cut], F32, "got_rest", halves0_at))
        first = tile([P, T], F32, "first")
        nc.vector.tensor_tensor(first[:], y[:].indirect(pos_list[0][:]), gates[:, 0, :], ALU.mult)
        second = [weigh(got[:, a:b], 1, a, b) for a, b in SUMS[:-1]]
        add(first[:, : SUMS[0][1]], second[0][:], *SUMS[0])
        second.append(weigh(got_rest[:], 1, cut, T))
        for (a, b), weighed in zip(SUMS[1:], second[1:]):
            add(first[:, a:b], weighed[:], a, b)
